import numpy as np
import ml_dtypes


def mxq(x, axis, fmt="e4m3"):
    dtype, down = {"e4m3": (ml_dtypes.float8_e4m3fn, 7), "e5m2": (ml_dtypes.float8_e5m2, 14)}[fmt]
    v = np.moveaxis(np.asarray(x, np.float32).astype(ml_dtypes.bfloat16).astype(np.float64), axis, -1)
    blocks = v.reshape(v.shape[:-1] + (-1, 32))
    amax = np.abs(blocks).max(-1, keepdims=True)
    byte = np.maximum(np.where(amax > 0, np.frexp(amax)[1] - 1 + 127, 0) - down, 1)
    scale = np.exp2(byte - 127.0)
    codes = (blocks / scale).astype(np.float32).astype(dtype).astype(np.float64)
    return np.moveaxis((codes * scale).reshape(v.shape), -1, axis)


WIDE = False


def mx_kscale(k):
    if not WIDE:
        return np.ones(k)
    levels = np.array([18, -18])
    if k % 512:
        return np.exp2(np.random.permutation(np.resize(levels, k // 32))).repeat(32)
    a = np.empty((k // 512, 16))
    for p in range(k // 512):
        a[p, :8] = np.random.permutation(np.resize(levels, 8))
        for g in range(8):
            far = levels[np.abs(levels - a[p, g]) >= 10]
            a[p, g + 8] = far[np.random.randint(len(far))]
    return np.exp2(a.ravel()).repeat(32)


def f64(x):
    return np.asarray(x).astype(np.float64)


def striped(idx):
    return np.tile(np.asarray(idx).reshape(-1, 16).T, (8, 1)).astype(np.uint16)


def unstriped(offs):
    return offs[:16].T.reshape(-1).astype(np.int64)


E2M1 = np.array([0.0, 0.5, 1.0, 1.5, 2.0, 3.0, 4.0, 6.0, -0.0, -0.5, -1.0, -1.5, -2.0, -3.0, -4.0, -6.0])


def pack_weight(w, fmt):
    k, n = w.shape
    w = f64(np.asarray(w, np.float32).astype(ml_dtypes.bfloat16)).reshape(k // 32, 32, n)
    amax = np.abs(w).max(1)
    if fmt == "e4m3":
        byte = np.frexp(amax)[1] - 1 + 127 - 7
    else:
        mant, ex = np.frexp(amax / 6.0)
        byte = np.where(mant > 0.5, ex, ex - 1) + 127
    byte = np.clip(np.where(amax > 0, byte, 1), 1, 254)
    scaled = (w * np.exp2(127.0 - byte)[:, None, :]).reshape(k, n).astype(np.float32)
    by_word = np.ascontiguousarray(scaled.reshape(k // 512, 128, 4, n).transpose(0, 1, 3, 2))
    if fmt == "e4m3":
        words = by_word.astype(ml_dtypes.float8_e4m3fn).view(np.uint8)
    else:
        c = by_word.astype(ml_dtypes.float4_e2m1fn).view(np.uint8) & 0xF
        words = (c[..., 0::2] | (c[..., 1::2] << 4)).reshape(k // 512, 128, 2 * n)
    return np.ascontiguousarray(words), np.ascontiguousarray(byte.astype(np.uint8).reshape(k // 512, 16, n))


def unpack_weight(words, scales, fmt):
    g, _, n = scales.shape
    words = np.ascontiguousarray(words).reshape(g, 128, n, -1)
    if fmt == "e4m3":
        vals = words.view(ml_dtypes.float8_e4m3fn).astype(np.float64)
    else:
        nib = np.empty((g, 128, n, 4), np.uint8)
        nib[..., 0::2] = words & 0xF
        nib[..., 1::2] = words >> 4
        vals = E2M1[nib]
    vals = vals * np.repeat(np.exp2(scales.astype(np.float64) - 127.0), 8, axis=1)[..., None]
    return vals.transpose(0, 1, 3, 2).reshape(g * 512, n)


B, N, T, D, R = 2, 512, 2048, 512, 512


def setup_inputs():
    n = np.random.standard_normal
    idx = np.random.permutation(T)[:B * N]
    s = mx_kscale(D)[:, None]
    z = mx_kscale(R)[:, None]
    x = n((B, D, R))
    wp = pack_weight(n((D, T)) * (0.50 / np.sqrt(D)) / s, "e4m3")
    return {
        "xT": (x * s).astype(np.float32),
        "w_words": wp[0],
        "w_scales": wp[1],
        "vT": (n((D, T)) / np.sqrt(D) / s).astype(np.float32),
        "wt": (np.random.uniform(0.5, 1.5, (B, R, 1)) * 1.0 / np.sqrt(R) * z).astype(np.float32),
        "xm": (x.transpose(0, 2, 1) / z).astype(np.float32),
        "offs": striped(idx),
    }


def reference(xT, w_words, w_scales, vT, wt, xm, offs):
    idx = unstriped(offs)
    w = unpack_weight(w_words, w_scales, "e4m3")
    pick = lambda x: x[:, idx].reshape(x.shape[0], B, N).transpose(1, 0, 2)
    xq = mxq(f64(xT), 1, "e4m3").transpose(0, 2, 1)
    a = xq @ pick(w)
    av = xq @ mxq(pick(f64(vT)), 1, "e4m3")
    g = f64(wt) * np.exp(a) * av
    dw = mxq(f64(xm), 1, "e4m3").transpose(0, 2, 1) @ mxq(g, 1, "e5m2")
    gw = np.zeros((D, T))
    gw[:, idx] = dw.transpose(1, 0, 2).reshape(D, B * N)
    return gw

@@ -1,0 +1,180 @@
+from contextlib import ExitStack
+
+import concourse.mybir as mybir
+
+B, N, T, D, R = 2, 512, 2048, 512, 512
+FLOPS = 3 * 2 * B * N * D * R
+
+F32 = mybir.dt.float32
+BF16 = mybir.dt.bfloat16
+I32 = mybir.dt.int32
+U32 = mybir.dt.uint32
+U16 = mybir.dt.uint16
+U8 = mybir.dt.uint8
+E4M3 = mybir.dt.float8_e4m3fn_x4
+E5M2 = mybir.dt.float8_e5m2_x4
+ACT = mybir.ActivationFunctionType
+MULT = mybir.AluOpType.mult
+
+P = 128
+PACK = 4
+LIST_ROWS = 16
+CHUNK = 128
+XM_PIECES = ((128, 128, 256), (512,))
+
+
+def tile_attend_ghv_poi_kernel(tc, xT, w_words, w_scales, vT, wt, xm, offs, out):
+    nc = tc.nc
+    with ExitStack() as ctx:
+        keep = ctx.enter_context(tc.tile_pool(name="keep", bufs=1))
+        psum_a = ctx.enter_context(tc.psum_pool(name="psum_a", bufs=2))
+        psum_av = ctx.enter_context(tc.psum_pool(name="psum_av", bufs=3))
+        psum_dw = ctx.enter_context(tc.psum_pool(name="psum_dw", bufs=3))
+
+        def sb(name, shape, dtype):
+            return keep.tile(shape, dtype, name=name, align_bytes=64)
+
+        offsets = keep.tile([P, B * N // LIST_ROWS], U16, name="offsets")
+        nc.sync.dma_start(offsets[:], offs)
+
+        def listed(first, count):
+            return offsets[:, first // LIST_ROWS : (first + count) // LIST_ROWS]
+
+        ws_all = sb("ws_all", [P, T // 4], I32)
+        nc.vector.memset(ws_all[:], 0)
+        ws_src = w_scales[0].bitcast(I32)
+        for q in range(4):
+            nc.scalar.dma_start(ws_all[32 * q : 32 * q + 4, :], ws_src[4 * q : 4 * q + 4, :])
+        wt_sb = sb("wt_sb", [P, B, PACK], F32)
+        nc.scalar.dma_start(wt_sb[:], wt.rearrange("b (p t) o -> p b (t o)", t=PACK))
+
+        x_raw = [sb("x_raw%d" % b, [P, PACK, R], F32) for b in range(B)]
+        xm_raw = [sb("xm_raw%d" % b, [P, PACK, D], F32) for b in range(B)]
+        v_all = [sb("v_all%d" % j, [P, T], F32) for j in range(PACK)]
+        w_all = sb("w_all", [P, T], I32)
+
+        def load_x(b):
+            nc.sync.dma_start(x_raw[b][:], xT[b].rearrange("(p j) r -> p j r", j=PACK))
+
+        def load_xm(b):
+            nc.sync.dma_start(xm_raw[b][:], xm[b].rearrange("(p j) d -> p j d", j=PACK))
+
+        load_x(0)
+        nc.sync.dma_start(w_all[:], w_words[0].rearrange("p n t -> p (n t)").bitcast(I32))
+        v_rows = vT.rearrange("(p j) t -> p j t", j=PACK)
+        for j in range(PACK):
+            nc.sync.dma_start(v_all[j][:], v_rows[:, j, :])
+        load_xm(0)
+        load_x(1)
+        load_xm(1)
+
+        placed = [sb("placed%d" % k, [P, T], F32) for k in range(D // P)]
+        for k in range(D // P):
+            nc.vector.memset(placed[k][:], 0.0)
+
+        ws = sb("ws", [P, B * N], U8)
+        nc.vector.tensor_copy(ws[:], ws_all[:].bitcast(U8).indirect(offsets[:]))
+
+        def interleaved(tile_nj):
+            return tile_nj.rearrange("p (c i) j -> p c j i", i=4)
+
+        def by_fours(tile_jn):
+            return tile_jn.rearrange("p j (c i) -> p c j i", i=4)
+
+        def quantize(codes, scales, grouped, fmt):
+            nc.vector.quantize_mx(out=codes.bitcast(fmt), scales=scales, in_=grouped)
+
+        dw = {}
+        for b in range(B):
+            w_codes = sb("w_codes%d" % b, [P, N], U32)
+            nc.vector.tensor_copy(w_codes[:], w_all[:].bitcast(U32).indirect(listed(b * N, N)))
+
+            x_bf = sb("x_bf%d" % b, [P, PACK, P, PACK], BF16)
+            nc.scalar.copy(
+                x_bf[:].rearrange("p t m j -> p m j t"),
+                x_raw[b][:].rearrange("p j (m t) -> p m j t", t=PACK),
+            )
+            x_codes = sb("x_codes%d" % b, [P, R], U32)
+            x_scales = sb("x_scales%d" % b, [P, R], U8)
+            quantize(x_codes[:], x_scales[:], x_bf[:].rearrange("p t m j -> p (t m j)"), E4M3)
+
+            mean = sb("mean%d" % b, [P, PACK, N], F32)
+            for t in range(PACK):
+                rows = slice(t * P, (t + 1) * P)
+                a = psum_a.tile([P, N], F32, name="a")
+                nc.tensor.matmul_mx(
+                    out=a[:],
+                    lhsT=x_codes[:, rows].bitcast(E4M3),
+                    lhsT_scale=x_scales[:, rows],
+                    rhs=w_codes[:].bitcast(E4M3),
+                    rhs_scale=ws[:, b * N : (b + 1) * N],
+                    start=True,
+                    stop=True,
+                )
+                nc.scalar.activation(mean[:, t, :], a[:], ACT.Exp)
+            for t in range(PACK):
+                nc.scalar.activation(mean[:, t, :], mean[:, t, :], ACT.Copy, scale=wt_sb[:, b, t : t + 1])
+
+            v_picked = [sb("v_picked%d_%d" % (b, h), [P, PACK, N // 2], F32) for h in range(2)]
+            for j in range(PACK):
+                for h in range(2):
+                    nc.vector.tensor_copy(
+                        v_picked[h][:, j, :], v_all[j][:].indirect(listed(b * N + h * (N // 2), N // 2))
+                    )
+
+            g_codes = sb("g_codes%d" % b, [P, N], U32)
+            g_scales = sb("g_scales%d" % b, [P, N], U8)
+            for c in range(N // CHUNK):
+                slots = slice(c * CHUNK, (c + 1) * CHUNK)
+                in_half = slice((c % 2) * CHUNK, (c % 2 + 1) * CHUNK)
+                v_bf = sb("v_bf%d_%d" % (b, c), [P, CHUNK, PACK], BF16)
+                nc.scalar.copy(interleaved(v_bf[:]), by_fours(v_picked[c // 2][:, :, in_half]))
+                v_codes = sb("v_codes%d_%d" % (b, c), [P, CHUNK], U32)
+                v_scales = sb("v_scales%d_%d" % (b, c), [P, CHUNK], U8)
+                quantize(v_codes[:], v_scales[:], v_bf[:].rearrange("p n j -> p (n j)"), E4M3)
+                av = psum_av.tile([P, PACK, CHUNK], F32, name="av")
+                for t in range(PACK):
+                    rows = slice(t * P, (t + 1) * P)
+                    nc.tensor.matmul_mx(
+                        out=av[:, t, :],
+                        lhsT=x_codes[:, rows].bitcast(E4M3),
+                        lhsT_scale=x_scales[:, rows],
+                        rhs=v_codes[:].bitcast(E4M3),
+                        rhs_scale=v_scales[:],
+                        start=True,
+                        stop=True,
+                    )
+                g_bf = sb("g_bf%d_%d" % (b, c), [P, CHUNK, PACK], BF16)
+                nc.vector.tensor_tensor(interleaved(g_bf[:]), by_fours(av[:]), by_fours(mean[:, :, slots]), MULT)
+                quantize(g_codes[:, slots], g_scales[:, slots], g_bf[:].rearrange("p n j -> p (n j)"), E5M2)
+
+            xm_codes = sb("xm_codes%d" % b, [P, D], U32)
+            xm_scales = sb("xm_scales%d" % b, [P, D], U8)
+            first = 0
+            for width in XM_PIECES[b]:
+                cols = slice(first, first + width)
+                xm_bf = sb("xm_bf%d_%d" % (b, first), [P, width, PACK], BF16)
+                nc.scalar.copy(interleaved(xm_bf[:]), by_fours(xm_raw[b][:, :, cols]))
+                quantize(xm_codes[:, cols], xm_scales[:, cols], xm_bf[:].rearrange("p n j -> p (n j)"), E4M3)
+                first += width
+
+            for k in range(D // P):
+                cols = slice(k * P, (k + 1) * P)
+                acc = psum_dw.tile([P, N], F32, name="acc")
+                nc.tensor.matmul_mx(
+                    out=acc[:],
+                    lhsT=xm_codes[:, cols].bitcast(E4M3),
+                    lhsT_scale=xm_scales[:, cols],
+                    rhs=g_codes[:].bitcast(E5M2),
+                    rhs_scale=g_scales[:],
+                    start=True,
+                    stop=True,
+                )
+                dw[b, k] = sb("dw%d_%d" % (b, k), [P, N], F32)
+                nc.scalar.copy(dw[b, k][:], acc[:])
+
+        for b in range(B):
+            for k in range(D // P):
+                nc.vector.tensor_copy(placed[k][:].indirect(listed(b * N, N)), dw[b, k][:])
+                if b == B - 1:
+                    nc.sync.dma_start(out[k * P : (k + 1) * P, :], placed[k][:])

@@ -20,7 +20,7 @@ P = 128
 PACK = 4
 LIST_ROWS = 16
 CHUNK = 128
-XM_PIECES = ((128, 128, 256), (512,))
+LAST_PLANE_PIECES = (256, 256, 512)
 
 
 def tile_attend_ghv_poi_kernel(tc, xT, w_words, w_scales, vT, wt, xm, offs, out):
@@ -28,11 +28,11 @@ def tile_attend_ghv_poi_kernel(tc, xT, w_words, w_scales, vT, wt, xm, offs, out)
     with ExitStack() as ctx:
         keep = ctx.enter_context(tc.tile_pool(name="keep", bufs=1))
         psum_a = ctx.enter_context(tc.psum_pool(name="psum_a", bufs=2))
-        psum_av = ctx.enter_context(tc.psum_pool(name="psum_av", bufs=3))
-        psum_dw = ctx.enter_context(tc.psum_pool(name="psum_dw", bufs=3))
+        psum_av = ctx.enter_context(tc.psum_pool(name="psum_av", bufs=4))
+        psum_dw = ctx.enter_context(tc.psum_pool(name="psum_dw", bufs=2))
 
-        def sb(name, shape, dtype):
-            return keep.tile(shape, dtype, name=name, align_bytes=64)
+        def sb(name, shape, dtype, tag=None):
+            return keep.tile(shape, dtype, name=name, tag=tag or name, align_bytes=64)
 
         offsets = keep.tile([P, B * N // LIST_ROWS], U16, name="offsets")
         nc.sync.dma_start(offsets[:], offs)
@@ -41,10 +41,7 @@ def tile_attend_ghv_poi_kernel(tc, xT, w_words, w_scales, vT, wt, xm, offs, out)
             return offsets[:, first // LIST_ROWS : (first + count) // LIST_ROWS]
 
         ws_all = sb("ws_all", [P, T // 4], I32)
-        nc.vector.memset(ws_all[:], 0)
-        ws_src = w_scales[0].bitcast(I32)
-        for q in range(4):
-            nc.scalar.dma_start(ws_all[32 * q : 32 * q + 4, :], ws_src[4 * q : 4 * q + 4, :])
+        nc.gpsimd.memset(ws_all[:], 0)
         wt_sb = sb("wt_sb", [P, B, PACK], F32)
         nc.scalar.dma_start(wt_sb[:], wt.rearrange("b (p t) o -> p b (t o)", t=PACK))
 
@@ -60,6 +57,9 @@ def tile_attend_ghv_poi_kernel(tc, xT, w_words, w_scales, vT, wt, xm, offs, out)
             nc.sync.dma_start(xm_raw[b][:], xm[b].rearrange("(p j) d -> p j d", j=PACK))
 
         load_x(0)
+        ws_src = w_scales[0].bitcast(I32)
+        for q in range(4):
+            nc.sync.dma_start(ws_all[32 * q : 32 * q + 4, :], ws_src[4 * q : 4 * q + 4, :])
         nc.sync.dma_start(w_all[:], w_words[0].rearrange("p n t -> p (n t)").bitcast(I32))
         v_rows = vT.rearrange("(p j) t -> p j t", j=PACK)
         for j in range(PACK):
@@ -70,10 +70,7 @@ def tile_attend_ghv_poi_kernel(tc, xT, w_words, w_scales, vT, wt, xm, offs, out)
 
         placed = [sb("placed%d" % k, [P, T], F32) for k in range(D // P)]
         for k in range(D // P):
-            nc.vector.memset(placed[k][:], 0.0)
-
-        ws = sb("ws", [P, B * N], U8)
-        nc.vector.tensor_copy(ws[:], ws_all[:].bitcast(U8).indirect(offsets[:]))
+            nc.gpsimd.memset(placed[k][:], 0.0)
 
         def interleaved(tile_nj):
             return tile_nj.rearrange("p (c i) j -> p c j i", i=4)
@@ -84,28 +81,34 @@ def tile_attend_ghv_poi_kernel(tc, xT, w_words, w_scales, vT, wt, xm, offs, out)
         def quantize(codes, scales, grouped, fmt):
             nc.vector.quantize_mx(out=codes.bitcast(fmt), scales=scales, in_=grouped)
 
-        dw = {}
-        for b in range(B):
-            w_codes = sb("w_codes%d" % b, [P, N], U32)
-            nc.vector.tensor_copy(w_codes[:], w_all[:].bitcast(U32).indirect(listed(b * N, N)))
+        def gather_w(b, tag):
+            codes = sb("w_codes%d" % b, [P, N], U32, tag)
+            nc.vector.tensor_copy(codes[:], w_all[:].bitcast(U32).indirect(listed(b * N, N)))
+            return codes
 
+        def quantize_x(b, copies):
             x_bf = sb("x_bf%d" % b, [P, PACK, P, PACK], BF16)
-            nc.scalar.copy(
-                x_bf[:].rearrange("p t m j -> p m j t"),
-                x_raw[b][:].rearrange("p j (m t) -> p m j t", t=PACK),
-            )
-            x_codes = sb("x_codes%d" % b, [P, R], U32)
-            x_scales = sb("x_scales%d" % b, [P, R], U8)
-            quantize(x_codes[:], x_scales[:], x_bf[:].rearrange("p t m j -> p (t m j)"), E4M3)
+            step = P // len(copies)
+            for piece, copy in enumerate(copies):
+                m0 = piece * step
+                copy(
+                    x_bf[:, :, m0 : m0 + step, :].rearrange("p t m j -> p m j t"),
+                    x_raw[b][:, :, PACK * m0 : PACK * (m0 + step)].rearrange("p j (m t) -> p m j t", t=PACK),
+                )
+            codes = sb("x_codes%d" % b, [P, R], U32)
+            scales = sb("x_scales%d" % b, [P, R], U8)
+            quantize(codes[:], scales[:], x_bf[:].rearrange("p t m j -> p (t m j)"), E4M3)
+            return codes, scales
 
+        def weighted_mean(b, x_q, w_codes):
             mean = sb("mean%d" % b, [P, PACK, N], F32)
             for t in range(PACK):
                 rows = slice(t * P, (t + 1) * P)
                 a = psum_a.tile([P, N], F32, name="a")
                 nc.tensor.matmul_mx(
                     out=a[:],
-                    lhsT=x_codes[:, rows].bitcast(E4M3),
-                    lhsT_scale=x_scales[:, rows],
+                    lhsT=x_q[0][:, rows].bitcast(E4M3),
+                    lhsT_scale=x_q[1][:, rows],
                     rhs=w_codes[:].bitcast(E4M3),
                     rhs_scale=ws[:, b * N : (b + 1) * N],
                     start=True,
@@ -114,67 +117,102 @@ def tile_attend_ghv_poi_kernel(tc, xT, w_words, w_scales, vT, wt, xm, offs, out)
                 nc.scalar.activation(mean[:, t, :], a[:], ACT.Exp)
             for t in range(PACK):
                 nc.scalar.activation(mean[:, t, :], mean[:, t, :], ACT.Copy, scale=wt_sb[:, b, t : t + 1])
+            return mean
 
-            v_picked = [sb("v_picked%d_%d" % (b, h), [P, PACK, N // 2], F32) for h in range(2)]
-            for j in range(PACK):
-                for h in range(2):
-                    nc.vector.tensor_copy(
-                        v_picked[h][:, j, :], v_all[j][:].indirect(listed(b * N + h * (N // 2), N // 2))
-                    )
-
-            g_codes = sb("g_codes%d" % b, [P, N], U32)
-            g_scales = sb("g_scales%d" % b, [P, N], U8)
-            for c in range(N // CHUNK):
-                slots = slice(c * CHUNK, (c + 1) * CHUNK)
-                in_half = slice((c % 2) * CHUNK, (c % 2 + 1) * CHUNK)
-                v_bf = sb("v_bf%d_%d" % (b, c), [P, CHUNK, PACK], BF16)
-                nc.scalar.copy(interleaved(v_bf[:]), by_fours(v_picked[c // 2][:, :, in_half]))
-                v_codes = sb("v_codes%d_%d" % (b, c), [P, CHUNK], U32)
-                v_scales = sb("v_scales%d_%d" % (b, c), [P, CHUNK], U8)
-                quantize(v_codes[:], v_scales[:], v_bf[:].rearrange("p n j -> p (n j)"), E4M3)
+        def direction_products(b, x_q, first, width):
+            in_list = slice(b * N + first, b * N + first + width)
+            v_bf = sb("v_bf%d_%d" % (b, first), [P, width, PACK], BF16)
+            nc.scalar.copy(interleaved(v_bf[:]), by_fours(v_picked[:, :, in_list]))
+            v_codes = sb("v_codes%d_%d" % (b, first), [P, width], U32)
+            v_scales = sb("v_scales%d_%d" % (b, first), [P, width], U8)
+            quantize(v_codes[:], v_scales[:], v_bf[:].rearrange("p n j -> p (n j)"), E4M3)
+            banks = []
+            for c0 in range(0, width, CHUNK):
+                chunk = slice(c0, c0 + CHUNK)
                 av = psum_av.tile([P, PACK, CHUNK], F32, name="av")
                 for t in range(PACK):
                     rows = slice(t * P, (t + 1) * P)
                     nc.tensor.matmul_mx(
                         out=av[:, t, :],
-                        lhsT=x_codes[:, rows].bitcast(E4M3),
-                        lhsT_scale=x_scales[:, rows],
-                        rhs=v_codes[:].bitcast(E4M3),
-                        rhs_scale=v_scales[:],
+                        lhsT=x_q[0][:, rows].bitcast(E4M3),
+                        lhsT_scale=x_q[1][:, rows],
+                        rhs=v_codes[:, chunk].bitcast(E4M3),
+                        rhs_scale=v_scales[:, chunk],
                         start=True,
                         stop=True,
                     )
-                g_bf = sb("g_bf%d_%d" % (b, c), [P, CHUNK, PACK], BF16)
-                nc.vector.tensor_tensor(interleaved(g_bf[:]), by_fours(av[:]), by_fours(mean[:, :, slots]), MULT)
-                quantize(g_codes[:, slots], g_scales[:, slots], g_bf[:].rearrange("p n j -> p (n j)"), E5M2)
+                banks.append(av)
+            return banks
 
-            xm_codes = sb("xm_codes%d" % b, [P, D], U32)
-            xm_scales = sb("xm_scales%d" % b, [P, D], U8)
-            first = 0
-            for width in XM_PIECES[b]:
-                cols = slice(first, first + width)
-                xm_bf = sb("xm_bf%d_%d" % (b, first), [P, width, PACK], BF16)
-                nc.scalar.copy(interleaved(xm_bf[:]), by_fours(xm_raw[b][:, :, cols]))
-                quantize(xm_codes[:, cols], xm_scales[:, cols], xm_bf[:].rearrange("p n j -> p (n j)"), E4M3)
-                first += width
-
-            for k in range(D // P):
-                cols = slice(k * P, (k + 1) * P)
-                acc = psum_dw.tile([P, N], F32, name="acc")
-                nc.tensor.matmul_mx(
-                    out=acc[:],
-                    lhsT=xm_codes[:, cols].bitcast(E4M3),
-                    lhsT_scale=xm_scales[:, cols],
-                    rhs=g_codes[:].bitcast(E5M2),
-                    rhs_scale=g_scales[:],
-                    start=True,
-                    stop=True,
+        def quantize_g(b, g_q, mean, first, banks):
+            width = CHUNK * len(banks)
+            g_bf = sb("g_bf%d_%d" % (b, first), [P, width, PACK], BF16)
+            for c, av in enumerate(banks):
+                c0 = c * CHUNK
+                nc.vector.tensor_tensor(
+                    interleaved(g_bf[:, c0 : c0 + CHUNK, :]),
+                    by_fours(av[:]),
+                    by_fours(mean[:, :, first + c0 : first + c0 + CHUNK]),
+                    MULT,
                 )
-                dw[b, k] = sb("dw%d_%d" % (b, k), [P, N], F32)
-                nc.scalar.copy(dw[b, k][:], acc[:])
+            slots = slice(first, first + width)
+            quantize(g_q[0][:, slots], g_q[1][:, slots], g_bf[:].rearrange("p n j -> p (n j)"), E5M2)
 
-        for b in range(B):
-            for k in range(D // P):
-                nc.vector.tensor_copy(placed[k][:].indirect(listed(b * N, N)), dw[b, k][:])
-                if b == B - 1:
-                    nc.sync.dma_start(out[k * P : (k + 1) * P, :], placed[k][:])
+        def quantize_xm(b):
+            codes = sb("xm_codes%d" % b, [P, D], U32)
+            scales = sb("xm_scales%d" % b, [P, D], U8)
+            xm_bf = sb("xm_bf%d" % b, [P, D, PACK], BF16)
+            nc.scalar.copy(interleaved(xm_bf[:]), by_fours(xm_raw[b][:]))
+            quantize(codes[:], scales[:], xm_bf[:].rearrange("p n j -> p (n j)"), E4M3)
+            return codes, scales
+
+        def place(b, k, xm_q, g_q, tag):
+            cols = slice(k * P, (k + 1) * P)
+            acc = psum_dw.tile([P, N], F32, name="acc")
+            nc.tensor.matmul_mx(
+                out=acc[:],
+                lhsT=xm_q[0][:, cols].bitcast(E4M3),
+                lhsT_scale=xm_q[1][:, cols],
+                rhs=g_q[0][:].bitcast(E5M2),
+                rhs_scale=g_q[1][:],
+                start=True,
+                stop=True,
+            )
+            dw = sb("dw%d_%d" % (b, k), [P, N], F32, tag)
+            nc.scalar.copy(dw[:], acc[:])
+            nc.vector.tensor_copy(placed[k][:].indirect(listed(b * N, N)), dw[:])
+
+        w_codes0 = gather_w(0, None)
+        ws = sb("ws", [P, B * N], U8)
+        nc.vector.tensor_copy(ws[:], ws_all[:].bitcast(U8).indirect(offsets[:]))
+        x_q0 = quantize_x(0, (nc.scalar.copy,))
+        mean0 = weighted_mean(0, x_q0, w_codes0)
+
+        v_picked = sb("v_picked", [P, PACK, B * N], F32)
+        for j in range(PACK - 1):
+            nc.vector.tensor_copy(v_picked[:, j, :], v_all[j][:].indirect(offsets[:]))
+        first = 0
+        for count in LAST_PLANE_PIECES:
+            nc.vector.tensor_copy(
+                v_picked[:, PACK - 1, first : first + count], v_all[PACK - 1][:].indirect(listed(first, count))
+            )
+            first += count
+
+        g_q0 = sb("g_codes0", [P, N], U32), sb("g_scales0", [P, N], U8)
+        for first in range(0, N, CHUNK):
+            quantize_g(0, g_q0, mean0, first, direction_products(0, x_q0, first, CHUNK))
+        xm_q0 = quantize_xm(0)
+        x_q1 = quantize_x(1, (nc.scalar.copy,))
+        w_codes1 = gather_w(1, "g_bf0_384")
+        place(0, 0, xm_q0, g_q0, "x_raw1")
+        place(0, 1, xm_q0, g_q0, None)
+        banks1 = direction_products(1, x_q1, 0, N)
+        place(0, 2, xm_q0, g_q0, "v_picked")
+        mean1 = weighted_mean(1, x_q1, w_codes1)
+        g_q1 = sb("g_codes1", [P, N], U32), sb("g_scales1", [P, N], U8)
+        quantize_g(1, g_q1, mean1, 0, banks1)
+        xm_q1 = quantize_xm(1)
+        place(0, 3, xm_q0, g_q0, "mean1")
+        for k in range(D // P):
+            place(1, k, xm_q1, g_q1, None)
+            nc.sync.dma_start(out[k * P : (k + 1) * P, :], placed[k][:])

@@ -56,11 +56,11 @@ def tile_attend_ghv_poi_kernel(tc, xT, w_words, w_scales, vT, wt, xm, offs, out)
         def load_xm(b):
             nc.sync.dma_start(xm_raw[b][:], xm[b].rearrange("(p j) d -> p j d", j=PACK))
 
-        load_x(0)
+        nc.sync.dma_start(w_all[:], w_words[0].rearrange("p n t -> p (n t)").bitcast(I32))
         ws_src = w_scales[0].bitcast(I32)
         for q in range(4):
             nc.sync.dma_start(ws_all[32 * q : 32 * q + 4, :], ws_src[4 * q : 4 * q + 4, :])
-        nc.sync.dma_start(w_all[:], w_words[0].rearrange("p n t -> p (n t)").bitcast(I32))
+        load_x(0)
         v_rows = vT.rearrange("(p j) t -> p j t", j=PACK)
         for j in range(PACK):
             nc.sync.dma_start(v_all[j][:], v_rows[:, j, :])
@@ -81,26 +81,18 @@ def tile_attend_ghv_poi_kernel(tc, xT, w_words, w_scales, vT, wt, xm, offs, out)
         def quantize(codes, scales, grouped, fmt):
             nc.vector.quantize_mx(out=codes.bitcast(fmt), scales=scales, in_=grouped)
 
-        def gather_w(b, tag):
-            codes = sb("w_codes%d" % b, [P, N], U32, tag)
-            nc.vector.tensor_copy(codes[:], w_all[:].bitcast(U32).indirect(listed(b * N, N)))
-            return codes
-
-        def quantize_x(b, copies):
+        def quantize_x(b):
             x_bf = sb("x_bf%d" % b, [P, PACK, P, PACK], BF16)
-            step = P // len(copies)
-            for piece, copy in enumerate(copies):
-                m0 = piece * step
-                copy(
-                    x_bf[:, :, m0 : m0 + step, :].rearrange("p t m j -> p m j t"),
-                    x_raw[b][:, :, PACK * m0 : PACK * (m0 + step)].rearrange("p j (m t) -> p m j t", t=PACK),
-                )
+            src = x_raw[b][:].rearrange("p j (m e t) -> p m j e t", e=2, t=PACK)
+            dst = x_bf[:].rearrange("p t (m e) j -> p m j e t", e=2)
+            for t0 in range(0, PACK, 2):
+                nc.scalar.copy(dst[:, :, :, :, t0 : t0 + 2], src[:, :, :, :, t0 : t0 + 2])
             codes = sb("x_codes%d" % b, [P, R], U32)
             scales = sb("x_scales%d" % b, [P, R], U8)
             quantize(codes[:], scales[:], x_bf[:].rearrange("p t m j -> p (t m j)"), E4M3)
             return codes, scales
 
-        def weighted_mean(b, x_q, w_codes):
+        def weighted_mean(b, x_q):
             mean = sb("mean%d" % b, [P, PACK, N], F32)
             for t in range(PACK):
                 rows = slice(t * P, (t + 1) * P)
@@ -109,7 +101,7 @@ def tile_attend_ghv_poi_kernel(tc, xT, w_words, w_scales, vT, wt, xm, offs, out)
                     out=a[:],
                     lhsT=x_q[0][:, rows].bitcast(E4M3),
                     lhsT_scale=x_q[1][:, rows],
-                    rhs=w_codes[:].bitcast(E4M3),
+                    rhs=w_codes[:, b * N : (b + 1) * N].bitcast(E4M3),
                     rhs_scale=ws[:, b * N : (b + 1) * N],
                     start=True,
                     stop=True,
@@ -158,13 +150,11 @@ def tile_attend_ghv_poi_kernel(tc, xT, w_words, w_scales, vT, wt, xm, offs, out)
             slots = slice(first, first + width)
             quantize(g_q[0][:, slots], g_q[1][:, slots], g_bf[:].rearrange("p n j -> p (n j)"), E5M2)
 
-        def quantize_xm(b):
-            codes = sb("xm_codes%d" % b, [P, D], U32)
-            scales = sb("xm_scales%d" % b, [P, D], U8)
-            xm_bf = sb("xm_bf%d" % b, [P, D, PACK], BF16)
-            nc.scalar.copy(interleaved(xm_bf[:]), by_fours(xm_raw[b][:]))
-            quantize(codes[:], scales[:], xm_bf[:].rearrange("p n j -> p (n j)"), E4M3)
-            return codes, scales
+        def quantize_xm(b, xm_q, first, width):
+            cols = slice(first, first + width)
+            xm_bf = sb("xm_bf%d_%d" % (b, first), [P, width, PACK], BF16)
+            nc.scalar.copy(interleaved(xm_bf[:]), by_fours(xm_raw[b][:, :, cols]))
+            quantize(xm_q[0][:, cols], xm_q[1][:, cols], xm_bf[:].rearrange("p n j -> p (n j)"), E4M3)
 
         def place(b, k, xm_q, g_q, tag):
             cols = slice(k * P, (k + 1) * P)
@@ -182,11 +172,12 @@ def tile_attend_ghv_poi_kernel(tc, xT, w_words, w_scales, vT, wt, xm, offs, out)
             nc.scalar.copy(dw[:], acc[:])
             nc.vector.tensor_copy(placed[k][:].indirect(listed(b * N, N)), dw[:])
 
-        w_codes0 = gather_w(0, None)
+        w_codes = sb("w_codes", [P, B * N], U32)
+        nc.vector.tensor_copy(w_codes[:], w_all[:].bitcast(U32).indirect(offsets[:]))
         ws = sb("ws", [P, B * N], U8)
         nc.vector.tensor_copy(ws[:], ws_all[:].bitcast(U8).indirect(offsets[:]))
-        x_q0 = quantize_x(0, (nc.scalar.copy,))
-        mean0 = weighted_mean(0, x_q0, w_codes0)
+        x_q0 = quantize_x(0)
+        mean0 = weighted_mean(0, x_q0)
 
         v_picked = sb("v_picked", [P, PACK, B * N], F32)
         for j in range(PACK - 1):
@@ -201,17 +192,19 @@ def tile_attend_ghv_poi_kernel(tc, xT, w_words, w_scales, vT, wt, xm, offs, out)
         g_q0 = sb("g_codes0", [P, N], U32), sb("g_scales0", [P, N], U8)
         for first in range(0, N, CHUNK):
             quantize_g(0, g_q0, mean0, first, direction_products(0, x_q0, first, CHUNK))
-        xm_q0 = quantize_xm(0)
-        x_q1 = quantize_x(1, (nc.scalar.copy,))
-        w_codes1 = gather_w(1, "g_bf0_384")
+        xm_q0 = sb("xm_codes0", [P, D], U32), sb("xm_scales0", [P, D], U8)
+        quantize_xm(0, xm_q0, 0, D // 2)
+        x_q1 = quantize_x(1)
         place(0, 0, xm_q0, g_q0, "x_raw1")
-        place(0, 1, xm_q0, g_q0, None)
+        quantize_xm(0, xm_q0, D // 2, D // 2)
+        place(0, 1, xm_q0, g_q0, "xm_raw0")
         banks1 = direction_products(1, x_q1, 0, N)
         place(0, 2, xm_q0, g_q0, "v_picked")
-        mean1 = weighted_mean(1, x_q1, w_codes1)
+        mean1 = weighted_mean(1, x_q1)
         g_q1 = sb("g_codes1", [P, N], U32), sb("g_scales1", [P, N], U8)
         quantize_g(1, g_q1, mean1, 0, banks1)
-        xm_q1 = quantize_xm(1)
+        xm_q1 = sb("xm_codes1", [P, D], U32), sb("xm_scales1", [P, D], U8)
+        quantize_xm(1, xm_q1, 0, D)
         place(0, 3, xm_q0, g_q0, "mean1")
         for k in range(D // P):
             place(1, k, xm_q1, g_q1, None)

@@ -15,6 +15,7 @@ E4M3 = mybir.dt.float8_e4m3fn_x4
 E5M2 = mybir.dt.float8_e5m2_x4
 ACT = mybir.ActivationFunctionType
 MULT = mybir.AluOpType.mult
+ADD = mybir.AluOpType.add
 
 P = 128
 PACK = 4
@@ -150,13 +151,13 @@ def tile_attend_ghv_poi_kernel(tc, xT, w_words, w_scales, vT, wt, xm, offs, out)
             slots = slice(first, first + width)
             quantize(g_q[0][:, slots], g_q[1][:, slots], g_bf[:].rearrange("p n j -> p (n j)"), E5M2)
 
-        def quantize_xm(b, xm_q, first, width):
+        def quantize_xm(b, xm_q, first, width, tag):
             cols = slice(first, first + width)
-            xm_bf = sb("xm_bf%d_%d" % (b, first), [P, width, PACK], BF16)
+            xm_bf = sb("xm_bf%d_%d" % (b, first), [P, width, PACK], BF16, tag)
             nc.scalar.copy(interleaved(xm_bf[:]), by_fours(xm_raw[b][:, :, cols]))
             quantize(xm_q[0][:, cols], xm_q[1][:, cols], xm_bf[:].rearrange("p n j -> p (n j)"), E4M3)
 
-        def place(b, k, xm_q, g_q, tag):
+        def product(k, xm_q, g_q):
             cols = slice(k * P, (k + 1) * P)
             acc = psum_dw.tile([P, N], F32, name="acc")
             nc.tensor.matmul_mx(
@@ -168,9 +169,15 @@ def tile_attend_ghv_poi_kernel(tc, xT, w_words, w_scales, vT, wt, xm, offs, out)
                 start=True,
                 stop=True,
             )
-            dw = sb("dw%d_%d" % (b, k), [P, N], F32, tag)
-            nc.scalar.copy(dw[:], acc[:])
-            nc.vector.tensor_copy(placed[k][:].indirect(listed(b * N, N)), dw[:])
+            return acc
+
+        def place_part(b, k, acc, first, count, tag):
+            dw = sb("dw%d_%d_%d" % (b, k, first), [P, count], F32, tag)
+            nc.scalar.copy(dw[:], acc[:, first : first + count])
+            nc.vector.tensor_copy(placed[k][:].indirect(listed(b * N + first, count)), dw[:])
+
+        def place(b, k, xm_q, g_q, tag):
+            place_part(b, k, product(k, xm_q, g_q), 0, N, tag)
 
         w_codes = sb("w_codes", [P, B * N], U32)
         nc.vector.tensor_copy(w_codes[:], w_all[:].bitcast(U32).indirect(offsets[:]))
@@ -193,19 +200,73 @@ def tile_attend_ghv_poi_kernel(tc, xT, w_words, w_scales, vT, wt, xm, offs, out)
         for first in range(0, N, CHUNK):
             quantize_g(0, g_q0, mean0, first, direction_products(0, x_q0, first, CHUNK))
         xm_q0 = sb("xm_codes0", [P, D], U32), sb("xm_scales0", [P, D], U8)
-        quantize_xm(0, xm_q0, 0, D // 2)
+        quantize_xm(0, xm_q0, 0, D // 2, None)
         x_q1 = quantize_x(1)
         place(0, 0, xm_q0, g_q0, "x_raw1")
-        quantize_xm(0, xm_q0, D // 2, D // 2)
+        xm_bf = sb("xm_bf0_late", [P, D // 2, PACK], BF16, "x_bf1")
+        nc.gpsimd.tensor_scalar(xm_bf[:], xm_raw[0][:, :, D // 2 :].rearrange("p j n -> p n j"), 1.0, 0.0, MULT, ADD)
+        quantize(xm_q0[0][:, D // 2 :], xm_q0[1][:, D // 2 :], xm_bf[:].rearrange("p n j -> p (n j)"), E4M3)
+
+        v_bf = sb("v_bf1", [P, N, PACK], BF16)
+        nc.scalar.copy(interleaved(v_bf[:]), by_fours(v_picked[:, :, N:]))
+        v_codes = sb("v_codes1", [P, N], U32)
+        v_scales = sb("v_scales1", [P, N], U8)
+        quantize(v_codes[:], v_scales[:], v_bf[:].rearrange("p n j -> p (n j)"), E4M3)
         place(0, 1, xm_q0, g_q0, "xm_raw0")
-        banks1 = direction_products(1, x_q1, 0, N)
-        place(0, 2, xm_q0, g_q0, "v_picked")
-        mean1 = weighted_mean(1, x_q1)
+
+        mean1 = sb("mean1", [P, N // 4, PACK, 4], F32)
+        for t in range(PACK):
+            rows = slice(t * P, (t + 1) * P)
+            a = psum_a.tile([P, N], F32, name="a")
+            nc.tensor.matmul_mx(
+                out=a[:],
+                lhsT=x_q1[0][:, rows].bitcast(E4M3),
+                lhsT_scale=x_q1[1][:, rows],
+                rhs=w_codes[:, N:].bitcast(E4M3),
+                rhs_scale=ws[:, N:],
+                start=True,
+                stop=True,
+            )
+            nc.scalar.activation(mean1[:, :, t, :], a[:].rearrange("p (c i) -> p c i", i=4), ACT.Exp)
+        banks = []
+        for t in range(PACK):
+            rows = slice(t * P, (t + 1) * P)
+            av = psum_av.tile([P, N], F32, name="av")
+            nc.tensor.matmul_mx(
+                out=av[:],
+                lhsT=x_q1[0][:, rows].bitcast(E4M3),
+                lhsT_scale=x_q1[1][:, rows],
+                rhs=v_codes[:].bitcast(E4M3),
+                rhs_scale=v_scales[:],
+                start=True,
+                stop=True,
+            )
+            banks.append(av)
+        av_wt = sb("av_wt", [P, N // 4, PACK, 4], F32)
+        g_bf = sb("g_bf1", [P, N, PACK], BF16)
+        for half in range(2):
+            fours = slice(half * N // 8, (half + 1) * N // 8)
+            for t in range(PACK):
+                nc.scalar.activation(
+                    av_wt[:, fours, t, :],
+                    banks[t][:].rearrange("p (c i) -> p c i", i=4)[:, fours, :],
+                    ACT.Copy,
+                    scale=wt_sb[:, 1, t : t + 1],
+                )
+            if half == 0:
+                place(0, 2, xm_q0, g_q0, "v_bf1")
+                last_acc = product(3, xm_q0, g_q0)
+                place_part(0, 3, last_acc, 0, N // 2, None)
+            for c0 in range(half * N // 2, (half + 1) * N // 2, CHUNK):
+                fours = slice(c0 // 4, (c0 + CHUNK) // 4)
+                nc.gpsimd.tensor_tensor(
+                    interleaved(g_bf[:, c0 : c0 + CHUNK, :]), mean1[:, fours, :, :], av_wt[:, fours, :, :], MULT
+                )
         g_q1 = sb("g_codes1", [P, N], U32), sb("g_scales1", [P, N], U8)
-        quantize_g(1, g_q1, mean1, 0, banks1)
+        quantize(g_q1[0][:], g_q1[1][:], g_bf[:].rearrange("p n j -> p (n j)"), E5M2)
         xm_q1 = sb("xm_codes1", [P, D], U32), sb("xm_scales1", [P, D], U8)
-        quantize_xm(1, xm_q1, 0, D)
-        place(0, 3, xm_q0, g_q0, "mean1")
+        quantize_xm(1, xm_q1, 0, D, "v_codes1")
+        place_part(0, 3, last_acc, N // 2, N // 2, "mean1")
         for k in range(D // P):
             place(1, k, xm_q1, g_q1, None)
             nc.sync.dma_start(out[k * P : (k + 1) * P, :], placed[k][:])

@@ -21,7 +21,7 @@ P = 128
 PACK = 4
 LIST_ROWS = 16
 CHUNK = 128
-LAST_PLANE_PIECES = (256, 256, 512)
+LAST_PLANE_PIECES = (256, 256, 256)
 
 
 def tile_attend_ghv_poi_kernel(tc, xT, w_words, w_scales, vT, wt, xm, offs, out):
@@ -44,7 +44,7 @@ def tile_attend_ghv_poi_kernel(tc, xT, w_words, w_scales, vT, wt, xm, offs, out)
         ws_all = sb("ws_all", [P, T // 4], I32)
         nc.gpsimd.memset(ws_all[:], 0)
         wt_sb = sb("wt_sb", [P, B, PACK], F32)
-        nc.scalar.dma_start(wt_sb[:], wt.rearrange("b (p t) o -> p b (t o)", t=PACK))
+        nc.sync.dma_start(wt_sb[:], wt.rearrange("b (p t) o -> p b (t o)", t=PACK))
 
         x_raw = [sb("x_raw%d" % b, [P, PACK, R], F32) for b in range(B)]
         xm_raw = [sb("xm_raw%d" % b, [P, PACK, D], F32) for b in range(B)]
@@ -57,10 +57,10 @@ def tile_attend_ghv_poi_kernel(tc, xT, w_words, w_scales, vT, wt, xm, offs, out)
         def load_xm(b):
             nc.sync.dma_start(xm_raw[b][:], xm[b].rearrange("(p j) d -> p j d", j=PACK))
 
-        nc.sync.dma_start(w_all[:], w_words[0].rearrange("p n t -> p (n t)").bitcast(I32))
         ws_src = w_scales[0].bitcast(I32)
         for q in range(4):
             nc.sync.dma_start(ws_all[32 * q : 32 * q + 4, :], ws_src[4 * q : 4 * q + 4, :])
+        nc.sync.dma_start(w_all[:], w_words[0].rearrange("p n t -> p (n t)").bitcast(I32))
         load_x(0)
         v_rows = vT.rearrange("(p j) t -> p j t", j=PACK)
         for j in range(PACK):
@@ -69,8 +69,8 @@ def tile_attend_ghv_poi_kernel(tc, xT, w_words, w_scales, vT, wt, xm, offs, out)
         load_x(1)
         load_xm(1)
 
-        placed = [sb("placed%d" % k, [P, T], F32) for k in range(D // P)]
-        for k in range(D // P):
+        placed = [sb("placed%d" % k, [P, T], F32) for k in range(2)]
+        for k in range(2):
             nc.gpsimd.memset(placed[k][:], 0.0)
 
         def interleaved(tile_nj):
@@ -82,111 +82,67 @@ def tile_attend_ghv_poi_kernel(tc, xT, w_words, w_scales, vT, wt, xm, offs, out)
         def quantize(codes, scales, grouped, fmt):
             nc.vector.quantize_mx(out=codes.bitcast(fmt), scales=scales, in_=grouped)
 
-        def quantize_x(b):
-            x_bf = sb("x_bf%d" % b, [P, PACK, P, PACK], BF16)
-            src = x_raw[b][:].rearrange("p j (m e t) -> p m j e t", e=2, t=PACK)
-            dst = x_bf[:].rearrange("p t (m e) j -> p m j e t", e=2)
-            for t0 in range(0, PACK, 2):
-                nc.scalar.copy(dst[:, :, :, :, t0 : t0 + 2], src[:, :, :, :, t0 : t0 + 2])
-            codes = sb("x_codes%d" % b, [P, R], U32)
-            scales = sb("x_scales%d" % b, [P, R], U8)
-            quantize(codes[:], scales[:], x_bf[:].rearrange("p t m j -> p (t m j)"), E4M3)
-            return codes, scales
-
-        def weighted_mean(b, x_q):
-            mean = sb("mean%d" % b, [P, PACK, N], F32)
-            for t in range(PACK):
-                rows = slice(t * P, (t + 1) * P)
-                a = psum_a.tile([P, N], F32, name="a")
-                nc.tensor.matmul_mx(
-                    out=a[:],
-                    lhsT=x_q[0][:, rows].bitcast(E4M3),
-                    lhsT_scale=x_q[1][:, rows],
-                    rhs=w_codes[:, b * N : (b + 1) * N].bitcast(E4M3),
-                    rhs_scale=ws[:, b * N : (b + 1) * N],
-                    start=True,
-                    stop=True,
-                )
-                nc.scalar.activation(mean[:, t, :], a[:], ACT.Exp)
-            for t in range(PACK):
-                nc.scalar.activation(mean[:, t, :], mean[:, t, :], ACT.Copy, scale=wt_sb[:, b, t : t + 1])
-            return mean
-
-        def direction_products(b, x_q, first, width):
-            in_list = slice(b * N + first, b * N + first + width)
-            v_bf = sb("v_bf%d_%d" % (b, first), [P, width, PACK], BF16)
-            nc.scalar.copy(interleaved(v_bf[:]), by_fours(v_picked[:, :, in_list]))
-            v_codes = sb("v_codes%d_%d" % (b, first), [P, width], U32)
-            v_scales = sb("v_scales%d_%d" % (b, first), [P, width], U8)
-            quantize(v_codes[:], v_scales[:], v_bf[:].rearrange("p n j -> p (n j)"), E4M3)
-            banks = []
-            for c0 in range(0, width, CHUNK):
-                chunk = slice(c0, c0 + CHUNK)
-                av = psum_av.tile([P, PACK, CHUNK], F32, name="av")
-                for t in range(PACK):
-                    rows = slice(t * P, (t + 1) * P)
-                    nc.tensor.matmul_mx(
-                        out=av[:, t, :],
-                        lhsT=x_q[0][:, rows].bitcast(E4M3),
-                        lhsT_scale=x_q[1][:, rows],
-                        rhs=v_codes[:, chunk].bitcast(E4M3),
-                        rhs_scale=v_scales[:, chunk],
-                        start=True,
-                        stop=True,
-                    )
-                banks.append(av)
-            return banks
-
-        def quantize_g(b, g_q, mean, first, banks):
-            width = CHUNK * len(banks)
-            g_bf = sb("g_bf%d_%d" % (b, first), [P, width, PACK], BF16)
-            for c, av in enumerate(banks):
-                c0 = c * CHUNK
-                nc.vector.tensor_tensor(
-                    interleaved(g_bf[:, c0 : c0 + CHUNK, :]),
-                    by_fours(av[:]),
-                    by_fours(mean[:, :, first + c0 : first + c0 + CHUNK]),
-                    MULT,
-                )
-            slots = slice(first, first + width)
-            quantize(g_q[0][:, slots], g_q[1][:, slots], g_bf[:].rearrange("p n j -> p (n j)"), E5M2)
-
-        def quantize_xm(b, xm_q, first, width, tag):
-            cols = slice(first, first + width)
-            xm_bf = sb("xm_bf%d_%d" % (b, first), [P, width, PACK], BF16, tag)
-            nc.scalar.copy(interleaved(xm_bf[:]), by_fours(xm_raw[b][:, :, cols]))
-            quantize(xm_q[0][:, cols], xm_q[1][:, cols], xm_bf[:].rearrange("p n j -> p (n j)"), E4M3)
-
-        def product(k, xm_q, g_q):
-            cols = slice(k * P, (k + 1) * P)
-            acc = psum_dw.tile([P, N], F32, name="acc")
+        def mx(acc, lhs_q, lhs_cols, rhs_q, rhs_cols, rhs_fmt):
             nc.tensor.matmul_mx(
-                out=acc[:],
-                lhsT=xm_q[0][:, cols].bitcast(E4M3),
-                lhsT_scale=xm_q[1][:, cols],
-                rhs=g_q[0][:].bitcast(E5M2),
-                rhs_scale=g_q[1][:],
+                out=acc,
+                lhsT=lhs_q[0][:, lhs_cols].bitcast(E4M3),
+                lhsT_scale=lhs_q[1][:, lhs_cols],
+                rhs=rhs_q[0][:, rhs_cols].bitcast(rhs_fmt),
+                rhs_scale=rhs_q[1][:, rhs_cols],
                 start=True,
                 stop=True,
             )
+
+        def flat(tile_nj):
+            return tile_nj.rearrange("p n j -> p (n j)")
+
+        def block(i, width=P):
+            return slice(i * width, (i + 1) * width)
+
+        def planes(name, width, tag=None):
+            return sb(name + "_codes", [P, width], U32, tag), sb(name + "_scales", [P, width], U8)
+
+        def quantize_x(b, x_bf, copies):
+            src = x_raw[b][:].rearrange("p j (m e t) -> p m j e t", e=2, t=PACK)
+            dst = x_bf.rearrange("p t (m e) j -> p m j e t", e=2)
+            for t0, copy_by in zip(range(0, PACK, 2), copies):
+                copy_by(dst[:, :, :, :, t0 : t0 + 2], src[:, :, :, :, t0 : t0 + 2])
+            x_q = planes("x%d" % b, R)
+            quantize(x_q[0][:], x_q[1][:], x_bf.rearrange("p t m j -> p (t m j)"), E4M3)
+            return x_q
+
+        def product(k, xm_q, g_q):
+            acc = psum_dw.tile([P, N], F32, name="acc")
+            mx(acc[:], xm_q[k][0], xm_q[k][1], g_q, slice(0, N), E5M2)
             return acc
 
-        def place_part(b, k, acc, first, count, tag):
+        def place_part(b, k, acc, first, count, tag=None):
             dw = sb("dw%d_%d_%d" % (b, k, first), [P, count], F32, tag)
             nc.scalar.copy(dw[:], acc[:, first : first + count])
             nc.vector.tensor_copy(placed[k][:].indirect(listed(b * N + first, count)), dw[:])
 
-        def place(b, k, xm_q, g_q, tag):
-            place_part(b, k, product(k, xm_q, g_q), 0, N, tag)
+        def place(b, k, xm_q, g_q):
+            place_part(b, k, product(k, xm_q, g_q), 0, N)
 
-        w_codes = sb("w_codes", [P, B * N], U32)
-        nc.vector.tensor_copy(w_codes[:], w_all[:].bitcast(U32).indirect(offsets[:]))
+        H = N // 2
+
         ws = sb("ws", [P, B * N], U8)
         nc.vector.tensor_copy(ws[:], ws_all[:].bitcast(U8).indirect(offsets[:]))
-        x_q0 = quantize_x(0)
-        mean0 = weighted_mean(0, x_q0)
+        w_codes = sb("w_codes", [P, B * N], U32)
+        nc.vector.tensor_copy(w_codes[:], w_all[:].bitcast(U32).indirect(offsets[:]))
+        v_flat = sb("v_flat", [P, PACK * B * N + H], F32)
+        v_picked = v_flat[:, : PACK * B * N].rearrange("p (j n) -> p j n", j=PACK)
+        x_bf0 = v_picked[:, 0, :].bitcast(BF16).rearrange("p (t m j) -> p t m j", t=PACK, j=PACK)
+        x_q0 = quantize_x(0, x_bf0, (nc.scalar.copy, nc.vector.tensor_copy))
+        w_q = w_codes, ws
+        mean0 = sb("mean0", [P, PACK, N], F32)
+        for t in range(PACK):
+            a = psum_a.tile([P, N], F32, name="a")
+            mx(a[:], x_q0, block(t), w_q, slice(0, N), E4M3)
+            nc.scalar.activation(mean0[:, t, :], a[:], ACT.Exp)
+        for t in range(PACK):
+            nc.scalar.activation(mean0[:, t, :], mean0[:, t, :], ACT.Copy, scale=wt_sb[:, 0, t : t + 1])
 
-        v_picked = sb("v_picked", [P, PACK, B * N], F32)
         for j in range(PACK - 1):
             nc.vector.tensor_copy(v_picked[:, j, :], v_all[j][:].indirect(offsets[:]))
         first = 0
@@ -195,78 +151,109 @@ def tile_attend_ghv_poi_kernel(tc, xT, w_words, w_scales, vT, wt, xm, offs, out)
                 v_picked[:, PACK - 1, first : first + count], v_all[PACK - 1][:].indirect(listed(first, count))
             )
             first += count
+        for k in range(2, D // P):
+            placed.append(sb("placed%d" % k, [P, T], F32, "v_all%d" % (k - 2)))
+            nc.gpsimd.memset(placed[k][:], 0.0)
 
-        g_q0 = sb("g_codes0", [P, N], U32), sb("g_scales0", [P, N], U8)
-        for first in range(0, N, CHUNK):
-            quantize_g(0, g_q0, mean0, first, direction_products(0, x_q0, first, CHUNK))
-        xm_q0 = sb("xm_codes0", [P, D], U32), sb("xm_scales0", [P, D], U8)
-        quantize_xm(0, xm_q0, 0, D // 2, None)
-        x_q1 = quantize_x(1)
-        place(0, 0, xm_q0, g_q0, "x_raw1")
-        xm_bf = sb("xm_bf0_late", [P, D // 2, PACK], BF16, "x_bf1")
-        nc.gpsimd.tensor_scalar(xm_bf[:], xm_raw[0][:, :, D // 2 :].rearrange("p j n -> p n j"), 1.0, 0.0, MULT, ADD)
-        quantize(xm_q0[0][:, D // 2 :], xm_q0[1][:, D // 2 :], xm_bf[:].rearrange("p n j -> p (n j)"), E4M3)
+        g_q0 = planes("g0", N)
+        g_bf0 = [
+            sb("g_bf0_0", [P, H, PACK], BF16)[:],
+            v_flat[:, PACK * B * N - H :].bitcast(BF16).rearrange("p (n j) -> p n j", j=PACK),
+        ]
+        xm_halves = [planes("xm0_%d" % h, H) for h in range(2)]
+        xm_q0 = [(xm_halves[k // 2], block(k % 2)) for k in range(D // P)]
+        banks = {}
 
-        v_bf = sb("v_bf1", [P, N, PACK], BF16)
-        nc.scalar.copy(interleaved(v_bf[:]), by_fours(v_picked[:, :, N:]))
-        v_codes = sb("v_codes1", [P, N], U32)
-        v_scales = sb("v_scales1", [P, N], U8)
-        quantize(v_codes[:], v_scales[:], v_bf[:].rearrange("p n j -> p (n j)"), E4M3)
-        place(0, 1, xm_q0, g_q0, "xm_raw0")
-
-        mean1 = sb("mean1", [P, N // 4, PACK, 4], F32)
-        for t in range(PACK):
-            rows = slice(t * P, (t + 1) * P)
-            a = psum_a.tile([P, N], F32, name="a")
-            nc.tensor.matmul_mx(
-                out=a[:],
-                lhsT=x_q1[0][:, rows].bitcast(E4M3),
-                lhsT_scale=x_q1[1][:, rows],
-                rhs=w_codes[:, N:].bitcast(E4M3),
-                rhs_scale=ws[:, N:],
-                start=True,
-                stop=True,
-            )
-            nc.scalar.activation(mean1[:, :, t, :], a[:].rearrange("p (c i) -> p c i", i=4), ACT.Exp)
-        banks = []
-        for t in range(PACK):
-            rows = slice(t * P, (t + 1) * P)
-            av = psum_av.tile([P, N], F32, name="av")
-            nc.tensor.matmul_mx(
-                out=av[:],
-                lhsT=x_q1[0][:, rows].bitcast(E4M3),
-                lhsT_scale=x_q1[1][:, rows],
-                rhs=v_codes[:].bitcast(E4M3),
-                rhs_scale=v_scales[:],
-                start=True,
-                stop=True,
-            )
-            banks.append(av)
-        av_wt = sb("av_wt", [P, N // 4, PACK, 4], F32)
-        g_bf = sb("g_bf1", [P, N, PACK], BF16)
-        for half in range(2):
-            fours = slice(half * N // 8, (half + 1) * N // 8)
+        def direction_chunk(c):
+            v_bf = sb("v_bf0_%d" % c, [P, CHUNK, PACK], BF16)
+            nc.scalar.copy(interleaved(v_bf[:]), by_fours(v_picked[:, :, block(c)]))
+            v_q = planes("v0_%d" % c, CHUNK)
+            quantize(v_q[0][:], v_q[1][:], flat(v_bf[:]), E4M3)
+            av = psum_av.tile([P, PACK, CHUNK], F32, name="av")
             for t in range(PACK):
+                mx(av[:, t, :], x_q0, block(t), v_q, slice(0, CHUNK), E4M3)
+            banks[c] = av
+
+        def multiply_chunk(c):
+            nc.vector.tensor_tensor(
+                interleaved(g_bf0[c // 2][:, block(c % 2), :]),
+                by_fours(banks[c][:]),
+                by_fours(mean0[:, :, block(c)]),
+                MULT,
+            )
+
+        def quantize_g0(h):
+            quantize(g_q0[0][:, block(h, H)], g_q0[1][:, block(h, H)], flat(g_bf0[h]), E5M2)
+
+        direction_chunk(0)
+        direction_chunk(1)
+        multiply_chunk(0)
+        direction_chunk(2)
+        multiply_chunk(1)
+        direction_chunk(3)
+        multiply_chunk(2)
+        quantize_g0(0)
+        multiply_chunk(3)
+        xm_bf = sb("xm_bf0_0", [P, H, PACK], BF16)
+        nc.scalar.copy(interleaved(xm_bf[:]), by_fours(xm_raw[0][:, :, :H]))
+        quantize(xm_halves[0][0][:], xm_halves[0][1][:], flat(xm_bf[:]), E4M3)
+        quantize_g0(1)
+
+        nc.vector.tensor_copy(v_picked[:, PACK - 1, N + H :], v_all[PACK - 1][:].indirect(listed(N + H, H)))
+        x_q1 = quantize_x(1, sb("x_bf1", [P, PACK, P, PACK], BF16)[:], (nc.scalar.copy, nc.scalar.copy))
+        place(0, 0, xm_q0, g_q0)
+        xm_bf = sb("xm_bf0_1", [P, H, PACK], BF16, "x_bf1")
+        nc.gpsimd.tensor_scalar(xm_bf[:], xm_raw[0][:, :, H:].rearrange("p j n -> p n j"), 1.0, 0.0, MULT, ADD)
+        quantize(xm_halves[1][0][:], xm_halves[1][1][:], flat(xm_bf[:]), E4M3)
+        v_bf1 = sb("v_bf1", [P, N, PACK], BF16, "xm0_0_codes")
+        nc.scalar.copy(interleaved(v_bf1[:]), by_fours(v_picked[:, :, N:]))
+        v_q1 = planes("v1", N)
+        quantize(v_q1[0][:], v_q1[1][:], flat(v_bf1[:]), E4M3)
+        place(0, 1, xm_q0, g_q0)
+
+        mean1 = [sb("mean1_%d" % h, [P, H // 4, PACK, 4], F32) for h in range(2)]
+        av_wt = [sb("av_wt_%d" % h, [P, H // 4, PACK, 4], F32) for h in range(2)]
+        g_bf1 = sb("g_bf1", [P, N, PACK], BF16)
+        for half in range(2):
+            for t0 in range(0, PACK, 2):
+                a = (psum_a if half == 0 else psum_av).tile([P, 2, H], F32, name="a" if half == 0 else "av")
+                for u in range(2):
+                    mx(a[:, u, :], x_q1, block(t0 + u), w_q, block(2 + half, H), E4M3)
                 nc.scalar.activation(
-                    av_wt[:, fours, t, :],
-                    banks[t][:].rearrange("p (c i) -> p c i", i=4)[:, fours, :],
-                    ACT.Copy,
-                    scale=wt_sb[:, 1, t : t + 1],
+                    mean1[half][:, :, t0 : t0 + 2, :], a[:].rearrange("p u (c i) -> p c u i", i=4), ACT.Exp
+                )
+        for half in range(2):
+            for t0 in range(0, PACK, 2):
+                av = psum_av.tile([P, 2, H], F32, name="av")
+                for u in range(2):
+                    mx(av[:, u, :], x_q1, block(t0 + u), v_q1, block(half, H), E4M3)
+                for u in range(2):
+                    nc.scalar.activation(
+                        av_wt[half][:, :, t0 + u, :],
+                        av[:, u, :].rearrange("p (c i) -> p c i", i=4),
+                        ACT.Copy,
+                        scale=wt_sb[:, 1, t0 + u : t0 + u + 1],
+                    )
+            for c in range(2):
+                part = block(c, CHUNK // 4)
+                nc.gpsimd.tensor_tensor(
+                    interleaved(g_bf1[:, block(2 * half + c), :]),
+                    mean1[half][:, part, :, :],
+                    av_wt[half][:, part, :, :],
+                    MULT,
                 )
             if half == 0:
-                place(0, 2, xm_q0, g_q0, "v_bf1")
-                last_acc = product(3, xm_q0, g_q0)
-                place_part(0, 3, last_acc, 0, N // 2, None)
-            for c0 in range(half * N // 2, (half + 1) * N // 2, CHUNK):
-                fours = slice(c0 // 4, (c0 + CHUNK) // 4)
-                nc.gpsimd.tensor_tensor(
-                    interleaved(g_bf[:, c0 : c0 + CHUNK, :]), mean1[:, fours, :, :], av_wt[:, fours, :, :], MULT
-                )
-        g_q1 = sb("g_codes1", [P, N], U32), sb("g_scales1", [P, N], U8)
-        quantize(g_q1[0][:], g_q1[1][:], g_bf[:].rearrange("p n j -> p (n j)"), E5M2)
-        xm_q1 = sb("xm_codes1", [P, D], U32), sb("xm_scales1", [P, D], U8)
-        quantize_xm(1, xm_q1, 0, D, "v_codes1")
-        place_part(0, 3, last_acc, N // 2, N // 2, "mean1")
+                place(0, 2, xm_q0, g_q0)
+        last_acc = product(3, xm_q0, g_q0)
+        place_part(0, 3, last_acc, 0, H)
+        xm_bf1 = sb("xm_bf1", [P, D, PACK], BF16, "mean1_0")
+        nc.scalar.copy(interleaved(xm_bf1[:]), by_fours(xm_raw[1][:]))
+        xm_planes = planes("xm1", D)
+        quantize(xm_planes[0][:], xm_planes[1][:], flat(xm_bf1[:]), E4M3)
+        xm_q1 = [(xm_planes, block(k)) for k in range(D // P)]
+        g_q1 = planes("g1", N)
+        quantize(g_q1[0][:], g_q1[1][:], flat(g_bf1[:]), E5M2)
+        place_part(0, 3, last_acc, H, H, "mean1_1")
         for k in range(D // P):
-            place(1, k, xm_q1, g_q1, None)
+            place(1, k, xm_q1, g_q1)
             nc.sync.dma_start(out[k * P : (k + 1) * P, :], placed[k][:])

@@ -58,8 +58,8 @@ def tile_attend_ghv_poi_kernel(tc, xT, w_words, w_scales, vT, wt, xm, offs, out)
             nc.sync.dma_start(xm_raw[b][:], xm[b].rearrange("(p j) d -> p j d", j=PACK))
 
         ws_src = w_scales[0].bitcast(I32)
-        for q in range(4):
-            nc.sync.dma_start(ws_all[32 * q : 32 * q + 4, :], ws_src[4 * q : 4 * q + 4, :])
+        for f in range(4):
+            nc.sync.dma_start(ws_all[f:P:32, :], ws_src[f:16:4, :])
         nc.sync.dma_start(w_all[:], w_words[0].rearrange("p n t -> p (n t)").bitcast(I32))
         load_x(0)
         v_rows = vT.rearrange("(p j) t -> p j t", j=PACK)
@@ -157,8 +157,8 @@ def tile_attend_ghv_poi_kernel(tc, xT, w_words, w_scales, vT, wt, xm, offs, out)
 
         g_q0 = planes("g0", N)
         g_bf0 = [
-            sb("g_bf0_0", [P, H, PACK], BF16)[:],
             v_flat[:, PACK * B * N - H :].bitcast(BF16).rearrange("p (n j) -> p n j", j=PACK),
+            sb("g_bf0_1", [P, H, PACK], BF16)[:],
         ]
         xm_halves = [planes("xm0_%d" % h, H) for h in range(2)]
         xm_q0 = [(xm_halves[k // 2], block(k % 2)) for k in range(D // P)]
@@ -187,16 +187,16 @@ def tile_attend_ghv_poi_kernel(tc, xT, w_words, w_scales, vT, wt, xm, offs, out)
 
         direction_chunk(0)
         direction_chunk(1)
-        multiply_chunk(0)
         direction_chunk(2)
-        multiply_chunk(1)
+        multiply_chunk(0)
         direction_chunk(3)
+        multiply_chunk(1)
         multiply_chunk(2)
-        quantize_g0(0)
         multiply_chunk(3)
         xm_bf = sb("xm_bf0_0", [P, H, PACK], BF16)
         nc.scalar.copy(interleaved(xm_bf[:]), by_fours(xm_raw[0][:, :, :H]))
         quantize(xm_halves[0][0][:], xm_halves[0][1][:], flat(xm_bf[:]), E4M3)
+        quantize_g0(0)
         quantize_g0(1)
 
         nc.vector.tensor_copy(v_picked[:, PACK - 1, N + H :], v_all[PACK - 1][:].indirect(listed(N + H, H)))

@@ -21,6 +21,8 @@ P = 128
 PACK = 4
 LIST_ROWS = 16
 CHUNK = 128
+X1_FIRST = 384
+X0_SCALAR = 384
 LAST_PLANE_PIECES = (256, 256, 256)
 
 
@@ -30,7 +32,7 @@ def tile_attend_ghv_poi_kernel(tc, xT, w_words, w_scales, vT, wt, xm, offs, out)
         keep = ctx.enter_context(tc.tile_pool(name="keep", bufs=1))
         psum_a = ctx.enter_context(tc.psum_pool(name="psum_a", bufs=2))
         psum_av = ctx.enter_context(tc.psum_pool(name="psum_av", bufs=4))
-        psum_dw = ctx.enter_context(tc.psum_pool(name="psum_dw", bufs=2))
+        psum_dw = ctx.enter_context(tc.psum_pool(name="psum_dw", bufs=1))
 
         def sb(name, shape, dtype, tag=None):
             return keep.tile(shape, dtype, name=name, tag=tag or name, align_bytes=64)
@@ -46,13 +48,13 @@ def tile_attend_ghv_poi_kernel(tc, xT, w_words, w_scales, vT, wt, xm, offs, out)
         wt_sb = sb("wt_sb", [P, B, PACK], F32)
         nc.sync.dma_start(wt_sb[:], wt.rearrange("b (p t) o -> p b (t o)", t=PACK))
 
-        x_raw = [sb("x_raw%d" % b, [P, PACK, R], F32) for b in range(B)]
+        v_flat = sb("v_flat", [P, PACK * B * N], F32)
+        v_picked = v_flat[:].rearrange("p (j n) -> p j n", j=PACK)
+        x_raw0 = v_flat[:, : PACK * R].rearrange("p (j r) -> p j r", j=PACK)
+        x_raw1 = [sb("x_raw1_0", [P, PACK, X1_FIRST], F32), sb("x_raw1_1", [P, PACK, R - X1_FIRST], F32)]
         xm_raw = [sb("xm_raw%d" % b, [P, PACK, D], F32) for b in range(B)]
         v_all = [sb("v_all%d" % j, [P, T], F32) for j in range(PACK)]
         w_all = sb("w_all", [P, T], I32)
-
-        def load_x(b):
-            nc.sync.dma_start(x_raw[b][:], xT[b].rearrange("(p j) r -> p j r", j=PACK))
 
         def load_xm(b):
             nc.sync.dma_start(xm_raw[b][:], xm[b].rearrange("(p j) d -> p j d", j=PACK))
@@ -61,12 +63,14 @@ def tile_attend_ghv_poi_kernel(tc, xT, w_words, w_scales, vT, wt, xm, offs, out)
         for f in range(4):
             nc.sync.dma_start(ws_all[f:P:32, :], ws_src[f:16:4, :])
         nc.sync.dma_start(w_all[:], w_words[0].rearrange("p n t -> p (n t)").bitcast(I32))
-        load_x(0)
+        nc.sync.dma_start(x_raw0, xT[0].rearrange("(p j) r -> p j r", j=PACK))
         v_rows = vT.rearrange("(p j) t -> p j t", j=PACK)
         for j in range(PACK):
             nc.sync.dma_start(v_all[j][:], v_rows[:, j, :])
         load_xm(0)
-        load_x(1)
+        x1_rows = xT[1].rearrange("(p j) r -> p j r", j=PACK)
+        nc.sync.dma_start(x_raw1[0][:], x1_rows[:, :, :X1_FIRST])
+        nc.sync.dma_start(x_raw1[1][:], x1_rows[:, :, X1_FIRST:])
         load_xm(1)
 
         placed = [sb("placed%d" % k, [P, T], F32) for k in range(2)]
@@ -102,17 +106,19 @@ def tile_attend_ghv_poi_kernel(tc, xT, w_words, w_scales, vT, wt, xm, offs, out)
         def planes(name, width, tag=None):
             return sb(name + "_codes", [P, width], U32, tag), sb(name + "_scales", [P, width], U8)
 
-        def quantize_x(b, x_bf, copies):
-            src = x_raw[b][:].rearrange("p j (m e t) -> p m j e t", e=2, t=PACK)
+        def deal_x(copy_by, x_bf, raw, first, t0):
+            src = raw.rearrange("p j (m e t) -> p m j e t", e=2, t=PACK)
             dst = x_bf.rearrange("p t (m e) j -> p m j e t", e=2)
-            for t0, copy_by in zip(range(0, PACK, 2), copies):
-                copy_by(dst[:, :, :, :, t0 : t0 + 2], src[:, :, :, :, t0 : t0 + 2])
+            pairs = slice(first // 8, first // 8 + src.shape[1])
+            copy_by(dst[:, pairs, :, :, t0 : t0 + 2], src[:, :, :, :, t0 : t0 + 2])
+
+        def quantize_x(b, x_bf):
             x_q = planes("x%d" % b, R)
             quantize(x_q[0][:], x_q[1][:], x_bf.rearrange("p t m j -> p (t m j)"), E4M3)
             return x_q
 
-        def product(k, xm_q, g_q):
-            acc = psum_dw.tile([P, N], F32, name="acc")
+        def product(k, xm_q, g_q, bank):
+            acc = psum_dw.tile([P, N], F32, name="acc%d" % bank)
             mx(acc[:], xm_q[k][0], xm_q[k][1], g_q, slice(0, N), E5M2)
             return acc
 
@@ -121,8 +127,8 @@ def tile_attend_ghv_poi_kernel(tc, xT, w_words, w_scales, vT, wt, xm, offs, out)
             nc.scalar.copy(dw[:], acc[:, first : first + count])
             nc.vector.tensor_copy(placed[k][:].indirect(listed(b * N + first, count)), dw[:])
 
-        def place(b, k, xm_q, g_q):
-            place_part(b, k, product(k, xm_q, g_q), 0, N)
+        def place(b, k, xm_q, g_q, bank):
+            place_part(b, k, product(k, xm_q, g_q, bank), 0, N)
 
         H = N // 2
 
@@ -130,10 +136,11 @@ def tile_attend_ghv_poi_kernel(tc, xT, w_words, w_scales, vT, wt, xm, offs, out)
         nc.vector.tensor_copy(ws[:], ws_all[:].bitcast(U8).indirect(offsets[:]))
         w_codes = sb("w_codes", [P, B * N], U32)
         nc.vector.tensor_copy(w_codes[:], w_all[:].bitcast(U32).indirect(offsets[:]))
-        v_flat = sb("v_flat", [P, PACK * B * N + H], F32)
-        v_picked = v_flat[:, : PACK * B * N].rearrange("p (j n) -> p j n", j=PACK)
-        x_bf0 = v_picked[:, 0, :].bitcast(BF16).rearrange("p (t m j) -> p t m j", t=PACK, j=PACK)
-        x_q0 = quantize_x(0, x_bf0, (nc.scalar.copy, nc.vector.tensor_copy))
+        x_bf0 = sb("x_bf0", [P, PACK, P, PACK], BF16)[:]
+        deal_x(nc.scalar.copy, x_bf0, x_raw0[:, :, :X0_SCALAR], 0, 0)
+        deal_x(nc.vector.tensor_copy, x_bf0, x_raw0, 0, 2)
+        deal_x(nc.vector.tensor_copy, x_bf0, x_raw0[:, :, X0_SCALAR:], X0_SCALAR, 0)
+        x_q0 = quantize_x(0, x_bf0)
         w_q = w_codes, ws
         mean0 = sb("mean0", [P, PACK, N], F32)
         for t in range(PACK):
@@ -155,20 +162,19 @@ def tile_attend_ghv_poi_kernel(tc, xT, w_words, w_scales, vT, wt, xm, offs, out)
             placed.append(sb("placed%d" % k, [P, T], F32, "v_all%d" % (k - 2)))
             nc.gpsimd.memset(placed[k][:], 0.0)
 
-        g_q0 = planes("g0", N)
-        g_bf0 = [
-            v_flat[:, PACK * B * N - H :].bitcast(BF16).rearrange("p (n j) -> p n j", j=PACK),
-            sb("g_bf0_1", [P, H, PACK], BF16)[:],
-        ]
-        xm_halves = [planes("xm0_%d" % h, H) for h in range(2)]
-        xm_q0 = [(xm_halves[k // 2], block(k % 2)) for k in range(D // P)]
+        g_wide = planes("g0", H + N)
+        nc.gpsimd.memset(g_wide[0][:, :H].bitcast(I32), 0)
+        nc.gpsimd.memset(g_wide[1][:, :H].bitcast(I32), 0)
+        g_q0 = g_wide[0][:, H:], g_wide[1][:, H:]
+        g_bf0 = [sb("g_bf0_%d" % h, [P, H, PACK], BF16) for h in range(2)]
+        xm_parts = [planes("xm0_0", P), planes("xm0_1", P)]
+        xm_q0 = [(xm_parts[0], block(0)), (xm_parts[1], block(0))]
         banks = {}
 
-        def direction_chunk(c):
-            v_bf = sb("v_bf0_%d" % c, [P, CHUNK, PACK], BF16)
-            nc.scalar.copy(interleaved(v_bf[:]), by_fours(v_picked[:, :, block(c)]))
+        def direction_chunk(c, v_bf):
+            nc.scalar.copy(interleaved(v_bf), by_fours(v_picked[:, :, block(c)]))
             v_q = planes("v0_%d" % c, CHUNK)
-            quantize(v_q[0][:], v_q[1][:], flat(v_bf[:]), E4M3)
+            quantize(v_q[0][:], v_q[1][:], flat(v_bf), E4M3)
             av = psum_av.tile([P, PACK, CHUNK], F32, name="av")
             for t in range(PACK):
                 mx(av[:, t, :], x_q0, block(t), v_q, slice(0, CHUNK), E4M3)
@@ -183,33 +189,54 @@ def tile_attend_ghv_poi_kernel(tc, xT, w_words, w_scales, vT, wt, xm, offs, out)
             )
 
         def quantize_g0(h):
-            quantize(g_q0[0][:, block(h, H)], g_q0[1][:, block(h, H)], flat(g_bf0[h]), E5M2)
+            quantize(g_q0[0][:, block(h, H)], g_q0[1][:, block(h, H)], flat(g_bf0[h][:]), E5M2)
 
-        direction_chunk(0)
-        direction_chunk(1)
-        direction_chunk(2)
+        def quantize_xm0(k):
+            xm_bf = sb("xm_bf0_%d" % k, [P, P, PACK], BF16)
+            nc.scalar.copy(interleaved(xm_bf[:]), by_fours(xm_raw[0][:, :, block(k)]))
+            quantize(xm_parts[k][0][:], xm_parts[k][1][:], flat(xm_bf[:]), E4M3)
+
+        def own_bf(c):
+            return sb("v_bf0_%d" % c, [P, CHUNK, PACK], BF16)[:]
+
+        last_picked = v_picked[:, PACK - 1, N + H :]
+        direction_chunk(0, last_picked.bitcast(BF16).rearrange("p (n j) -> p n j", j=PACK))
+        nc.vector.tensor_copy(last_picked, v_all[PACK - 1][:].indirect(listed(N + H, H)))
+        direction_chunk(1, own_bf(1))
+        direction_chunk(2, own_bf(2))
         multiply_chunk(0)
-        direction_chunk(3)
+        direction_chunk(3, own_bf(3))
         multiply_chunk(1)
+        quantize_xm0(0)
+        quantize_g0(0)
+        early = product(0, xm_q0, g_wide, 0)
         multiply_chunk(2)
         multiply_chunk(3)
-        xm_bf = sb("xm_bf0_0", [P, H, PACK], BF16)
-        nc.scalar.copy(interleaved(xm_bf[:]), by_fours(xm_raw[0][:, :, :H]))
-        quantize(xm_halves[0][0][:], xm_halves[0][1][:], flat(xm_bf[:]), E4M3)
-        quantize_g0(0)
+        quantize_xm0(1)
         quantize_g0(1)
 
-        nc.vector.tensor_copy(v_picked[:, PACK - 1, N + H :], v_all[PACK - 1][:].indirect(listed(N + H, H)))
-        x_q1 = quantize_x(1, sb("x_bf1", [P, PACK, P, PACK], BF16)[:], (nc.scalar.copy, nc.scalar.copy))
-        place(0, 0, xm_q0, g_q0)
-        xm_bf = sb("xm_bf0_1", [P, H, PACK], BF16, "x_bf1")
+        x_bf1 = sb("x_bf1", [P, PACK, P, PACK], BF16)[:]
+        for t0 in range(0, PACK, 2):
+            deal_x(nc.scalar.copy, x_bf1, x_raw1[0][:], 0, t0)
+        spent = x_raw1[0][:].rearrange("p j r -> p (j r)")
+        dw = spent[:, :H]
+        nc.scalar.copy(dw, early[:, H:])
+        nc.vector.tensor_copy(placed[0][:].indirect(listed(0, H)), dw)
+        for t0 in range(0, PACK, 2):
+            deal_x(nc.scalar.copy, x_bf1, x_raw1[1][:], X1_FIRST, t0)
+        x_q1 = quantize_x(1, x_bf1)
+        xm_bf = sb("xm_bf0_2", [P, H, PACK], BF16, "g_bf0_1")
         nc.gpsimd.tensor_scalar(xm_bf[:], xm_raw[0][:, :, H:].rearrange("p j n -> p n j"), 1.0, 0.0, MULT, ADD)
-        quantize(xm_halves[1][0][:], xm_halves[1][1][:], flat(xm_bf[:]), E4M3)
-        v_bf1 = sb("v_bf1", [P, N, PACK], BF16, "xm0_0_codes")
-        nc.scalar.copy(interleaved(v_bf1[:]), by_fours(v_picked[:, :, N:]))
+        late = planes("xm0_2", H, "x_raw1_1")
+        quantize(late[0][:], late[1][:], flat(xm_bf[:]), E4M3)
+        xm_q0.extend([(late, block(0)), (late, block(1))])
+        v_bf1 = spent[:, N:].bitcast(BF16).rearrange("p (n j) -> p n j", j=PACK)
+        nc.scalar.copy(interleaved(v_bf1[:, :H, :]), by_fours(v_picked[:, :, N : N + H]))
+        place_part(0, 0, product(0, xm_q0, g_q0, 1), H, H)
+        nc.scalar.copy(interleaved(v_bf1[:, H:, :]), by_fours(v_picked[:, :, N + H :]))
         v_q1 = planes("v1", N)
-        quantize(v_q1[0][:], v_q1[1][:], flat(v_bf1[:]), E4M3)
-        place(0, 1, xm_q0, g_q0)
+        quantize(v_q1[0][:], v_q1[1][:], flat(v_bf1), E4M3)
+        place(0, 1, xm_q0, g_q0, 0)
 
         mean1 = [sb("mean1_%d" % h, [P, H // 4, PACK, 4], F32) for h in range(2)]
         av_wt = [sb("av_wt_%d" % h, [P, H // 4, PACK, 4], F32) for h in range(2)]
@@ -243,10 +270,10 @@ def tile_attend_ghv_poi_kernel(tc, xT, w_words, w_scales, vT, wt, xm, offs, out)
                     MULT,
                 )
             if half == 0:
-                place(0, 2, xm_q0, g_q0)
-        last_acc = product(3, xm_q0, g_q0)
+                place(0, 2, xm_q0, g_q0, 1)
+        last_acc = product(3, xm_q0, g_q0, 1)
         place_part(0, 3, last_acc, 0, H)
-        xm_bf1 = sb("xm_bf1", [P, D, PACK], BF16, "mean1_0")
+        xm_bf1 = sb("xm_bf1", [P, D, PACK], BF16, "wt_sb")
         nc.scalar.copy(interleaved(xm_bf1[:]), by_fours(xm_raw[1][:]))
         xm_planes = planes("xm1", D)
         quantize(xm_planes[0][:], xm_planes[1][:], flat(xm_bf1[:]), E4M3)
@@ -255,5 +282,5 @@ def tile_attend_ghv_poi_kernel(tc, xT, w_words, w_scales, vT, wt, xm, offs, out)
         quantize(g_q1[0][:], g_q1[1][:], flat(g_bf1[:]), E5M2)
         place_part(0, 3, last_acc, H, H, "mean1_1")
         for k in range(D // P):
-            place(1, k, xm_q1, g_q1)
-            nc.sync.dma_start(out[k * P : (k + 1) * P, :], placed[k][:])
+            place(1, k, xm_q1, g_q1, k % 2)
+            nc.sync.dma_start(out[block(k), :], placed[k][:])

@@ -225,17 +225,18 @@ def tile_attend_ghv_poi_kernel(tc, xT, w_words, w_scales, vT, wt, xm, offs, out)
         for t0 in range(0, PACK, 2):
             deal_x(nc.scalar.copy, x_bf1, x_raw1[1][:], X1_FIRST, t0)
         x_q1 = quantize_x(1, x_bf1)
-        xm_bf = sb("xm_bf0_2", [P, H, PACK], BF16, "g_bf0_1")
-        nc.gpsimd.tensor_scalar(xm_bf[:], xm_raw[0][:, :, H:].rearrange("p j n -> p n j"), 1.0, 0.0, MULT, ADD)
-        late = planes("xm0_2", H, "x_raw1_1")
-        quantize(late[0][:], late[1][:], flat(xm_bf[:]), E4M3)
-        xm_q0.extend([(late, block(0)), (late, block(1))])
         v_bf1 = spent[:, N:].bitcast(BF16).rearrange("p (n j) -> p n j", j=PACK)
+        v_late = sb("v_late", [P, H, PACK], BF16, "g_bf0_1")
+        nc.gpsimd.tensor_scalar(v_late[:], v_picked[:, :, N + H :].rearrange("p j n -> p n j"), 1.0, 0.0, MULT, ADD)
         nc.scalar.copy(interleaved(v_bf1[:, :H, :]), by_fours(v_picked[:, :, N : N + H]))
+        v_q1 = planes("v1", N, "x_raw1_1")
+        quantize(v_q1[0][:, :H], v_q1[1][:, :H], flat(v_bf1[:, :H, :]), E4M3)
+        quantize(v_q1[0][:, H:], v_q1[1][:, H:], flat(v_late[:]), E4M3)
         place_part(0, 0, product(0, xm_q0, g_q0, 1), H, H)
-        nc.scalar.copy(interleaved(v_bf1[:, H:, :]), by_fours(v_picked[:, :, N + H :]))
-        v_q1 = planes("v1", N)
-        quantize(v_q1[0][:], v_q1[1][:], flat(v_bf1), E4M3)
+        nc.scalar.copy(interleaved(v_bf1[:, H:, :]), by_fours(xm_raw[0][:, :, H:]))
+        late = planes("xm0_2", H)
+        quantize(late[0][:], late[1][:], flat(v_bf1[:, H:, :]), E4M3)
+        xm_q0.extend([(late, block(0)), (late, block(1))])
         place(0, 1, xm_q0, g_q0, 0)
 
         mean1 = [sb("mean1_%d" % h, [P, H // 4, PACK, 4], F32) for h in range(2)]
@@ -243,15 +244,16 @@ def tile_attend_ghv_poi_kernel(tc, xT, w_words, w_scales, vT, wt, xm, offs, out)
         g_bf1 = sb("g_bf1", [P, N, PACK], BF16)
         for half in range(2):
             for t0 in range(0, PACK, 2):
-                a = (psum_a if half == 0 else psum_av).tile([P, 2, H], F32, name="a" if half == 0 else "av")
+                a = (psum_a, psum_av)[half].tile([P, 2, H], F32, name=("a", "av")[half])
                 for u in range(2):
                     mx(a[:, u, :], x_q1, block(t0 + u), w_q, block(2 + half, H), E4M3)
                 nc.scalar.activation(
                     mean1[half][:, :, t0 : t0 + 2, :], a[:].rearrange("p u (c i) -> p c u i", i=4), ACT.Exp
                 )
-        for half in range(2):
+            if half == 1:
+                place(0, 2, xm_q0, g_q0, 1)
             for t0 in range(0, PACK, 2):
-                av = psum_av.tile([P, 2, H], F32, name="av")
+                av = (psum_av, psum_a)[half].tile([P, 2, H], F32, name=("av", "a")[half])
                 for u in range(2):
                     mx(av[:, u, :], x_q1, block(t0 + u), v_q1, block(half, H), E4M3)
                 for u in range(2):
@@ -269,18 +271,19 @@ def tile_attend_ghv_poi_kernel(tc, xT, w_words, w_scales, vT, wt, xm, offs, out)
                     av_wt[half][:, part, :, :],
                     MULT,
                 )
-            if half == 0:
-                place(0, 2, xm_q0, g_q0, 1)
         last_acc = product(3, xm_q0, g_q0, 1)
         place_part(0, 3, last_acc, 0, H)
         xm_bf1 = sb("xm_bf1", [P, D, PACK], BF16, "wt_sb")
         nc.scalar.copy(interleaved(xm_bf1[:]), by_fours(xm_raw[1][:]))
-        xm_planes = planes("xm1", D)
-        quantize(xm_planes[0][:], xm_planes[1][:], flat(xm_bf1[:]), E4M3)
-        xm_q1 = [(xm_planes, block(k)) for k in range(D // P)]
+        xm_first = planes("xm1_0", P)
+        quantize(xm_first[0][:], xm_first[1][:], flat(xm_bf1[:, :P, :]), E4M3)
         g_q1 = planes("g1", N)
         quantize(g_q1[0][:], g_q1[1][:], flat(g_bf1[:]), E5M2)
         place_part(0, 3, last_acc, H, H, "mean1_1")
+        xm_rest = planes("xm1_1", D - P, "g_bf1")
+        quantize(xm_rest[0][:, :P], xm_rest[1][:, :P], flat(xm_bf1[:, P:H, :]), E4M3)
+        quantize(xm_rest[0][:, P:], xm_rest[1][:, P:], flat(xm_bf1[:, H:, :]), E4M3)
+        xm_q1 = [(xm_first, block(0))] + [(xm_rest, block(k)) for k in range(D // P - 1)]
         for k in range(D // P):
             place(1, k, xm_q1, g_q1, k % 2)
             nc.sync.dma_start(out[block(k), :], placed[k][:])

@@ -172,7 +172,7 @@ def tile_attend_ghv_poi_kernel(tc, xT, w_words, w_scales, vT, wt, xm, offs, out)
         banks = {}
 
         def direction_chunk(c, v_bf):
-            nc.scalar.copy(interleaved(v_bf), by_fours(v_picked[:, :, block(c)]))
+            nc.scalar.copy(interleaved(v_bf[:, :, 2:]), by_fours(v_picked[:, 2:, block(c)]))
             v_q = planes("v0_%d" % c, CHUNK)
             quantize(v_q[0][:], v_q[1][:], flat(v_bf), E4M3)
             av = psum_av.tile([P, PACK, CHUNK], F32, name="av")
@@ -200,12 +200,15 @@ def tile_attend_ghv_poi_kernel(tc, xT, w_words, w_scales, vT, wt, xm, offs, out)
             return sb("v_bf0_%d" % c, [P, CHUNK, PACK], BF16)[:]
 
         last_picked = v_picked[:, PACK - 1, N + H :]
-        direction_chunk(0, last_picked.bitcast(BF16).rearrange("p (n j) -> p n j", j=PACK))
+        v_bf0 = [last_picked.bitcast(BF16).rearrange("p (n j) -> p n j", j=PACK)] + [own_bf(c) for c in range(1, 4)]
+        for c in range(4):
+            nc.scalar.copy(interleaved(v_bf0[c][:, :, :2]), by_fours(v_picked[:, :2, block(c)]))
+        direction_chunk(0, v_bf0[0])
         nc.vector.tensor_copy(last_picked, v_all[PACK - 1][:].indirect(listed(N + H, H)))
-        direction_chunk(1, own_bf(1))
-        direction_chunk(2, own_bf(2))
+        direction_chunk(1, v_bf0[1])
+        direction_chunk(2, v_bf0[2])
         multiply_chunk(0)
-        direction_chunk(3, own_bf(3))
+        direction_chunk(3, v_bf0[3])
         multiply_chunk(1)
         quantize_xm0(0)
         quantize_g0(0)

@@ -229,16 +229,27 @@ def tile_attend_ghv_poi_kernel(tc, xT, w_words, w_scales, vT, wt, xm, offs, out)
             deal_x(nc.scalar.copy, x_bf1, x_raw1[1][:], X1_FIRST, t0)
         x_q1 = quantize_x(1, x_bf1)
         v_bf1 = spent[:, N:].bitcast(BF16).rearrange("p (n j) -> p n j", j=PACK)
-        v_late = sb("v_late", [P, H, PACK], BF16, "g_bf0_1")
-        nc.gpsimd.tensor_scalar(v_late[:], v_picked[:, :, N + H :].rearrange("p j n -> p n j"), 1.0, 0.0, MULT, ADD)
+
+        def weave_on_gpsimd(c, v_late):
+            cols = block(N // CHUNK + c)
+            nc.gpsimd.tensor_scalar(v_late, v_picked[:, :, cols].rearrange("p j n -> p n j"), 1.0, 0.0, MULT, ADD)
+
+        def quantize_late(c, v_late):
+            quantize(v_q1[0][:, block(c)], v_q1[1][:, block(c)], flat(v_late), E4M3)
+
+        v_late = sb("v_late", [P, CHUNK, PACK], BF16, "g_bf0_1")[:]
+        weave_on_gpsimd(2, v_late)
         nc.scalar.copy(interleaved(v_bf1[:, :H, :]), by_fours(v_picked[:, :, N : N + H]))
         v_q1 = planes("v1", N, "x_raw1_1")
+        quantize_late(2, v_late)
         quantize(v_q1[0][:, :H], v_q1[1][:, :H], flat(v_bf1[:, :H, :]), E4M3)
-        quantize(v_q1[0][:, H:], v_q1[1][:, H:], flat(v_late[:]), E4M3)
+        v_last = v_bf1[:, :CHUNK, :]
+        weave_on_gpsimd(3, v_last)
         place_part(0, 0, product(0, xm_q0, g_q0, 1), H, H)
         nc.scalar.copy(interleaved(v_bf1[:, H:, :]), by_fours(xm_raw[0][:, :, H:]))
         late = planes("xm0_2", H)
         quantize(late[0][:], late[1][:], flat(v_bf1[:, H:, :]), E4M3)
+        quantize_late(3, v_last)
         xm_q0.extend([(late, block(0)), (late, block(1))])
         place(0, 1, xm_q0, g_q0, 0)
 

@@ -30,9 +30,10 @@ def tile_attend_ghv_poi_kernel(tc, xT, w_words, w_scales, vT, wt, xm, offs, out)
     nc = tc.nc
     with ExitStack() as ctx:
         keep = ctx.enter_context(tc.tile_pool(name="keep", bufs=1))
-        psum_a = ctx.enter_context(tc.psum_pool(name="psum_a", bufs=2))
-        psum_av = ctx.enter_context(tc.psum_pool(name="psum_av", bufs=4))
-        psum_dw = ctx.enter_context(tc.psum_pool(name="psum_dw", bufs=1))
+        psum = ctx.enter_context(tc.psum_pool(name="psum", bufs=1))
+
+        def in_bank(i, shape):
+            return psum.tile(shape, F32, name="bank%d" % i)
 
         def sb(name, shape, dtype, tag=None):
             return keep.tile(shape, dtype, name=name, tag=tag or name, align_bytes=64)
@@ -118,7 +119,7 @@ def tile_attend_ghv_poi_kernel(tc, xT, w_words, w_scales, vT, wt, xm, offs, out)
             return x_q
 
         def product(k, xm_q, g_q, bank):
-            acc = psum_dw.tile([P, N], F32, name="acc%d" % bank)
+            acc = in_bank(bank, [P, N])
             mx(acc[:], xm_q[k][0], xm_q[k][1], g_q, slice(0, N), E5M2)
             return acc
 
@@ -144,7 +145,7 @@ def tile_attend_ghv_poi_kernel(tc, xT, w_words, w_scales, vT, wt, xm, offs, out)
         w_q = w_codes, ws
         mean0 = sb("mean0", [P, PACK, N], F32)
         for t in range(PACK):
-            a = psum_a.tile([P, N], F32, name="a")
+            a = in_bank(t % 2, [P, N])
             mx(a[:], x_q0, block(t), w_q, slice(0, N), E4M3)
             nc.scalar.activation(mean0[:, t, :], a[:], ACT.Exp)
         for t in range(PACK):
@@ -175,7 +176,7 @@ def tile_attend_ghv_poi_kernel(tc, xT, w_words, w_scales, vT, wt, xm, offs, out)
             nc.scalar.copy(interleaved(v_bf[:, :, 2:]), by_fours(v_picked[:, 2:, block(c)]))
             v_q = planes("v0_%d" % c, CHUNK)
             quantize(v_q[0][:], v_q[1][:], flat(v_bf), E4M3)
-            av = psum_av.tile([P, PACK, CHUNK], F32, name="av")
+            av = in_bank(2 + c, [P, PACK, CHUNK])
             for t in range(PACK):
                 mx(av[:, t, :], x_q0, block(t), v_q, slice(0, CHUNK), E4M3)
             banks[c] = av
@@ -212,7 +213,7 @@ def tile_attend_ghv_poi_kernel(tc, xT, w_words, w_scales, vT, wt, xm, offs, out)
         multiply_chunk(1)
         quantize_xm0(0)
         quantize_g0(0)
-        early = product(0, xm_q0, g_wide, 0)
+        early = product(0, xm_q0, g_wide, 6)
         multiply_chunk(2)
         multiply_chunk(3)
         quantize_xm0(1)
@@ -245,47 +246,55 @@ def tile_attend_ghv_poi_kernel(tc, xT, w_words, w_scales, vT, wt, xm, offs, out)
         quantize(v_q1[0][:, :H], v_q1[1][:, :H], flat(v_bf1[:, :H, :]), E4M3)
         v_last = v_bf1[:, :CHUNK, :]
         weave_on_gpsimd(3, v_last)
-        place_part(0, 0, product(0, xm_q0, g_q0, 1), H, H)
+        place_part(0, 0, product(0, xm_q0, g_q0, 7), H, H)
         nc.scalar.copy(interleaved(v_bf1[:, H:, :]), by_fours(xm_raw[0][:, :, H:]))
         late = planes("xm0_2", H)
         quantize(late[0][:], late[1][:], flat(v_bf1[:, H:, :]), E4M3)
         quantize_late(3, v_last)
         xm_q0.extend([(late, block(0)), (late, block(1))])
-        place(0, 1, xm_q0, g_q0, 0)
+        place(0, 1, xm_q0, g_q0, 6)
 
         mean1 = [sb("mean1_%d" % h, [P, H // 4, PACK, 4], F32) for h in range(2)]
         av_wt = [sb("av_wt_%d" % h, [P, H // 4, PACK, 4], F32) for h in range(2)]
         g_bf1 = sb("g_bf1", [P, N, PACK], BF16)
-        for half in range(2):
-            for t0 in range(0, PACK, 2):
-                a = (psum_a, psum_av)[half].tile([P, 2, H], F32, name=("a", "av")[half])
+
+        def mean_chunk(c):
+            a = in_bank(c % 2, [P, PACK, CHUNK])
+            for t in range(PACK):
+                mx(a[:, t, :], x_q1, block(t), w_q, block(N // CHUNK + c), E4M3)
+            nc.scalar.activation(mean1[c // 2][:, block(c % 2, CHUNK // 4), :, :], by_fours(a[:]), ACT.Exp)
+
+        def weighted_half(half):
+            for pair in range(2):
+                av = in_bank(2 + 2 * half + pair, [P, 2, H])
                 for u in range(2):
-                    mx(a[:, u, :], x_q1, block(t0 + u), w_q, block(2 + half, H), E4M3)
-                nc.scalar.activation(
-                    mean1[half][:, :, t0 : t0 + 2, :], a[:].rearrange("p u (c i) -> p c u i", i=4), ACT.Exp
-                )
-            if half == 1:
-                place(0, 2, xm_q0, g_q0, 1)
-            for t0 in range(0, PACK, 2):
-                av = (psum_av, psum_a)[half].tile([P, 2, H], F32, name=("av", "a")[half])
+                    mx(av[:, u, :], x_q1, block(2 * pair + u), v_q1, block(half, H), E4M3)
                 for u in range(2):
-                    mx(av[:, u, :], x_q1, block(t0 + u), v_q1, block(half, H), E4M3)
-                for u in range(2):
+                    t = 2 * pair + u
                     nc.scalar.activation(
-                        av_wt[half][:, :, t0 + u, :],
+                        av_wt[half][:, :, t, :],
                         av[:, u, :].rearrange("p (c i) -> p c i", i=4),
                         ACT.Copy,
-                        scale=wt_sb[:, 1, t0 + u : t0 + u + 1],
+                        scale=wt_sb[:, 1, t : t + 1],
                     )
-            for c in range(2):
-                part = block(c, CHUNK // 4)
-                nc.gpsimd.tensor_tensor(
-                    interleaved(g_bf1[:, block(2 * half + c), :]),
-                    mean1[half][:, part, :, :],
-                    av_wt[half][:, part, :, :],
-                    MULT,
-                )
-        last_acc = product(3, xm_q0, g_q0, 1)
+
+        def multiply_group1(c):
+            part = block(c % 2, CHUNK // 4)
+            nc.gpsimd.tensor_tensor(
+                interleaved(g_bf1[:, block(c), :]), mean1[c // 2][:, part, :, :], av_wt[c // 2][:, part, :, :], MULT
+            )
+
+        mean_chunk(0)
+        mean_chunk(1)
+        weighted_half(0)
+        multiply_group1(0)
+        multiply_group1(1)
+        place(0, 2, xm_q0, g_q0, 7)
+        weighted_half(1)
+        for c in (2, 3):
+            mean_chunk(c)
+            multiply_group1(c)
+        last_acc = product(3, xm_q0, g_q0, 7)
         place_part(0, 3, last_acc, 0, H)
         xm_bf1 = sb("xm_bf1", [P, D, PACK], BF16, "wt_sb")
         nc.scalar.copy(interleaved(xm_bf1[:]), by_fours(xm_raw[1][:]))
@@ -299,5 +308,5 @@ def tile_attend_ghv_poi_kernel(tc, xT, w_words, w_scales, vT, wt, xm, offs, out)
         quantize(xm_rest[0][:, P:], xm_rest[1][:, P:], flat(xm_bf1[:, H:, :]), E4M3)
         xm_q1 = [(xm_first, block(0))] + [(xm_rest, block(k)) for k in range(D // P - 1)]
         for k in range(D // P):
-            place(1, k, xm_q1, g_q1, k % 2)
+            place(1, k, xm_q1, g_q1, 6 + k % 2)
             nc.sync.dma_start(out[block(k), :], placed[k][:])

@@ -23,6 +23,7 @@ LIST_ROWS = 16
 CHUNK = 128
 X1_FIRST = 384
 X0_SCALAR = 384
+SCALE_FIRST = 32
 LAST_PLANE_PIECES = (256, 256, 256)
 
 
@@ -46,33 +47,26 @@ def tile_attend_ghv_poi_kernel(tc, xT, w_words, w_scales, vT, wt, xm, offs, out)
 
         ws_all = sb("ws_all", [P, T // 4], I32)
         nc.gpsimd.memset(ws_all[:], 0)
+        ws = sb("ws", [P, B * N // 4], I32)
+        nc.gpsimd.memset(ws[:], 0)
         wt_sb = sb("wt_sb", [P, B, PACK], F32)
         nc.sync.dma_start(wt_sb[:], wt.rearrange("b (p t) o -> p b (t o)", t=PACK))
 
         v_flat = sb("v_flat", [P, PACK * B * N], F32)
         v_picked = v_flat[:].rearrange("p (j n) -> p j n", j=PACK)
         x_raw0 = v_flat[:, : PACK * R].rearrange("p (j r) -> p j r", j=PACK)
-        x_raw1 = [sb("x_raw1_0", [P, PACK, X1_FIRST], F32), sb("x_raw1_1", [P, PACK, R - X1_FIRST], F32)]
-        xm_raw = [sb("xm_raw%d" % b, [P, PACK, D], F32) for b in range(B)]
-        v_all = [sb("v_all%d" % j, [P, T], F32) for j in range(PACK)]
+        v_all = [sb("v_all0", [P, T], F32)]
         w_all = sb("w_all", [P, T], I32)
 
-        def load_xm(b):
-            nc.sync.dma_start(xm_raw[b][:], xm[b].rearrange("(p j) d -> p j d", j=PACK))
-
-        ws_src = w_scales[0].bitcast(I32)
-        for f in range(4):
-            nc.sync.dma_start(ws_all[f:P:32, :], ws_src[f:16:4, :])
+        nc.sync.dma_start(ws_all[SCALE_FIRST : SCALE_FIRST + 16 * 4 : 4, :], w_scales[0].bitcast(I32))
         nc.sync.dma_start(w_all[:], w_words[0].rearrange("p n t -> p (n t)").bitcast(I32))
         nc.sync.dma_start(x_raw0, xT[0].rearrange("(p j) r -> p j r", j=PACK))
         v_rows = vT.rearrange("(p j) t -> p j t", j=PACK)
-        for j in range(PACK):
+        nc.sync.dma_start(v_all[0][:], v_rows[:, 0, :])
+
+        def load_plane(j, tag):
+            v_all.append(sb("v_all%d" % j, [P, T], F32, tag))
             nc.sync.dma_start(v_all[j][:], v_rows[:, j, :])
-        load_xm(0)
-        x1_rows = xT[1].rearrange("(p j) r -> p j r", j=PACK)
-        nc.sync.dma_start(x_raw1[0][:], x1_rows[:, :, :X1_FIRST])
-        nc.sync.dma_start(x_raw1[1][:], x1_rows[:, :, X1_FIRST:])
-        load_xm(1)
 
         placed = [sb("placed%d" % k, [P, T], F32) for k in range(2)]
         for k in range(2):
@@ -111,7 +105,7 @@ def tile_attend_ghv_poi_kernel(tc, xT, w_words, w_scales, vT, wt, xm, offs, out)
             src = raw.rearrange("p j (m e t) -> p m j e t", e=2, t=PACK)
             dst = x_bf.rearrange("p t (m e) j -> p m j e t", e=2)
             pairs = slice(first // 8, first // 8 + src.shape[1])
-            copy_by(dst[:, pairs, :, :, t0 : t0 + 2], src[:, :, :, :, t0 : t0 + 2])
+            copy_by(dst[:, pairs, :, :, :], src[:, :, :, :, t0 : t0 + 2])
 
         def quantize_x(b, x_bf):
             x_q = planes("x%d" % b, R)
@@ -133,16 +127,34 @@ def tile_attend_ghv_poi_kernel(tc, xT, w_words, w_scales, vT, wt, xm, offs, out)
 
         H = N // 2
 
-        ws = sb("ws", [P, B * N], U8)
-        nc.vector.tensor_copy(ws[:], ws_all[:].bitcast(U8).indirect(offsets[:]))
+        ws_picked = sb("ws_picked", [P, B * N], U8)
+        nc.vector.tensor_copy(ws_picked[:], ws_all[:].bitcast(U8).indirect(offsets[:]))
+        for q in range(4):
+            rows = slice(SCALE_FIRST + 16 * q, SCALE_FIRST + 16 * (q + 1), 4)
+            nc.sync.dma_start(ws[32 * q : 32 * q + 4, :], ws_picked[rows, :].bitcast(I32))
+        load_plane(1, "ws_all")
         w_codes = sb("w_codes", [P, B * N], U32)
         nc.vector.tensor_copy(w_codes[:], w_all[:].bitcast(U32).indirect(offsets[:]))
-        x_bf0 = sb("x_bf0", [P, PACK, P, PACK], BF16)[:]
-        deal_x(nc.scalar.copy, x_bf0, x_raw0[:, :, :X0_SCALAR], 0, 0)
-        deal_x(nc.vector.tensor_copy, x_bf0, x_raw0, 0, 2)
-        deal_x(nc.vector.tensor_copy, x_bf0, x_raw0[:, :, X0_SCALAR:], X0_SCALAR, 0)
-        x_q0 = quantize_x(0, x_bf0)
-        w_q = w_codes, ws
+        load_plane(2, "w_all")
+        x_bf0 = [sb("x_bf0_%d" % h, [P, 2, P, PACK], BF16)[:] for h in range(2)]
+        deal_x(nc.scalar.copy, x_bf0[0], x_raw0[:, :, :X0_SCALAR], 0, 0)
+        deal_x(nc.vector.tensor_copy, x_bf0[1], x_raw0, 0, 2)
+        deal_x(nc.vector.tensor_copy, x_bf0[0], x_raw0[:, :, X0_SCALAR:], X0_SCALAR, 0)
+        x_q0 = planes("x0", R)
+        for h in (1, 0):
+            cols = block(h, R // 2)
+            quantize(x_q0[0][:, cols], x_q0[1][:, cols], x_bf0[h].rearrange("p t m j -> p (t m j)"), E4M3)
+        load_plane(3, "x_bf0_1")
+        placed.append(sb("placed2", [P, T], F32, "x_bf0_0"))
+        nc.gpsimd.memset(placed[2][:], 0.0)
+        w_q = w_codes, ws[:].bitcast(U8)
+
+        def load_xm(b, tag):
+            raw = sb("xm_raw%d" % b, [P, PACK, D], F32, tag)
+            nc.sync.dma_start(raw[:], xm[b].rearrange("(p j) d -> p j d", j=PACK))
+            return raw
+
+        xm_raw = [load_xm(0, "ws_picked")]
         mean0 = sb("mean0", [P, PACK, N], F32)
         for t in range(PACK):
             a = in_bank(t % 2, [P, N])
@@ -153,15 +165,18 @@ def tile_attend_ghv_poi_kernel(tc, xT, w_words, w_scales, vT, wt, xm, offs, out)
 
         for j in range(PACK - 1):
             nc.vector.tensor_copy(v_picked[:, j, :], v_all[j][:].indirect(offsets[:]))
+        x1_rows = xT[1].rearrange("(p j) r -> p j r", j=PACK)
+        x_raw1 = [sb("x_raw1_0", [P, PACK, X1_FIRST], F32, "ws_all"), sb("x_raw1_1", [P, PACK, R - X1_FIRST], F32, "w_all")]
+        nc.sync.dma_start(x_raw1[0][:], x1_rows[:, :, :X1_FIRST])
+        nc.sync.dma_start(x_raw1[1][:], x1_rows[:, :, X1_FIRST:])
         first = 0
         for count in LAST_PLANE_PIECES:
             nc.vector.tensor_copy(
                 v_picked[:, PACK - 1, first : first + count], v_all[PACK - 1][:].indirect(listed(first, count))
             )
             first += count
-        for k in range(2, D // P):
-            placed.append(sb("placed%d" % k, [P, T], F32, "v_all%d" % (k - 2)))
-            nc.gpsimd.memset(placed[k][:], 0.0)
+        placed.append(sb("placed3", [P, T], F32, "v_all0"))
+        nc.gpsimd.memset(placed[3][:], 0.0)
 
         g_wide = planes("g0", H + N)
         nc.gpsimd.memset(g_wide[0][:, :H].bitcast(I32), 0)
@@ -206,6 +221,7 @@ def tile_attend_ghv_poi_kernel(tc, xT, w_words, w_scales, vT, wt, xm, offs, out)
             nc.scalar.copy(interleaved(v_bf0[c][:, :, :2]), by_fours(v_picked[:, :2, block(c)]))
         direction_chunk(0, v_bf0[0])
         nc.vector.tensor_copy(last_picked, v_all[PACK - 1][:].indirect(listed(N + H, H)))
+        xm_raw.append(load_xm(1, "x_bf0_1"))
         direction_chunk(1, v_bf0[1])
         direction_chunk(2, v_bf0[2])
         multiply_chunk(0)
@@ -221,13 +237,13 @@ def tile_attend_ghv_poi_kernel(tc, xT, w_words, w_scales, vT, wt, xm, offs, out)
 
         x_bf1 = sb("x_bf1", [P, PACK, P, PACK], BF16)[:]
         for t0 in range(0, PACK, 2):
-            deal_x(nc.scalar.copy, x_bf1, x_raw1[0][:], 0, t0)
+            deal_x(nc.scalar.copy, x_bf1[:, t0 : t0 + 2], x_raw1[0][:], 0, t0)
         spent = x_raw1[0][:].rearrange("p j r -> p (j r)")
         dw = spent[:, :H]
         nc.scalar.copy(dw, early[:, H:])
         nc.vector.tensor_copy(placed[0][:].indirect(listed(0, H)), dw)
         for t0 in range(0, PACK, 2):
-            deal_x(nc.scalar.copy, x_bf1, x_raw1[1][:], X1_FIRST, t0)
+            deal_x(nc.scalar.copy, x_bf1[:, t0 : t0 + 2], x_raw1[1][:], X1_FIRST, t0)
         x_q1 = quantize_x(1, x_bf1)
         v_bf1 = spent[:, N:].bitcast(BF16).rearrange("p (n j) -> p n j", j=PACK)
 
@@ -241,7 +257,7 @@ def tile_attend_ghv_poi_kernel(tc, xT, w_words, w_scales, vT, wt, xm, offs, out)
         v_late = sb("v_late", [P, CHUNK, PACK], BF16, "g_bf0_1")[:]
         weave_on_gpsimd(2, v_late)
         nc.scalar.copy(interleaved(v_bf1[:, :H, :]), by_fours(v_picked[:, :, N : N + H]))
-        v_q1 = planes("v1", N, "x_raw1_1")
+        v_q1 = planes("v1", N, "w_all")
         quantize_late(2, v_late)
         quantize(v_q1[0][:, :H], v_q1[1][:, :H], flat(v_bf1[:, :H, :]), E4M3)
         v_last = v_bf1[:, :CHUNK, :]

@@ -101,11 +101,11 @@ def tile_attend_ghv_poi_kernel(tc, xT, w_words, w_scales, vT, wt, xm, offs, out)
         def planes(name, width, tag=None):
             return sb(name + "_codes", [P, width], U32, tag), sb(name + "_scales", [P, width], U8)
 
-        def deal_x(copy_by, x_bf, raw, first, t0):
+        def deal_x(copy_by, x_bf, raw, first, t0, tiles=2):
             src = raw.rearrange("p j (m e t) -> p m j e t", e=2, t=PACK)
             dst = x_bf.rearrange("p t (m e) j -> p m j e t", e=2)
             pairs = slice(first // 8, first // 8 + src.shape[1])
-            copy_by(dst[:, pairs, :, :, :], src[:, :, :, :, t0 : t0 + 2])
+            copy_by(dst[:, pairs, :, :, :], src[:, :, :, :, t0 : t0 + tiles])
 
         def quantize_x(b, x_bf):
             x_q = planes("x%d" % b, R)
@@ -212,13 +212,11 @@ def tile_attend_ghv_poi_kernel(tc, xT, w_words, w_scales, vT, wt, xm, offs, out)
             nc.scalar.copy(interleaved(xm_bf[:]), by_fours(xm_raw[0][:, :, block(k)]))
             quantize(xm_parts[k][0][:], xm_parts[k][1][:], flat(xm_bf[:]), E4M3)
 
-        def own_bf(c):
-            return sb("v_bf0_%d" % c, [P, CHUNK, PACK], BF16)[:]
-
+        v_rest = sb("v_rest", [P, N - CHUNK, PACK], BF16)
         last_picked = v_picked[:, PACK - 1, N + H :]
-        v_bf0 = [last_picked.bitcast(BF16).rearrange("p (n j) -> p n j", j=PACK)] + [own_bf(c) for c in range(1, 4)]
-        for c in range(4):
-            nc.scalar.copy(interleaved(v_bf0[c][:, :, :2]), by_fours(v_picked[:, :2, block(c)]))
+        v_bf0 = [last_picked.bitcast(BF16).rearrange("p (n j) -> p n j", j=PACK)] + [v_rest[:, block(c), :] for c in range(3)]
+        nc.scalar.copy(interleaved(v_bf0[0][:, :, :2]), by_fours(v_picked[:, :2, :CHUNK]))
+        nc.scalar.copy(interleaved(v_rest[:, :, :2]), by_fours(v_picked[:, :2, CHUNK:N]))
         direction_chunk(0, v_bf0[0])
         nc.vector.tensor_copy(last_picked, v_all[PACK - 1][:].indirect(listed(N + H, H)))
         xm_raw.append(load_xm(1, "x_bf0_1"))
@@ -236,14 +234,12 @@ def tile_attend_ghv_poi_kernel(tc, xT, w_words, w_scales, vT, wt, xm, offs, out)
         quantize_g0(1)
 
         x_bf1 = sb("x_bf1", [P, PACK, P, PACK], BF16)[:]
-        for t0 in range(0, PACK, 2):
-            deal_x(nc.scalar.copy, x_bf1[:, t0 : t0 + 2], x_raw1[0][:], 0, t0)
+        deal_x(nc.scalar.copy, x_bf1, x_raw1[0][:], 0, 0, PACK)
         spent = x_raw1[0][:].rearrange("p j r -> p (j r)")
         dw = spent[:, :H]
         nc.scalar.copy(dw, early[:, H:])
         nc.vector.tensor_copy(placed[0][:].indirect(listed(0, H)), dw)
-        for t0 in range(0, PACK, 2):
-            deal_x(nc.scalar.copy, x_bf1[:, t0 : t0 + 2], x_raw1[1][:], X1_FIRST, t0)
+        deal_x(nc.scalar.copy, x_bf1, x_raw1[1][:], X1_FIRST, 0, PACK)
         x_q1 = quantize_x(1, x_bf1)
         v_bf1 = spent[:, N:].bitcast(BF16).rearrange("p (n j) -> p n j", j=PACK)
 

@@ -24,6 +24,7 @@ CHUNK = 128
 X1_FIRST = 384
 X0_SCALAR = 384
 SCALE_FIRST = 32
+W_FIRST = 512
 LAST_PLANE_PIECES = (256, 256, 256)
 
 
@@ -39,6 +40,9 @@ def tile_attend_ghv_poi_kernel(tc, xT, w_words, w_scales, vT, wt, xm, offs, out)
         def sb(name, shape, dtype, tag=None):
             return keep.tile(shape, dtype, name=name, tag=tag or name, align_bytes=64)
 
+        w_all = sb("w_all", [P, T], I32)
+        w_src = w_words[0].rearrange("p n t -> p (n t)").bitcast(I32)
+        nc.sync.dma_start(w_all[:, :W_FIRST], w_src[:, :W_FIRST])
         offsets = keep.tile([P, B * N // LIST_ROWS], U16, name="offsets")
         nc.sync.dma_start(offsets[:], offs)
 
@@ -50,17 +54,16 @@ def tile_attend_ghv_poi_kernel(tc, xT, w_words, w_scales, vT, wt, xm, offs, out)
         ws = sb("ws", [P, B * N // 4], I32)
         nc.gpsimd.memset(ws[:], 0)
         wt_sb = sb("wt_sb", [P, B, PACK], F32)
-        nc.sync.dma_start(wt_sb[:], wt.rearrange("b (p t) o -> p b (t o)", t=PACK))
 
         v_flat = sb("v_flat", [P, PACK * B * N], F32)
         v_picked = v_flat[:].rearrange("p (j n) -> p j n", j=PACK)
         x_raw0 = v_flat[:, : PACK * R].rearrange("p (j r) -> p j r", j=PACK)
         v_all = [sb("v_all0", [P, T], F32)]
-        w_all = sb("w_all", [P, T], I32)
 
         nc.sync.dma_start(ws_all[SCALE_FIRST : SCALE_FIRST + 16 * 4 : 4, :], w_scales[0].bitcast(I32))
-        nc.sync.dma_start(w_all[:], w_words[0].rearrange("p n t -> p (n t)").bitcast(I32))
+        nc.sync.dma_start(w_all[:, W_FIRST:], w_src[:, W_FIRST:])
         nc.sync.dma_start(x_raw0, xT[0].rearrange("(p j) r -> p j r", j=PACK))
+        nc.sync.dma_start(wt_sb[:], wt.rearrange("b (p t) o -> p b (t o)", t=PACK))
         v_rows = vT.rearrange("(p j) t -> p j t", j=PACK)
         nc.sync.dma_start(v_all[0][:], v_rows[:, 0, :])
 

@@ -22,7 +22,7 @@ PACK = 4
 LIST_ROWS = 16
 CHUNK = 128
 X1_FIRST = 384
-X0_SCALAR = 384
+X0_SCALAR = 448
 SCALE_FIRST = 32
 W_FIRST = 512
 LAST_PLANE_PIECES = (256, 256, 256)
@@ -53,7 +53,11 @@ def tile_attend_ghv_poi_kernel(tc, xT, w_words, w_scales, vT, wt, xm, offs, out)
         nc.gpsimd.memset(ws_all[:], 0)
         ws = sb("ws", [P, B * N // 4], I32)
         nc.gpsimd.memset(ws[:], 0)
-        wt_sb = sb("wt_sb", [P, B, PACK], F32)
+
+        def load_wt(b, tag=None):
+            wt_b = sb("wt%d" % b, [P, PACK], F32, tag)
+            nc.sync.dma_start(wt_b[:], wt[b].rearrange("(p t) o -> p (t o)", t=PACK))
+            return wt_b
 
         v_flat = sb("v_flat", [P, PACK * B * N], F32)
         v_picked = v_flat[:].rearrange("p (j n) -> p j n", j=PACK)
@@ -63,7 +67,7 @@ def tile_attend_ghv_poi_kernel(tc, xT, w_words, w_scales, vT, wt, xm, offs, out)
         nc.sync.dma_start(ws_all[SCALE_FIRST : SCALE_FIRST + 16 * 4 : 4, :], w_scales[0].bitcast(I32))
         nc.sync.dma_start(w_all[:, W_FIRST:], w_src[:, W_FIRST:])
         nc.sync.dma_start(x_raw0, xT[0].rearrange("(p j) r -> p j r", j=PACK))
-        nc.sync.dma_start(wt_sb[:], wt.rearrange("b (p t) o -> p b (t o)", t=PACK))
+        wt0 = load_wt(0)
         v_rows = vT.rearrange("(p j) t -> p j t", j=PACK)
         nc.sync.dma_start(v_all[0][:], v_rows[:, 0, :])
 
@@ -164,7 +168,7 @@ def tile_attend_ghv_poi_kernel(tc, xT, w_words, w_scales, vT, wt, xm, offs, out)
             mx(a[:], x_q0, block(t), w_q, slice(0, N), E4M3)
             nc.scalar.activation(mean0[:, t, :], a[:], ACT.Exp)
         for t in range(PACK):
-            nc.scalar.activation(mean0[:, t, :], mean0[:, t, :], ACT.Copy, scale=wt_sb[:, 0, t : t + 1])
+            nc.scalar.activation(mean0[:, t, :], mean0[:, t, :], ACT.Copy, scale=wt0[:, t : t + 1])
 
         for j in range(PACK - 1):
             nc.vector.tensor_copy(v_picked[:, j, :], v_all[j][:].indirect(offsets[:]))
@@ -235,6 +239,7 @@ def tile_attend_ghv_poi_kernel(tc, xT, w_words, w_scales, vT, wt, xm, offs, out)
         multiply_chunk(3)
         quantize_xm0(1)
         quantize_g0(1)
+        wt1 = load_wt(1, "mean0")
 
         x_bf1 = sb("x_bf1", [P, PACK, P, PACK], BF16)[:]
         deal_x(nc.scalar.copy, x_bf1, x_raw1[0][:], 0, 0, PACK)
@@ -290,7 +295,7 @@ def tile_attend_ghv_poi_kernel(tc, xT, w_words, w_scales, vT, wt, xm, offs, out)
                         av_wt[half][:, :, t, :],
                         av[:, u, :].rearrange("p (c i) -> p c i", i=4),
                         ACT.Copy,
-                        scale=wt_sb[:, 1, t : t + 1],
+                        scale=wt1[:, t : t + 1],
                     )
 
         def multiply_group1(c):
@@ -311,7 +316,7 @@ def tile_attend_ghv_poi_kernel(tc, xT, w_words, w_scales, vT, wt, xm, offs, out)
             multiply_group1(c)
         last_acc = product(3, xm_q0, g_q0, 7)
         place_part(0, 3, last_acc, 0, H)
-        xm_bf1 = sb("xm_bf1", [P, D, PACK], BF16, "wt_sb")
+        xm_bf1 = sb("xm_bf1", [P, D, PACK], BF16, "mean0")
         nc.scalar.copy(interleaved(xm_bf1[:]), by_fours(xm_raw[1][:]))
         xm_first = planes("xm1_0", P)
         quantize(xm_first[0][:], xm_first[1][:], flat(xm_bf1[:, :P, :]), E4M3)

@@ -24,7 +24,7 @@ CHUNK = 128
 X1_FIRST = 384
 X0_SCALAR = 448
 SCALE_FIRST = 32
-W_FIRST = 512
+W_FIRST = 896
 LAST_PLANE_PIECES = (256, 256, 256)
 
 

@@ -21,11 +21,9 @@ P = 128
 PACK = 4
 LIST_ROWS = 16
 CHUNK = 128
-X1_FIRST = 384
-X0_SCALAR = 448
+H = N // 2
 SCALE_FIRST = 32
-W_FIRST = 896
-LAST_PLANE_PIECES = (256, 256, 256)
+V_FIRST = 896
 
 
 def tile_attend_ghv_poi_kernel(tc, xT, w_words, w_scales, vT, wt, xm, offs, out):
@@ -40,44 +38,8 @@ def tile_attend_ghv_poi_kernel(tc, xT, w_words, w_scales, vT, wt, xm, offs, out)
         def sb(name, shape, dtype, tag=None):
             return keep.tile(shape, dtype, name=name, tag=tag or name, align_bytes=64)
 
-        w_all = sb("w_all", [P, T], I32)
-        w_src = w_words[0].rearrange("p n t -> p (n t)").bitcast(I32)
-        nc.sync.dma_start(w_all[:, :W_FIRST], w_src[:, :W_FIRST])
-        offsets = keep.tile([P, B * N // LIST_ROWS], U16, name="offsets")
-        nc.sync.dma_start(offsets[:], offs)
-
-        def listed(first, count):
-            return offsets[:, first // LIST_ROWS : (first + count) // LIST_ROWS]
-
-        ws_all = sb("ws_all", [P, T // 4], I32)
-        nc.gpsimd.memset(ws_all[:], 0)
-        ws = sb("ws", [P, B * N // 4], I32)
-        nc.gpsimd.memset(ws[:], 0)
-
-        def load_wt(b, tag=None):
-            wt_b = sb("wt%d" % b, [P, PACK], F32, tag)
-            nc.sync.dma_start(wt_b[:], wt[b].rearrange("(p t) o -> p (t o)", t=PACK))
-            return wt_b
-
-        v_flat = sb("v_flat", [P, PACK * B * N], F32)
-        v_picked = v_flat[:].rearrange("p (j n) -> p j n", j=PACK)
-        x_raw0 = v_flat[:, : PACK * R].rearrange("p (j r) -> p j r", j=PACK)
-        v_all = [sb("v_all0", [P, T], F32)]
-
-        nc.sync.dma_start(ws_all[SCALE_FIRST : SCALE_FIRST + 16 * 4 : 4, :], w_scales[0].bitcast(I32))
-        nc.sync.dma_start(w_all[:, W_FIRST:], w_src[:, W_FIRST:])
-        nc.sync.dma_start(x_raw0, xT[0].rearrange("(p j) r -> p j r", j=PACK))
-        wt0 = load_wt(0)
-        v_rows = vT.rearrange("(p j) t -> p j t", j=PACK)
-        nc.sync.dma_start(v_all[0][:], v_rows[:, 0, :])
-
-        def load_plane(j, tag):
-            v_all.append(sb("v_all%d" % j, [P, T], F32, tag))
-            nc.sync.dma_start(v_all[j][:], v_rows[:, j, :])
-
-        placed = [sb("placed%d" % k, [P, T], F32) for k in range(2)]
-        for k in range(2):
-            nc.gpsimd.memset(placed[k][:], 0.0)
+        def block(i, width=P):
+            return slice(i * width, (i + 1) * width)
 
         def interleaved(tile_nj):
             return tile_nj.rearrange("p (c i) j -> p c j i", i=4)
@@ -85,8 +47,14 @@ def tile_attend_ghv_poi_kernel(tc, xT, w_words, w_scales, vT, wt, xm, offs, out)
         def by_fours(tile_jn):
             return tile_jn.rearrange("p j (c i) -> p c j i", i=4)
 
-        def quantize(codes, scales, grouped, fmt):
-            nc.vector.quantize_mx(out=codes.bitcast(fmt), scales=scales, in_=grouped)
+        def flat(tile_nj):
+            return tile_nj.rearrange("p n j -> p (n j)")
+
+        def planes(name, width, tag=None):
+            return sb(name + "_codes", [P, width], U32, tag), sb(name + "_scales", [P, width], U8)
+
+        def quantize(q, cols, grouped, fmt):
+            nc.vector.quantize_mx(out=q[0][:, cols].bitcast(fmt), scales=q[1][:, cols], in_=grouped)
 
         def mx(acc, lhs_q, lhs_cols, rhs_q, rhs_cols, rhs_fmt):
             nc.tensor.matmul_mx(
@@ -99,234 +67,232 @@ def tile_attend_ghv_poi_kernel(tc, xT, w_words, w_scales, vT, wt, xm, offs, out)
                 stop=True,
             )
 
-        def flat(tile_nj):
-            return tile_nj.rearrange("p n j -> p (n j)")
+        v_rows = vT.rearrange("(p j) t -> p j t", j=PACK)
+        v_all = [sb("v_all%d" % j, [P, T], F32) for j in range(PACK)]
+        nc.sync.dma_start(v_all[0][:, :V_FIRST], v_rows[:, 0, :V_FIRST])
+        offsets = keep.tile([P, B * N // LIST_ROWS], U16, name="offsets")
+        nc.sync.dma_start(offsets[:], offs)
 
-        def block(i, width=P):
-            return slice(i * width, (i + 1) * width)
+        def listed(first, count):
+            return offsets[:, first // LIST_ROWS : (first + count) // LIST_ROWS]
 
-        def planes(name, width, tag=None):
-            return sb(name + "_codes", [P, width], U32, tag), sb(name + "_scales", [P, width], U8)
+        ws_all = sb("ws_all", [P, T // 4], I32)
+        nc.gpsimd.memset(ws_all[:], 0)
+        ws = sb("ws", [P, B * N // 4], I32)
+        nc.gpsimd.memset(ws[:], 0)
+        nc.sync.dma_start(ws_all[SCALE_FIRST : SCALE_FIRST + 16 * 4 : 4, :], w_scales[0].bitcast(I32))
+        nc.sync.dma_start(v_all[0][:, V_FIRST:], v_rows[:, 0, V_FIRST:])
+        for j in range(1, PACK):
+            nc.sync.dma_start(v_all[j][:], v_rows[:, j, :])
 
-        def deal_x(copy_by, x_bf, raw, first, t0, tiles=2):
-            src = raw.rearrange("p j (m e t) -> p m j e t", e=2, t=PACK)
-            dst = x_bf.rearrange("p t (m e) j -> p m j e t", e=2)
-            pairs = slice(first // 8, first // 8 + src.shape[1])
-            copy_by(dst[:, pairs, :, :, :], src[:, :, :, :, t0 : t0 + tiles])
+        def load_wt(b, tag=None):
+            wt_b = sb("wt%d" % b, [P, PACK], F32, tag)
+            nc.sync.dma_start(wt_b[:], wt[b].rearrange("(p t) o -> p (t o)", t=PACK))
+            return wt_b
 
-        def quantize_x(b, x_bf):
-            x_q = planes("x%d" % b, R)
-            quantize(x_q[0][:], x_q[1][:], x_bf.rearrange("p t m j -> p (t m j)"), E4M3)
-            return x_q
-
-        def product(k, xm_q, g_q, bank):
-            acc = in_bank(bank, [P, N])
-            mx(acc[:], xm_q[k][0], xm_q[k][1], g_q, slice(0, N), E5M2)
-            return acc
-
-        def place_part(b, k, acc, first, count, tag=None):
-            dw = sb("dw%d_%d_%d" % (b, k, first), [P, count], F32, tag)
-            nc.scalar.copy(dw[:], acc[:, first : first + count])
-            nc.vector.tensor_copy(placed[k][:].indirect(listed(b * N + first, count)), dw[:])
-
-        def place(b, k, xm_q, g_q, bank):
-            place_part(b, k, product(k, xm_q, g_q, bank), 0, N)
-
-        H = N // 2
+        placed = [sb("placed%d" % k, [P, T], F32) for k in range(D // P)]
+        for k in range(D // P):
+            nc.gpsimd.memset(placed[k][:], 0.0)
+        g_q = planes("g", B * N)
+        nc.gpsimd.memset(g_q[0][:, H:].bitcast(I32), 0)
+        nc.gpsimd.memset(g_q[1][:, H:].bitcast(I32), 0)
 
         ws_picked = sb("ws_picked", [P, B * N], U8)
         nc.vector.tensor_copy(ws_picked[:], ws_all[:].bitcast(U8).indirect(offsets[:]))
         for q in range(4):
             rows = slice(SCALE_FIRST + 16 * q, SCALE_FIRST + 16 * (q + 1), 4)
             nc.sync.dma_start(ws[32 * q : 32 * q + 4, :], ws_picked[rows, :].bitcast(I32))
-        load_plane(1, "ws_all")
-        w_codes = sb("w_codes", [P, B * N], U32)
-        nc.vector.tensor_copy(w_codes[:], w_all[:].bitcast(U32).indirect(offsets[:]))
-        load_plane(2, "w_all")
-        x_bf0 = [sb("x_bf0_%d" % h, [P, 2, P, PACK], BF16)[:] for h in range(2)]
-        deal_x(nc.scalar.copy, x_bf0[0], x_raw0[:, :, :X0_SCALAR], 0, 0)
-        deal_x(nc.vector.tensor_copy, x_bf0[1], x_raw0, 0, 2)
-        deal_x(nc.vector.tensor_copy, x_bf0[0], x_raw0[:, :, X0_SCALAR:], X0_SCALAR, 0)
-        x_q0 = planes("x0", R)
-        for h in (1, 0):
-            cols = block(h, R // 2)
-            quantize(x_q0[0][:, cols], x_q0[1][:, cols], x_bf0[h].rearrange("p t m j -> p (t m j)"), E4M3)
-        load_plane(3, "x_bf0_1")
-        placed.append(sb("placed2", [P, T], F32, "x_bf0_0"))
-        nc.gpsimd.memset(placed[2][:], 0.0)
-        w_q = w_codes, ws[:].bitcast(U8)
 
-        def load_xm(b, tag):
-            raw = sb("xm_raw%d" % b, [P, PACK, D], F32, tag)
-            nc.sync.dma_start(raw[:], xm[b].rearrange("(p j) d -> p j d", j=PACK))
-            return raw
+        xm_rows = [xm[b].rearrange("(p j) d -> p j d", j=PACK) for b in range(B)]
+        x0_rows = xT[0].rearrange("(p j) r -> p j r", j=PACK)
+        x_flat0 = sb("x_flat0", [P, PACK * R], F32, "ws_all")
+        x_raw0 = [x_flat0[:, block(h, PACK * R // 2)].rearrange("p (j r) -> p j r", j=PACK) for h in range(2)]
+        for h in range(2):
+            nc.sync.dma_start(x_raw0[h], x0_rows[:, :, block(h, R // 2)])
 
-        xm_raw = [load_xm(0, "ws_picked")]
-        mean0 = sb("mean0", [P, PACK, N], F32)
-        for t in range(PACK):
-            a = in_bank(t % 2, [P, N])
-            mx(a[:], x_q0, block(t), w_q, slice(0, N), E4M3)
-            nc.scalar.activation(mean0[:, t, :], a[:], ACT.Exp)
-        for t in range(PACK):
-            nc.scalar.activation(mean0[:, t, :], mean0[:, t, :], ACT.Copy, scale=wt0[:, t : t + 1])
+        v_flat = sb("v_flat", [P, PACK * B * N], F32)
+        v_picked = v_flat[:].rearrange("p (j n) -> p j n", j=PACK)
 
-        for j in range(PACK - 1):
-            nc.vector.tensor_copy(v_picked[:, j, :], v_all[j][:].indirect(offsets[:]))
-        x1_rows = xT[1].rearrange("(p j) r -> p j r", j=PACK)
-        x_raw1 = [sb("x_raw1_0", [P, PACK, X1_FIRST], F32, "ws_all"), sb("x_raw1_1", [P, PACK, R - X1_FIRST], F32, "w_all")]
-        nc.sync.dma_start(x_raw1[0][:], x1_rows[:, :, :X1_FIRST])
-        nc.sync.dma_start(x_raw1[1][:], x1_rows[:, :, X1_FIRST:])
-        first = 0
-        for count in LAST_PLANE_PIECES:
-            nc.vector.tensor_copy(
-                v_picked[:, PACK - 1, first : first + count], v_all[PACK - 1][:].indirect(listed(first, count))
-            )
-            first += count
-        placed.append(sb("placed3", [P, T], F32, "v_all0"))
-        nc.gpsimd.memset(placed[3][:], 0.0)
+        def gather_v(j, first, count):
+            nc.vector.tensor_copy(v_picked[:, j, first : first + count], v_all[j][:].indirect(listed(first, count)))
 
-        g_wide = planes("g0", H + N)
-        nc.gpsimd.memset(g_wide[0][:, :H].bitcast(I32), 0)
-        nc.gpsimd.memset(g_wide[1][:, :H].bitcast(I32), 0)
-        g_q0 = g_wide[0][:, H:], g_wide[1][:, H:]
-        g_bf0 = [sb("g_bf0_%d" % h, [P, H, PACK], BF16) for h in range(2)]
-        xm_parts = [planes("xm0_0", P), planes("xm0_1", P)]
-        xm_q0 = [(xm_parts[0], block(0)), (xm_parts[1], block(0))]
-        banks = {}
+        gather_v(0, 0, B * N)
+        w_all = sb("w_all", [P, T], I32, "v_all0")
+        nc.sync.dma_start(w_all[:], w_words[0].rearrange("p n t -> p (n t)").bitcast(I32))
+        wt0 = load_wt(0, "ws_picked")
+        gather_v(1, 0, B * N)
+        xm_raw0a = sb("xm_raw0a", [P, PACK, D // 2], F32, "v_all1")
+        nc.sync.dma_start(xm_raw0a[:], xm_rows[0][:, :, : D // 2])
+        v_bf0 = [sb("v_bf0_%d" % h, [P, H, PACK], BF16) for h in range(2)]
+        for h in range(2):
+            nc.scalar.copy(interleaved(v_bf0[h][:, :, :2]), by_fours(v_picked[:, :2, block(h, H)]))
+        gather_v(2, 0, B * N)
+        xm_raw0b = sb("xm_raw0b", [P, PACK, D // 2], F32, "v_all2")
+        nc.sync.dma_start(xm_raw0b[:], xm_rows[0][:, :, D // 2 :])
 
-        def direction_chunk(c, v_bf):
-            nc.scalar.copy(interleaved(v_bf[:, :, 2:]), by_fours(v_picked[:, 2:, block(c)]))
-            v_q = planes("v0_%d" % c, CHUNK)
-            quantize(v_q[0][:], v_q[1][:], flat(v_bf), E4M3)
-            av = in_bank(2 + c, [P, PACK, CHUNK])
-            for t in range(PACK):
-                mx(av[:, t, :], x_q0, block(t), v_q, slice(0, CHUNK), E4M3)
-            banks[c] = av
+        def weave(dst_nj, src_jn):
+            nc.gpsimd.tensor_scalar(dst_nj, src_jn.rearrange("p j n -> p n j"), 1.0, 0.0, MULT, ADD)
 
-        def multiply_chunk(c):
-            nc.vector.tensor_tensor(
-                interleaved(g_bf0[c // 2][:, block(c % 2), :]),
-                by_fours(banks[c][:]),
-                by_fours(mean0[:, :, block(c)]),
-                MULT,
-            )
+        for h in range(2):
+            gather_v(3, h * H, H)
+            weave(v_bf0[h][:, :, 2:], v_picked[:, 2:, block(h, H)])
+        gather_v(3, N, N)
+        x_raw1 = sb("x_raw1", [P, PACK, R], F32, "v_all3")
+        nc.sync.dma_start(x_raw1[:], xT[1].rearrange("(p j) r -> p j r", j=PACK))
 
-        def quantize_g0(h):
-            quantize(g_q0[0][:, block(h, H)], g_q0[1][:, block(h, H)], flat(g_bf0[h][:]), E5M2)
+        def deal_x(x_bf, raw, first, t0=0, tiles=PACK):
+            src = raw.rearrange("p j (m e t) -> p m j e t", e=2, t=PACK)
+            dst = x_bf.rearrange("p t (m e) j -> p m j e t", e=2)
+            pairs = slice(first // 8, first // 8 + src.shape[1])
+            nc.scalar.copy(dst[:, pairs, :, :, :], src[:, :, :, :, t0 : t0 + tiles])
 
-        def quantize_xm0(k):
-            xm_bf = sb("xm_bf0_%d" % k, [P, P, PACK], BF16)
-            nc.scalar.copy(interleaved(xm_bf[:]), by_fours(xm_raw[0][:, :, block(k)]))
-            quantize(xm_parts[k][0][:], xm_parts[k][1][:], flat(xm_bf[:]), E4M3)
+        x_bf0 = [sb("x_bf0_%d" % u, [P, 2, P, PACK], BF16) for u in range(2)]
+        for h in range(2):
+            for u in range(2):
+                deal_x(x_bf0[u][:], x_raw0[h], h * R // 2, 2 * u, 2)
+        v_q = [planes("v0", H)]
+        quantize(v_q[0], slice(0, H), flat(v_bf0[0][:]), E4M3)
+        x_q0 = []
+        for u, tag in enumerate((None, "v_bf0_0")):
+            pair_q = planes("x0_%d" % u, R // 2, tag)
+            quantize(pair_q, slice(0, R // 2), x_bf0[u][:].rearrange("p t m j -> p (t m j)"), E4M3)
+            x_q0.extend([(pair_q, block(0)), (pair_q, block(1))])
+        v_q.append(planes("v1", H, "x_bf0_0"))
+        quantize(v_q[1], slice(0, H), flat(v_bf0[1][:]), E4M3)
+        xm_raw1a = sb("xm_raw1a", [P, PACK, D // 2], F32, "x_bf0_1")
+        nc.sync.dma_start(xm_raw1a[:], xm_rows[1][:, :, : D // 2])
+        v_bf3 = sb("v_bf3", [P, H, PACK], BF16, "ws_all")
+        nc.scalar.copy(interleaved(v_bf3[:]), by_fours(v_picked[:, :, block(3, H)]))
+        v_bf2 = v_flat[:, 3 * H : 5 * H].bitcast(BF16).rearrange("p (n j) -> p n j", j=PACK)
+        weave(v_bf2, v_picked[:, :, block(2, H)])
 
-        v_rest = sb("v_rest", [P, N - CHUNK, PACK], BF16)
-        last_picked = v_picked[:, PACK - 1, N + H :]
-        v_bf0 = [last_picked.bitcast(BF16).rearrange("p (n j) -> p n j", j=PACK)] + [v_rest[:, block(c), :] for c in range(3)]
-        nc.scalar.copy(interleaved(v_bf0[0][:, :, :2]), by_fours(v_picked[:, :2, :CHUNK]))
-        nc.scalar.copy(interleaved(v_rest[:, :, :2]), by_fours(v_picked[:, :2, CHUNK:N]))
-        direction_chunk(0, v_bf0[0])
-        nc.vector.tensor_copy(last_picked, v_all[PACK - 1][:].indirect(listed(N + H, H)))
-        xm_raw.append(load_xm(1, "x_bf0_1"))
-        direction_chunk(1, v_bf0[1])
-        direction_chunk(2, v_bf0[2])
-        multiply_chunk(0)
-        direction_chunk(3, v_bf0[3])
-        multiply_chunk(1)
-        quantize_xm0(0)
-        quantize_g0(0)
-        early = product(0, xm_q0, g_wide, 6)
-        multiply_chunk(2)
-        multiply_chunk(3)
-        quantize_xm0(1)
-        quantize_g0(1)
-        wt1 = load_wt(1, "mean0")
+        mean = [sb("mean%d" % h, [P, H // 4, PACK, 4], F32) for h in range(4)]
+        av_wt = [sb("av_wt%d" % h, [P, H // 4, PACK, 4], F32) for h in range(4)]
 
-        x_bf1 = sb("x_bf1", [P, PACK, P, PACK], BF16)[:]
-        deal_x(nc.scalar.copy, x_bf1, x_raw1[0][:], 0, 0, PACK)
-        spent = x_raw1[0][:].rearrange("p j r -> p (j r)")
-        dw = spent[:, :H]
-        nc.scalar.copy(dw, early[:, H:])
-        nc.vector.tensor_copy(placed[0][:].indirect(listed(0, H)), dw)
-        deal_x(nc.scalar.copy, x_bf1, x_raw1[1][:], X1_FIRST, 0, PACK)
-        x_q1 = quantize_x(1, x_bf1)
-        v_bf1 = spent[:, N:].bitcast(BF16).rearrange("p (n j) -> p n j", j=PACK)
-
-        def weave_on_gpsimd(c, v_late):
-            cols = block(N // CHUNK + c)
-            nc.gpsimd.tensor_scalar(v_late, v_picked[:, :, cols].rearrange("p j n -> p n j"), 1.0, 0.0, MULT, ADD)
-
-        def quantize_late(c, v_late):
-            quantize(v_q1[0][:, block(c)], v_q1[1][:, block(c)], flat(v_late), E4M3)
-
-        v_late = sb("v_late", [P, CHUNK, PACK], BF16, "g_bf0_1")[:]
-        weave_on_gpsimd(2, v_late)
-        nc.scalar.copy(interleaved(v_bf1[:, :H, :]), by_fours(v_picked[:, :, N : N + H]))
-        v_q1 = planes("v1", N, "w_all")
-        quantize_late(2, v_late)
-        quantize(v_q1[0][:, :H], v_q1[1][:, :H], flat(v_bf1[:, :H, :]), E4M3)
-        v_last = v_bf1[:, :CHUNK, :]
-        weave_on_gpsimd(3, v_last)
-        place_part(0, 0, product(0, xm_q0, g_q0, 7), H, H)
-        nc.scalar.copy(interleaved(v_bf1[:, H:, :]), by_fours(xm_raw[0][:, :, H:]))
-        late = planes("xm0_2", H)
-        quantize(late[0][:], late[1][:], flat(v_bf1[:, H:, :]), E4M3)
-        quantize_late(3, v_last)
-        xm_q0.extend([(late, block(0)), (late, block(1))])
-        place(0, 1, xm_q0, g_q0, 6)
-
-        mean1 = [sb("mean1_%d" % h, [P, H // 4, PACK, 4], F32) for h in range(2)]
-        av_wt = [sb("av_wt_%d" % h, [P, H // 4, PACK, 4], F32) for h in range(2)]
-        g_bf1 = sb("g_bf1", [P, N, PACK], BF16)
-
-        def mean_chunk(c):
-            a = in_bank(c % 2, [P, PACK, CHUNK])
-            for t in range(PACK):
-                mx(a[:, t, :], x_q1, block(t), w_q, block(N // CHUNK + c), E4M3)
-            nc.scalar.activation(mean1[c // 2][:, block(c % 2, CHUNK // 4), :, :], by_fours(a[:]), ACT.Exp)
-
-        def weighted_half(half):
+        def weighted_half(half, x_q, wt_b, bank):
             for pair in range(2):
-                av = in_bank(2 + 2 * half + pair, [P, 2, H])
+                av = in_bank(bank + pair, [P, 2, H])
                 for u in range(2):
-                    mx(av[:, u, :], x_q1, block(2 * pair + u), v_q1, block(half, H), E4M3)
+                    mx(av[:, u, :], *x_q[2 * pair + u], v_q[half], slice(0, H), E4M3)
                 for u in range(2):
                     t = 2 * pair + u
                     nc.scalar.activation(
                         av_wt[half][:, :, t, :],
                         av[:, u, :].rearrange("p (c i) -> p c i", i=4),
                         ACT.Copy,
-                        scale=wt1[:, t : t + 1],
+                        scale=wt_b[:, t : t + 1],
                     )
 
-        def multiply_group1(c):
+        w_codes = sb("w_codes", [P, B * N], U32, "v_bf0_1")
+        w_q = w_codes, ws[:].bitcast(U8)
+
+        def gather_w(first, count):
+            nc.vector.tensor_copy(w_codes[:, first : first + count], w_all[:].bitcast(U32).indirect(listed(first, count)))
+
+        def mean_chunk(c, x_q, bank):
+            a = in_bank(bank, [P, PACK, CHUNK])
+            for t in range(PACK):
+                mx(a[:, t, :], *x_q[t], w_q, block(c), E4M3)
+            nc.scalar.activation(mean[c // 2][:, block(c % 2, CHUNK // 4), :, :], by_fours(a[:]), ACT.Exp)
+
+        def multiply(engine, c, g_bf):
             part = block(c % 2, CHUNK // 4)
-            nc.gpsimd.tensor_tensor(
-                interleaved(g_bf1[:, block(c), :]), mean1[c // 2][:, part, :, :], av_wt[c // 2][:, part, :, :], MULT
+            engine.tensor_tensor(
+                interleaved(g_bf[:, block(c % 2), :]), mean[c // 2][:, part, :, :], av_wt[c // 2][:, part, :, :], MULT
             )
 
-        mean_chunk(0)
-        mean_chunk(1)
-        weighted_half(0)
-        multiply_group1(0)
-        multiply_group1(1)
-        place(0, 2, xm_q0, g_q0, 7)
-        weighted_half(1)
+        def quantize_g(half, g_bf):
+            quantize(g_q, block(half, H), flat(g_bf[:]), E5M2)
+
+        def product(xm_q, cols, half, bank):
+            acc = in_bank(bank, [P, N])
+            mx(acc[:], xm_q, cols, g_q, slice(min(half, 2) * H, min(half, 2) * H + N), E5M2)
+            return acc
+
+        def place(k, acc, half, count, tag=None):
+            dw = sb("dw%d_%d" % (k, half), [P, count], F32, tag)
+            first = max(half - 2, 0) * H
+            nc.scalar.copy(dw[:], acc[:, first : first + count])
+            nc.vector.tensor_copy(placed[k][:].indirect(listed(half * H, count)), dw[:])
+
+        weighted_half(0, x_q0, wt0, 2)
+        gather_w(0, H)
+        gather_w(H, H)
+        gather_w(N, N)
+        xm_raw1b = sb("xm_raw1b", [P, PACK, D // 2], F32, "v_all0")
+        nc.sync.dma_start(xm_raw1b[:], xm_rows[1][:, :, D // 2 :])
+        g_bf0 = sb("g_bf0", [P, H, PACK], BF16)
+        for c in range(2):
+            mean_chunk(c, x_q0, c)
+            multiply(nc.vector, c, g_bf0)
+        xm_q0 = planes("xm0", D)
+        xm_bf00 = sb("xm_bf00", [P, P, PACK], BF16)
+        nc.scalar.copy(interleaved(xm_bf00[:]), by_fours(xm_raw0a[:, :, block(0)]))
+        quantize(xm_q0, block(0), flat(xm_bf00[:]), E4M3)
+        wt1 = load_wt(1, "xm_bf00")
+        quantize_g(0, g_bf0)
+        v_q.append(planes("v2", H, "mean0"))
+        quantize(v_q[2], slice(0, H), flat(v_bf2), E4M3)
+        v_q.append(planes("v3", H, "av_wt0"))
+        quantize(v_q[3], slice(0, H), flat(v_bf3[:]), E4M3)
+        xm_bf01 = sb("xm_bf01", [P, P, PACK], BF16)
+        nc.scalar.copy(interleaved(xm_bf01[:]), by_fours(xm_raw0a[:, :, block(1)]))
+        quantize(xm_q0, block(1), flat(xm_bf01[:]), E4M3)
+        place(0, product(xm_q0, block(0), 0, 6), 0, H)
+        xm_bf0b = sb("xm_bf0b", [P, D // 2, PACK], BF16, "xm_bf01")
+        weave(xm_bf0b[:], xm_raw0b[:])
+        weighted_half(1, x_q0, wt0, 0)
+        quantize(xm_q0, block(1, D // 2), flat(xm_bf0b[:]), E4M3)
+        place(1, product(xm_q0, block(1), 0, 7), 0, H, "v_all2")
+        g_bf1 = sb("g_bf1", [P, H, PACK], BF16, "xm_bf01")
         for c in (2, 3):
-            mean_chunk(c)
-            multiply_group1(c)
-        last_acc = product(3, xm_q0, g_q0, 7)
-        place_part(0, 3, last_acc, 0, H)
-        xm_bf1 = sb("xm_bf1", [P, D, PACK], BF16, "mean0")
-        nc.scalar.copy(interleaved(xm_bf1[:]), by_fours(xm_raw[1][:]))
-        xm_first = planes("xm1_0", P)
-        quantize(xm_first[0][:], xm_first[1][:], flat(xm_bf1[:, :P, :]), E4M3)
-        g_q1 = planes("g1", N)
-        quantize(g_q1[0][:], g_q1[1][:], flat(g_bf1[:]), E5M2)
-        place_part(0, 3, last_acc, H, H, "mean1_1")
-        xm_rest = planes("xm1_1", D - P, "g_bf1")
-        quantize(xm_rest[0][:, :P], xm_rest[1][:, :P], flat(xm_bf1[:, P:H, :]), E4M3)
-        quantize(xm_rest[0][:, P:], xm_rest[1][:, P:], flat(xm_bf1[:, H:, :]), E4M3)
-        xm_q1 = [(xm_first, block(0))] + [(xm_rest, block(k)) for k in range(D // P - 1)]
+            mean_chunk(c, x_q0, c)
+            multiply(nc.gpsimd, c, g_bf1)
+        x_bf1 = sb("x_bf1", [P, PACK, P, PACK], BF16)
+        deal_x(x_bf1[:], x_raw1[:, :, : R // 2], 0)
+        place(2, product(xm_q0, block(2), 0, 6), 0, H)
+        deal_x(x_bf1[:], x_raw1[:, :, R // 2 :], R // 2)
+        acc = product(xm_q0, block(3), 0, 6)
+        quantize_g(1, g_bf1)
+        whole_q = planes("x1", R)
+        quantize(whole_q, slice(0, R), x_bf1[:].rearrange("p t m j -> p (t m j)"), E4M3)
+        x_q1 = [(whole_q, block(t)) for t in range(PACK)]
+        place(3, acc, 0, H, "mean1")
+
+        xm_bf1a = sb("xm_bf1a", [P, D // 2, PACK], BF16, "x_bf1")
+        weave(xm_bf1a[:], xm_raw1a[:])
+        xm_q1a = planes("xm1a", D // 2)
+        quantize(xm_q1a, slice(0, D // 2), flat(xm_bf1a[:]), E4M3)
+        place(0, product(xm_q0, block(0), 1, 7), 1, H, "x_bf0_1")
+        g_bf2 = sb("g_bf2", [P, H, PACK], BF16)
+        mean_chunk(4, x_q1, 4)
+        weighted_half(2, x_q1, wt1, 0)
+        multiply(nc.gpsimd, 4, g_bf2)
+        place(1, product(xm_q0, block(1), 1, 6), 1, H)
+        mean_chunk(5, x_q1, 5)
+        multiply(nc.gpsimd, 5, g_bf2)
+        place(2, product(xm_q0, block(2), 1, 7), 1, H)
+        acc = product(xm_q0, block(3), 1, 7)
+        quantize_g(2, g_bf2)
+        place(3, acc, 1, H, "mean2")
+        weighted_half(3, x_q1, wt1, 2)
+        g_bf3 = sb("g_bf3", [P, H, PACK], BF16, "g_bf2")
+        for c in (6, 7):
+            mean_chunk(c, x_q1, c - 2)
+            multiply(nc.gpsimd, c, g_bf3)
+        place(0, product(xm_q1a, block(0), 2, 6), 2, H)
+        xm_bf1b = sb("xm_bf1b", [P, D // 2, PACK], BF16)
+        nc.scalar.copy(interleaved(xm_bf1b[:]), by_fours(xm_raw1b[:]))
+        acc = product(xm_q1a, block(1), 2, 6)
+        quantize_g(3, g_bf3)
+        place(1, acc, 2, H, "mean3")
+        xm_q1b = planes("xm1b", D // 2, "mean3")
+        quantize(xm_q1b, slice(0, D // 2), flat(xm_bf1b[:]), E4M3)
         for k in range(D // P):
-            place(1, k, xm_q1, g_q1, 6 + k % 2)
+            xm_q1 = xm_q1a if k < 2 else xm_q1b
+            acc = product(xm_q1, block(k % 2), 3, 7 - k % 2)
+            if k < 2:
+                place(k, acc, 3, H)
+            else:
+                place(k, acc, 2, N)
             nc.sync.dma_start(out[block(k), :], placed[k][:])

@@ -113,8 +113,11 @@ def tile_attend_ghv_poi_kernel(tc, xT, w_words, w_scales, vT, wt, xm, offs, out)
         v_flat = sb("v_flat", [P, PACK * B * N], F32)
         v_picked = v_flat[:].rearrange("p (j n) -> p j n", j=PACK)
 
-        def gather_v(j, first, count):
-            nc.vector.tensor_copy(v_picked[:, j, first : first + count], v_all[j][:].indirect(listed(first, count)))
+        late_pair = [v_flat[:, block(5 - h, N)].rearrange("p (j n) -> p j n", j=2) for h in range(2)]
+
+        def gather_v(j, first, count, dst=None):
+            dst = v_picked[:, j, first : first + count] if dst is None else dst
+            nc.vector.tensor_copy(dst, v_all[j][:].indirect(listed(first, count)))
 
         gather_v(0, 0, B * N)
         w_all = sb("w_all", [P, T], I32, "v_all0")
@@ -126,18 +129,20 @@ def tile_attend_ghv_poi_kernel(tc, xT, w_words, w_scales, vT, wt, xm, offs, out)
         v_bf0 = [sb("v_bf0_%d" % h, [P, H, PACK], BF16) for h in range(2)]
         for h in range(2):
             nc.scalar.copy(interleaved(v_bf0[h][:, :, :2]), by_fours(v_picked[:, :2, block(h, H)]))
-        gather_v(2, 0, B * N)
-        xm_raw0b = sb("xm_raw0b", [P, PACK, D // 2], F32, "v_all2")
-        nc.sync.dma_start(xm_raw0b[:], xm_rows[0][:, :, D // 2 :])
+        for h in range(2):
+            gather_v(2, h * H, H, late_pair[h][:, 0, :])
 
         def weave(dst_nj, src_jn):
             nc.gpsimd.tensor_scalar(dst_nj, src_jn.rearrange("p j n -> p n j"), 1.0, 0.0, MULT, ADD)
 
         for h in range(2):
-            gather_v(3, h * H, H)
-            weave(v_bf0[h][:, :, 2:], v_picked[:, 2:, block(h, H)])
+            gather_v(3, h * H, H, late_pair[h][:, 1, :])
+            weave(v_bf0[h][:, :, 2:], late_pair[h])
         gather_v(3, N, N)
-        x_raw1 = sb("x_raw1", [P, PACK, R], F32, "v_all3")
+        xm_raw0b = sb("xm_raw0b", [P, PACK, D // 2], F32, "v_all3")
+        nc.sync.dma_start(xm_raw0b[:], xm_rows[0][:, :, D // 2 :])
+        gather_v(2, N, N)
+        x_raw1 = sb("x_raw1", [P, PACK, R], F32, "v_all2")
         nc.sync.dma_start(x_raw1[:], xT[1].rearrange("(p j) r -> p j r", j=PACK))
 
         def deal_x(x_bf, raw, first, t0=0, tiles=PACK):
@@ -215,6 +220,9 @@ def tile_attend_ghv_poi_kernel(tc, xT, w_words, w_scales, vT, wt, xm, offs, out)
             nc.scalar.copy(dw[:], acc[:, first : first + count])
             nc.vector.tensor_copy(placed[k][:].indirect(listed(half * H, count)), dw[:])
 
+        def regroup(dst_nj, src_jn):
+            nc.scalar.copy(interleaved(dst_nj), by_fours(src_jn))
+
         weighted_half(0, x_q0, wt0, 2)
         gather_w(0, H)
         gather_w(H, H)
@@ -243,11 +251,11 @@ def tile_attend_ghv_poi_kernel(tc, xT, w_words, w_scales, vT, wt, xm, offs, out)
         weave(xm_bf0b[:], xm_raw0b[:])
         weighted_half(1, x_q0, wt0, 0)
         quantize(xm_q0, block(1, D // 2), flat(xm_bf0b[:]), E4M3)
-        place(1, product(xm_q0, block(1), 0, 7), 0, H, "v_all2")
         g_bf1 = sb("g_bf1", [P, H, PACK], BF16, "xm_bf01")
         for c in (2, 3):
             mean_chunk(c, x_q0, c)
             multiply(nc.gpsimd, c, g_bf1)
+        place(1, product(xm_q0, block(1), 0, 7), 0, H)
         x_bf1 = sb("x_bf1", [P, PACK, P, PACK], BF16)
         deal_x(x_bf1[:], x_raw1[:, :, : R // 2], 0)
         place(2, product(xm_q0, block(2), 0, 6), 0, H)
@@ -257,13 +265,11 @@ def tile_attend_ghv_poi_kernel(tc, xT, w_words, w_scales, vT, wt, xm, offs, out)
         whole_q = planes("x1", R)
         quantize(whole_q, slice(0, R), x_bf1[:].rearrange("p t m j -> p (t m j)"), E4M3)
         x_q1 = [(whole_q, block(t)) for t in range(PACK)]
-        place(3, acc, 0, H, "mean1")
+        place(3, acc, 0, H)
 
         xm_bf1a = sb("xm_bf1a", [P, D // 2, PACK], BF16, "x_bf1")
         weave(xm_bf1a[:], xm_raw1a[:])
-        xm_q1a = planes("xm1a", D // 2)
-        quantize(xm_q1a, slice(0, D // 2), flat(xm_bf1a[:]), E4M3)
-        place(0, product(xm_q0, block(0), 1, 7), 1, H, "x_bf0_1")
+        place(0, product(xm_q0, block(0), 1, 7), 1, H)
         g_bf2 = sb("g_bf2", [P, H, PACK], BF16)
         mean_chunk(4, x_q1, 4)
         weighted_half(2, x_q1, wt1, 0)
@@ -273,21 +279,27 @@ def tile_attend_ghv_poi_kernel(tc, xT, w_words, w_scales, vT, wt, xm, offs, out)
         multiply(nc.gpsimd, 5, g_bf2)
         place(2, product(xm_q0, block(2), 1, 7), 1, H)
         acc = product(xm_q0, block(3), 1, 7)
+        xm_q1a = planes("xm1a", D // 2, "xm0_codes")
+        quantize(xm_q1a, slice(0, D // 2), flat(xm_bf1a[:]), E4M3)
         quantize_g(2, g_bf2)
-        place(3, acc, 1, H, "mean2")
         weighted_half(3, x_q1, wt1, 2)
         g_bf3 = sb("g_bf3", [P, H, PACK], BF16, "g_bf2")
-        for c in (6, 7):
-            mean_chunk(c, x_q1, c - 2)
-            multiply(nc.gpsimd, c, g_bf3)
+        mean_chunk(6, x_q1, 4)
+        multiply(nc.gpsimd, 6, g_bf3)
+        place(3, acc, 1, H)
+        mean_chunk(7, x_q1, 5)
+        multiply(nc.gpsimd, 7, g_bf3)
+        xm_bf1b = []
+        for k, tag in enumerate(("dw1_1", "x_bf1")):
+            xm_bf1b.append(sb("xm_bf1b%d" % k, [P, P, PACK], BF16, tag))
+            regroup(xm_bf1b[k][:], xm_raw1b[:, :, block(k)])
         place(0, product(xm_q1a, block(0), 2, 6), 2, H)
-        xm_bf1b = sb("xm_bf1b", [P, D // 2, PACK], BF16)
-        nc.scalar.copy(interleaved(xm_bf1b[:]), by_fours(xm_raw1b[:]))
         acc = product(xm_q1a, block(1), 2, 6)
         quantize_g(3, g_bf3)
-        place(1, acc, 2, H, "mean3")
-        xm_q1b = planes("xm1b", D // 2, "mean3")
-        quantize(xm_q1b, slice(0, D // 2), flat(xm_bf1b[:]), E4M3)
+        place(1, acc, 2, H, "dw1_2")
+        xm_q1b = planes("xm1b", D // 2, "dw1_2")
+        for k in range(2):
+            quantize(xm_q1b, block(k), flat(xm_bf1b[k][:]), E4M3)
         for k in range(D // P):
             xm_q1 = xm_q1a if k < 2 else xm_q1b
             acc = product(xm_q1, block(k % 2), 3, 7 - k % 2)

@@ -166,8 +166,9 @@ def tile_attend_ghv_poi_kernel(tc, xT, w_words, w_scales, vT, wt, xm, offs, out)
         quantize(v_q[1], slice(0, H), flat(v_bf0[1][:]), E4M3)
         xm_raw1a = sb("xm_raw1a", [P, PACK, D // 2], F32, "x_bf0_1")
         nc.sync.dma_start(xm_raw1a[:], xm_rows[1][:, :, : D // 2])
-        v_bf3 = sb("v_bf3", [P, H, PACK], BF16, "ws_all")
-        nc.scalar.copy(interleaved(v_bf3[:]), by_fours(v_picked[:, :, block(3, H)]))
+        work = sb("work", [P, 7 * P, PACK], BF16, "ws_all")
+        v_bf3 = work[:, : 2 * P, :]
+        nc.scalar.copy(interleaved(v_bf3), by_fours(v_picked[:, :, block(3, H)]))
         v_bf2 = v_flat[:, 3 * H : 5 * H].bitcast(BF16).rearrange("p (n j) -> p n j", j=PACK)
         weave(v_bf2, v_picked[:, :, block(2, H)])
 
@@ -207,7 +208,7 @@ def tile_attend_ghv_poi_kernel(tc, xT, w_words, w_scales, vT, wt, xm, offs, out)
             )
 
         def quantize_g(half, g_bf):
-            quantize(g_q, block(half, H), flat(g_bf[:]), E5M2)
+            quantize(g_q, block(half, H), flat(g_bf), E5M2)
 
         def product(xm_q, cols, half, bank):
             acc = in_bank(bank, [P, N])
@@ -229,7 +230,7 @@ def tile_attend_ghv_poi_kernel(tc, xT, w_words, w_scales, vT, wt, xm, offs, out)
         gather_w(N, N)
         xm_raw1b = sb("xm_raw1b", [P, PACK, D // 2], F32, "v_all0")
         nc.sync.dma_start(xm_raw1b[:], xm_rows[1][:, :, D // 2 :])
-        g_bf0 = sb("g_bf0", [P, H, PACK], BF16)
+        g_bf0 = sb("g_bf0", [P, H, PACK], BF16)[:]
         for c in range(2):
             mean_chunk(c, x_q0, c)
             multiply(nc.vector, c, g_bf0)
@@ -242,35 +243,35 @@ def tile_attend_ghv_poi_kernel(tc, xT, w_words, w_scales, vT, wt, xm, offs, out)
         v_q.append(planes("v2", H, "mean0"))
         quantize(v_q[2], slice(0, H), flat(v_bf2), E4M3)
         v_q.append(planes("v3", H, "av_wt0"))
-        quantize(v_q[3], slice(0, H), flat(v_bf3[:]), E4M3)
-        xm_bf01 = sb("xm_bf01", [P, P, PACK], BF16)
-        nc.scalar.copy(interleaved(xm_bf01[:]), by_fours(xm_raw0a[:, :, block(1)]))
-        quantize(xm_q0, block(1), flat(xm_bf01[:]), E4M3)
+        quantize(v_q[3], slice(0, H), flat(v_bf3), E4M3)
+        xm_bf01 = work[:, 2 * P : 3 * P, :]
+        nc.scalar.copy(interleaved(xm_bf01), by_fours(xm_raw0a[:, :, block(1)]))
+        quantize(xm_q0, block(1), flat(xm_bf01), E4M3)
         place(0, product(xm_q0, block(0), 0, 6), 0, H)
-        xm_bf0b = sb("xm_bf0b", [P, D // 2, PACK], BF16, "xm_bf01")
-        weave(xm_bf0b[:], xm_raw0b[:])
+        xm_bf0b = work[:, P : 3 * P, :]
+        weave(xm_bf0b, xm_raw0b[:])
         weighted_half(1, x_q0, wt0, 0)
-        quantize(xm_q0, block(1, D // 2), flat(xm_bf0b[:]), E4M3)
-        g_bf1 = sb("g_bf1", [P, H, PACK], BF16, "xm_bf01")
+        quantize(xm_q0, block(1, D // 2), flat(xm_bf0b), E4M3)
+        g_bf1 = xm_bf0b
         for c in (2, 3):
             mean_chunk(c, x_q0, c)
             multiply(nc.gpsimd, c, g_bf1)
         place(1, product(xm_q0, block(1), 0, 7), 0, H)
-        x_bf1 = sb("x_bf1", [P, PACK, P, PACK], BF16)
-        deal_x(x_bf1[:], x_raw1[:, :, : R // 2], 0)
+        x_bf1 = work[:, 3 * P :, :].rearrange("p (t m) j -> p t m j", t=PACK)
+        deal_x(x_bf1, x_raw1[:, :, : R // 2], 0)
         place(2, product(xm_q0, block(2), 0, 6), 0, H)
-        deal_x(x_bf1[:], x_raw1[:, :, R // 2 :], R // 2)
+        deal_x(x_bf1, x_raw1[:, :, R // 2 :], R // 2)
         acc = product(xm_q0, block(3), 0, 6)
         quantize_g(1, g_bf1)
         whole_q = planes("x1", R)
-        quantize(whole_q, slice(0, R), x_bf1[:].rearrange("p t m j -> p (t m j)"), E4M3)
+        quantize(whole_q, slice(0, R), x_bf1.rearrange("p t m j -> p (t m j)"), E4M3)
         x_q1 = [(whole_q, block(t)) for t in range(PACK)]
         place(3, acc, 0, H)
 
-        xm_bf1a = sb("xm_bf1a", [P, D // 2, PACK], BF16, "x_bf1")
-        weave(xm_bf1a[:], xm_raw1a[:])
+        xm_bf1a = work[:, 2 * P : 4 * P, :]
+        weave(xm_bf1a, xm_raw1a[:])
         place(0, product(xm_q0, block(0), 1, 7), 1, H)
-        g_bf2 = sb("g_bf2", [P, H, PACK], BF16)
+        g_bf2 = work[:, 4 * P : 6 * P, :]
         mean_chunk(4, x_q1, 4)
         weighted_half(2, x_q1, wt1, 0)
         multiply(nc.gpsimd, 4, g_bf2)
@@ -280,17 +281,17 @@ def tile_attend_ghv_poi_kernel(tc, xT, w_words, w_scales, vT, wt, xm, offs, out)
         place(2, product(xm_q0, block(2), 1, 7), 1, H)
         acc = product(xm_q0, block(3), 1, 7)
         xm_q1a = planes("xm1a", D // 2, "xm0_codes")
-        quantize(xm_q1a, slice(0, D // 2), flat(xm_bf1a[:]), E4M3)
+        quantize(xm_q1a, slice(0, D // 2), flat(xm_bf1a), E4M3)
         quantize_g(2, g_bf2)
         weighted_half(3, x_q1, wt1, 2)
-        g_bf3 = sb("g_bf3", [P, H, PACK], BF16, "g_bf2")
+        g_bf3 = work[:, 7 * P // 2 : 11 * P // 2, :]
         mean_chunk(6, x_q1, 4)
         multiply(nc.gpsimd, 6, g_bf3)
         place(3, acc, 1, H)
         mean_chunk(7, x_q1, 5)
         multiply(nc.gpsimd, 7, g_bf3)
         xm_bf1b = []
-        for k, tag in enumerate(("dw1_1", "x_bf1")):
+        for k, tag in enumerate(("dw1_1", "dw2_1")):
             xm_bf1b.append(sb("xm_bf1b%d" % k, [P, P, PACK], BF16, tag))
             regroup(xm_bf1b[k][:], xm_raw1b[:, :, block(k)])
         place(0, product(xm_q1a, block(0), 2, 6), 2, H)

@@ -24,6 +24,8 @@ CHUNK = 128
 H = N // 2
 SCALE_FIRST = 32
 V_FIRST = 896
+SCALAR_SHARE = 64
+W_EARLY = 3 * H
 
 
 def tile_attend_ghv_poi_kernel(tc, xT, w_words, w_scales, vT, wt, xm, offs, out):
@@ -113,8 +115,6 @@ def tile_attend_ghv_poi_kernel(tc, xT, w_words, w_scales, vT, wt, xm, offs, out)
         v_flat = sb("v_flat", [P, PACK * B * N], F32)
         v_picked = v_flat[:].rearrange("p (j n) -> p j n", j=PACK)
 
-        late_pair = [v_flat[:, block(5 - h, N)].rearrange("p (j n) -> p j n", j=2) for h in range(2)]
-
         def gather_v(j, first, count, dst=None):
             dst = v_picked[:, j, first : first + count] if dst is None else dst
             nc.vector.tensor_copy(dst, v_all[j][:].indirect(listed(first, count)))
@@ -124,26 +124,21 @@ def tile_attend_ghv_poi_kernel(tc, xT, w_words, w_scales, vT, wt, xm, offs, out)
         nc.sync.dma_start(w_all[:], w_words[0].rearrange("p n t -> p (n t)").bitcast(I32))
         wt0 = load_wt(0, "ws_picked")
         gather_v(1, 0, B * N)
-        xm_raw0a = sb("xm_raw0a", [P, PACK, D // 2], F32, "v_all1")
-        nc.sync.dma_start(xm_raw0a[:], xm_rows[0][:, :, : D // 2])
+        xm_raw0 = sb("xm_raw0", [P, PACK, D], F32, "v_all1")
+        nc.sync.dma_start(xm_raw0[:], xm_rows[0])
         v_bf0 = [sb("v_bf0_%d" % h, [P, H, PACK], BF16) for h in range(2)]
         for h in range(2):
             nc.scalar.copy(interleaved(v_bf0[h][:, :, :2]), by_fours(v_picked[:, :2, block(h, H)]))
-        for h in range(2):
-            gather_v(2, h * H, H, late_pair[h][:, 0, :])
 
         def weave(dst_nj, src_jn):
             nc.gpsimd.tensor_scalar(dst_nj, src_jn.rearrange("p j n -> p n j"), 1.0, 0.0, MULT, ADD)
 
-        for h in range(2):
-            gather_v(3, h * H, H, late_pair[h][:, 1, :])
-            weave(v_bf0[h][:, :, 2:], late_pair[h])
-        gather_v(3, N, N)
-        xm_raw0b = sb("xm_raw0b", [P, PACK, D // 2], F32, "v_all3")
-        nc.sync.dma_start(xm_raw0b[:], xm_rows[0][:, :, D // 2 :])
-        gather_v(2, N, N)
+        gather_v(2, 0, B * N)
         x_raw1 = sb("x_raw1", [P, PACK, R], F32, "v_all2")
         nc.sync.dma_start(x_raw1[:], xT[1].rearrange("(p j) r -> p j r", j=PACK))
+        gather_v(3, 0, H)
+        weave(v_bf0[0][:, :, 2:], v_picked[:, 2:, :H])
+        gather_v(3, N, N)
 
         def deal_x(x_bf, raw, first, t0=0, tiles=PACK):
             src = raw.rearrange("p j (m e t) -> p m j e t", e=2, t=PACK)
@@ -162,15 +157,11 @@ def tile_attend_ghv_poi_kernel(tc, xT, w_words, w_scales, vT, wt, xm, offs, out)
             pair_q = planes("x0_%d" % u, R // 2, tag)
             quantize(pair_q, slice(0, R // 2), x_bf0[u][:].rearrange("p t m j -> p (t m j)"), E4M3)
             x_q0.extend([(pair_q, block(0)), (pair_q, block(1))])
-        v_q.append(planes("v1", H, "x_bf0_0"))
-        quantize(v_q[1], slice(0, H), flat(v_bf0[1][:]), E4M3)
-        xm_raw1a = sb("xm_raw1a", [P, PACK, D // 2], F32, "x_bf0_1")
+        xm_raw1a = sb("xm_raw1a", [P, PACK, D // 2], F32, "x_bf0_0")
         nc.sync.dma_start(xm_raw1a[:], xm_rows[1][:, :, : D // 2])
-        work = sb("work", [P, 7 * P, PACK], BF16, "ws_all")
-        v_bf3 = work[:, : 2 * P, :]
-        nc.scalar.copy(interleaved(v_bf3), by_fours(v_picked[:, :, block(3, H)]))
-        v_bf2 = v_flat[:, 3 * H : 5 * H].bitcast(BF16).rearrange("p (n j) -> p n j", j=PACK)
-        weave(v_bf2, v_picked[:, :, block(2, H)])
+        work = sb("work", [P, 8 * P, PACK], BF16, "ws_all")
+        v_bf2 = work[:, : 2 * P, :]
+        nc.scalar.copy(interleaved(v_bf2), by_fours(v_picked[:, :, block(2, H)]))
 
         mean = [sb("mean%d" % h, [P, H // 4, PACK, 4], F32) for h in range(4)]
         av_wt = [sb("av_wt%d" % h, [P, H // 4, PACK, 4], F32) for h in range(4)]
@@ -189,16 +180,17 @@ def tile_attend_ghv_poi_kernel(tc, xT, w_words, w_scales, vT, wt, xm, offs, out)
                         scale=wt_b[:, t : t + 1],
                     )
 
-        w_codes = sb("w_codes", [P, B * N], U32, "v_bf0_1")
-        w_q = w_codes, ws[:].bitcast(U8)
+        w_early = sb("w_early", [P, W_EARLY], U32, "x_bf0_1")
+        w_q = [(w_early, ws[:].bitcast(U8)[:, :W_EARLY])]
 
-        def gather_w(first, count):
-            nc.vector.tensor_copy(w_codes[:, first : first + count], w_all[:].bitcast(U32).indirect(listed(first, count)))
+        def gather_w(dst, first, count):
+            nc.vector.tensor_copy(dst, w_all[:].bitcast(U32).indirect(listed(first, count)))
 
         def mean_chunk(c, x_q, bank):
+            late = c * CHUNK // W_EARLY
             a = in_bank(bank, [P, PACK, CHUNK])
             for t in range(PACK):
-                mx(a[:, t, :], *x_q[t], w_q, block(c), E4M3)
+                mx(a[:, t, :], *x_q[t], w_q[late], block(c - late * W_EARLY // CHUNK), E4M3)
             nc.scalar.activation(mean[c // 2][:, block(c % 2, CHUNK // 4), :, :], by_fours(a[:]), ACT.Exp)
 
         def multiply(engine, c, g_bf):
@@ -215,49 +207,60 @@ def tile_attend_ghv_poi_kernel(tc, xT, w_words, w_scales, vT, wt, xm, offs, out)
             mx(acc[:], xm_q, cols, g_q, slice(min(half, 2) * H, min(half, 2) * H + N), E5M2)
             return acc
 
-        def place(k, acc, half, count, tag=None):
-            dw = sb("dw%d_%d" % (k, half), [P, count], F32, tag)
+        def place(k, acc, half, count, tag=None, unit=None):
+            if unit is None:
+                dw = sb("dw%d_%d" % (k, half), [P, count], F32, tag)[:]
+            else:
+                dw = flat(work[:, block(unit), :]).bitcast(F32)
             first = max(half - 2, 0) * H
-            nc.scalar.copy(dw[:], acc[:, first : first + count])
-            nc.vector.tensor_copy(placed[k][:].indirect(listed(half * H, count)), dw[:])
+            nc.scalar.copy(dw, acc[:, first : first + count])
+            nc.vector.tensor_copy(placed[k][:].indirect(listed(half * H, count)), dw)
 
         def regroup(dst_nj, src_jn):
             nc.scalar.copy(interleaved(dst_nj), by_fours(src_jn))
 
         weighted_half(0, x_q0, wt0, 2)
-        gather_w(0, H)
-        gather_w(H, H)
-        gather_w(N, N)
-        xm_raw1b = sb("xm_raw1b", [P, PACK, D // 2], F32, "v_all0")
+        late_pair = v_picked[:, 2, H : 3 * H].rearrange("p (j n) -> p j n", j=2)
+        gather_w(w_early[:, :H], 0, H)
+        gather_v(3, H, H, late_pair[:, 1, :])
+        xm_raw1b = sb("xm_raw1b", [P, PACK, D // 2], F32, "v_all3")
         nc.sync.dma_start(xm_raw1b[:], xm_rows[1][:, :, D // 2 :])
-        g_bf0 = sb("g_bf0", [P, H, PACK], BF16)[:]
+        weave(v_bf0[1][:, :, 2:], late_pair)
+        gather_w(w_early[:, H:], H, W_EARLY - H)
+        g_bf0 = sb("g_bf0", [P, H, PACK], BF16)
         for c in range(2):
             mean_chunk(c, x_q0, c)
             multiply(nc.vector, c, g_bf0)
         xm_q0 = planes("xm0", D)
         xm_bf00 = sb("xm_bf00", [P, P, PACK], BF16)
-        nc.scalar.copy(interleaved(xm_bf00[:]), by_fours(xm_raw0a[:, :, block(0)]))
+        regroup(xm_bf00[:], xm_raw0[:, :, block(0)])
         quantize(xm_q0, block(0), flat(xm_bf00[:]), E4M3)
         wt1 = load_wt(1, "xm_bf00")
-        quantize_g(0, g_bf0)
+        quantize_g(0, g_bf0[:])
+        v_q.append(planes("v1", H, "av_wt0"))
+        quantize(v_q[1], slice(0, H), flat(v_bf0[1][:]), E4M3)
+        w_late = sb("w_late", [P, B * N - W_EARLY], U32, "g_bf0")
+        w_q.append((w_late, ws[:].bitcast(U8)[:, W_EARLY:]))
+        gather_w(w_late[:], W_EARLY, B * N - W_EARLY)
         v_q.append(planes("v2", H, "mean0"))
         quantize(v_q[2], slice(0, H), flat(v_bf2), E4M3)
-        v_q.append(planes("v3", H, "av_wt0"))
-        quantize(v_q[3], slice(0, H), flat(v_bf3), E4M3)
-        xm_bf01 = work[:, 2 * P : 3 * P, :]
-        nc.scalar.copy(interleaved(xm_bf01), by_fours(xm_raw0a[:, :, block(1)]))
+        xm_bf01 = work[:, block(2), :]
+        regroup(xm_bf01, xm_raw0[:, :, block(1)])
         quantize(xm_q0, block(1), flat(xm_bf01), E4M3)
         place(0, product(xm_q0, block(0), 0, 6), 0, H)
         xm_bf0b = work[:, P : 3 * P, :]
-        weave(xm_bf0b, xm_raw0b[:])
+        xm_raw0b = xm_raw0[:, :, D // 2 :]
+        weave(xm_bf0b[:, SCALAR_SHARE:, :], xm_raw0b[:, :, SCALAR_SHARE:])
+        regroup(xm_bf0b[:, :SCALAR_SHARE, :], xm_raw0b[:, :, :SCALAR_SHARE])
         weighted_half(1, x_q0, wt0, 0)
         quantize(xm_q0, block(1, D // 2), flat(xm_bf0b), E4M3)
-        g_bf1 = xm_bf0b
-        for c in (2, 3):
-            mean_chunk(c, x_q0, c)
-            multiply(nc.gpsimd, c, g_bf1)
-        place(1, product(xm_q0, block(1), 0, 7), 0, H)
-        x_bf1 = work[:, 3 * P :, :].rearrange("p (t m) j -> p t m j", t=PACK)
+        g_bf1 = work[:, 2 * P : 4 * P, :]
+        mean_chunk(2, x_q0, 2)
+        multiply(nc.gpsimd, 2, g_bf1)
+        place(1, product(xm_q0, block(1), 0, 7), 0, H, unit=3)
+        mean_chunk(3, x_q0, 3)
+        multiply(nc.gpsimd, 3, g_bf1)
+        x_bf1 = work[:, 4 * P :, :].rearrange("p (t m) j -> p t m j", t=PACK)
         deal_x(x_bf1, x_raw1[:, :, : R // 2], 0)
         place(2, product(xm_q0, block(2), 0, 6), 0, H)
         deal_x(x_bf1, x_raw1[:, :, R // 2 :], R // 2)
@@ -268,44 +271,47 @@ def tile_attend_ghv_poi_kernel(tc, xT, w_words, w_scales, vT, wt, xm, offs, out)
         x_q1 = [(whole_q, block(t)) for t in range(PACK)]
         place(3, acc, 0, H)
 
-        xm_bf1a = work[:, 2 * P : 4 * P, :]
-        weave(xm_bf1a, xm_raw1a[:])
+        v_bf3 = work[:, 3 * P : 5 * P, :]
+        v_last = v_picked[:, :, block(3, H)]
+        weave(v_bf3[:, SCALAR_SHARE:, :], v_last[:, :, SCALAR_SHARE:])
+        regroup(v_bf3[:, :SCALAR_SHARE, :], v_last[:, :, :SCALAR_SHARE])
+        xm_bf1a = sb("xm_bf1a", [P, D // 2, PACK], BF16, "dw3_0")
+        weave(xm_bf1a[:], xm_raw1a[:])
         place(0, product(xm_q0, block(0), 1, 7), 1, H)
+        v_q.append(planes("v3", H))
+        quantize(v_q[3], slice(0, H), flat(v_bf3), E4M3)
         g_bf2 = work[:, 4 * P : 6 * P, :]
         mean_chunk(4, x_q1, 4)
         weighted_half(2, x_q1, wt1, 0)
         multiply(nc.gpsimd, 4, g_bf2)
-        place(1, product(xm_q0, block(1), 1, 6), 1, H)
+        place(1, product(xm_q0, block(1), 1, 4), 1, H, unit=5)
         mean_chunk(5, x_q1, 5)
         multiply(nc.gpsimd, 5, g_bf2)
         place(2, product(xm_q0, block(2), 1, 7), 1, H)
         acc = product(xm_q0, block(3), 1, 7)
         xm_q1a = planes("xm1a", D // 2, "xm0_codes")
-        quantize(xm_q1a, slice(0, D // 2), flat(xm_bf1a), E4M3)
+        quantize(xm_q1a, slice(0, D // 2), flat(xm_bf1a[:]), E4M3)
         quantize_g(2, g_bf2)
         weighted_half(3, x_q1, wt1, 2)
-        g_bf3 = work[:, 7 * P // 2 : 11 * P // 2, :]
+        g_bf3 = work[:, 5 * P : 7 * P, :]
         mean_chunk(6, x_q1, 4)
         multiply(nc.gpsimd, 6, g_bf3)
-        place(3, acc, 1, H)
+        place(3, acc, 1, H, unit=6)
         mean_chunk(7, x_q1, 5)
         multiply(nc.gpsimd, 7, g_bf3)
-        xm_bf1b = []
-        for k, tag in enumerate(("dw1_1", "dw2_1")):
-            xm_bf1b.append(sb("xm_bf1b%d" % k, [P, P, PACK], BF16, tag))
-            regroup(xm_bf1b[k][:], xm_raw1b[:, :, block(k)])
         place(0, product(xm_q1a, block(0), 2, 6), 2, H)
         acc = product(xm_q1a, block(1), 2, 6)
         quantize_g(3, g_bf3)
-        place(1, acc, 2, H, "dw1_2")
-        xm_q1b = planes("xm1b", D // 2, "dw1_2")
-        for k in range(2):
-            quantize(xm_q1b, block(k), flat(xm_bf1b[k][:]), E4M3)
+        place(1, acc, 2, H)
+        xm_bf1b = work[:, 6 * P :, :]
+        weave(xm_bf1b, xm_raw1b[:])
+        xm_q1b = planes("xm1b", D // 2)
+        quantize(xm_q1b, slice(0, D // 2), flat(xm_bf1b), E4M3)
         for k in range(D // P):
             xm_q1 = xm_q1a if k < 2 else xm_q1b
             acc = product(xm_q1, block(k % 2), 3, 7 - k % 2)
             if k < 2:
-                place(k, acc, 3, H)
+                place(k, acc, 3, H, "v_all3" if k == 1 else None)
             else:
                 place(k, acc, 2, N)
             nc.sync.dma_start(out[block(k), :], placed[k][:])

@@ -52,8 +52,8 @@ def tile_attend_ghv_poi_kernel(tc, xT, w_words, w_scales, vT, wt, xm, offs, out)
         def flat(tile_nj):
             return tile_nj.rearrange("p n j -> p (n j)")
 
-        def planes(name, width, tag=None):
-            return sb(name + "_codes", [P, width], U32, tag), sb(name + "_scales", [P, width], U8)
+        def planes(name, width, tag=None, scale_tag=None):
+            return sb(name + "_codes", [P, width], U32, tag), sb(name + "_scales", [P, width], U8, scale_tag)
 
         def quantize(q, cols, grouped, fmt):
             nc.vector.quantize_mx(out=q[0][:, cols].bitcast(fmt), scales=q[1][:, cols], in_=grouped)
@@ -133,11 +133,13 @@ def tile_attend_ghv_poi_kernel(tc, xT, w_words, w_scales, vT, wt, xm, offs, out)
         def weave(dst_nj, src_jn):
             nc.gpsimd.tensor_scalar(dst_nj, src_jn.rearrange("p j n -> p n j"), 1.0, 0.0, MULT, ADD)
 
-        gather_v(2, 0, B * N)
+        early_pair = sb("early_pair", [P, 2, H], F32)
+        gather_v(2, 0, H, early_pair[:, 0, :])
+        gather_v(2, H, B * N - H)
         x_raw1 = sb("x_raw1", [P, PACK, R], F32, "v_all2")
         nc.sync.dma_start(x_raw1[:], xT[1].rearrange("(p j) r -> p j r", j=PACK))
-        gather_v(3, 0, H)
-        weave(v_bf0[0][:, :, 2:], v_picked[:, 2:, :H])
+        gather_v(3, 0, H, early_pair[:, 1, :])
+        weave(v_bf0[0][:, :, 2:], early_pair[:])
         gather_v(3, N, N)
 
         def deal_x(x_bf, raw, first, t0=0, tiles=PACK):
@@ -153,7 +155,7 @@ def tile_attend_ghv_poi_kernel(tc, xT, w_words, w_scales, vT, wt, xm, offs, out)
         v_q = [planes("v0", H)]
         quantize(v_q[0], slice(0, H), flat(v_bf0[0][:]), E4M3)
         x_q0 = []
-        for u, tag in enumerate((None, "v_bf0_0")):
+        for u, tag in enumerate(("early_pair", "v_bf0_0")):
             pair_q = planes("x0_%d" % u, R // 2, tag)
             quantize(pair_q, slice(0, R // 2), x_bf0[u][:].rearrange("p t m j -> p (t m j)"), E4M3)
             x_q0.extend([(pair_q, block(0)), (pair_q, block(1))])
@@ -227,7 +229,7 @@ def tile_attend_ghv_poi_kernel(tc, xT, w_words, w_scales, vT, wt, xm, offs, out)
         nc.sync.dma_start(xm_raw1b[:], xm_rows[1][:, :, D // 2 :])
         weave(v_bf0[1][:, :, 2:], late_pair)
         gather_w(w_early[:, H:], H, W_EARLY - H)
-        g_bf0 = sb("g_bf0", [P, H, PACK], BF16)
+        g_bf0 = late_pair.rearrange("p j n -> p (j n)").bitcast(BF16).rearrange("p (n j) -> p n j", j=PACK)
         for c in range(2):
             mean_chunk(c, x_q0, c)
             multiply(nc.vector, c, g_bf0)
@@ -235,11 +237,11 @@ def tile_attend_ghv_poi_kernel(tc, xT, w_words, w_scales, vT, wt, xm, offs, out)
         xm_bf00 = sb("xm_bf00", [P, P, PACK], BF16)
         regroup(xm_bf00[:], xm_raw0[:, :, block(0)])
         quantize(xm_q0, block(0), flat(xm_bf00[:]), E4M3)
-        wt1 = load_wt(1, "xm_bf00")
-        quantize_g(0, g_bf0[:])
+        quantize_g(0, g_bf0)
         v_q.append(planes("v1", H, "av_wt0"))
         quantize(v_q[1], slice(0, H), flat(v_bf0[1][:]), E4M3)
-        w_late = sb("w_late", [P, B * N - W_EARLY], U32, "g_bf0")
+        wt1 = load_wt(1, "v_bf0_1")
+        w_late = sb("w_late", [P, B * N - W_EARLY], U32, "xm_bf00")
         w_q.append((w_late, ws[:].bitcast(U8)[:, W_EARLY:]))
         gather_w(w_late[:], W_EARLY, B * N - W_EARLY)
         v_q.append(planes("v2", H, "mean0"))
@@ -257,7 +259,7 @@ def tile_attend_ghv_poi_kernel(tc, xT, w_words, w_scales, vT, wt, xm, offs, out)
         g_bf1 = work[:, 2 * P : 4 * P, :]
         mean_chunk(2, x_q0, 2)
         multiply(nc.gpsimd, 2, g_bf1)
-        place(1, product(xm_q0, block(1), 0, 7), 0, H, unit=3)
+        place(1, product(xm_q0, block(1), 0, 7), 0, H)
         mean_chunk(3, x_q0, 3)
         multiply(nc.gpsimd, 3, g_bf1)
         x_bf1 = work[:, 4 * P :, :].rearrange("p (t m) j -> p t m j", t=PACK)
@@ -266,7 +268,7 @@ def tile_attend_ghv_poi_kernel(tc, xT, w_words, w_scales, vT, wt, xm, offs, out)
         deal_x(x_bf1, x_raw1[:, :, R // 2 :], R // 2)
         acc = product(xm_q0, block(3), 0, 6)
         quantize_g(1, g_bf1)
-        whole_q = planes("x1", R)
+        whole_q = planes("x1", R, "mean1")
         quantize(whole_q, slice(0, R), x_bf1.rearrange("p t m j -> p (t m j)"), E4M3)
         x_q1 = [(whole_q, block(t)) for t in range(PACK)]
         place(3, acc, 0, H)
@@ -275,28 +277,29 @@ def tile_attend_ghv_poi_kernel(tc, xT, w_words, w_scales, vT, wt, xm, offs, out)
         v_last = v_picked[:, :, block(3, H)]
         weave(v_bf3[:, SCALAR_SHARE:, :], v_last[:, :, SCALAR_SHARE:])
         regroup(v_bf3[:, :SCALAR_SHARE, :], v_last[:, :, :SCALAR_SHARE])
-        xm_bf1a = sb("xm_bf1a", [P, D // 2, PACK], BF16, "dw3_0")
-        weave(xm_bf1a[:], xm_raw1a[:])
-        place(0, product(xm_q0, block(0), 1, 7), 1, H)
+        xm_bf1a = work[:, 5 * P : 7 * P, :]
+        regroup(xm_bf1a[:, block(0), :], xm_raw1a[:, :, block(0)])
         v_q.append(planes("v3", H))
         quantize(v_q[3], slice(0, H), flat(v_bf3), E4M3)
-        g_bf2 = work[:, 4 * P : 6 * P, :]
+        place(0, product(xm_q0, block(0), 1, 7), 1, H, unit=7)
+        g_bf2 = v_bf3
         mean_chunk(4, x_q1, 4)
         weighted_half(2, x_q1, wt1, 0)
         multiply(nc.gpsimd, 4, g_bf2)
-        place(1, product(xm_q0, block(1), 1, 4), 1, H, unit=5)
+        place(1, product(xm_q0, block(1), 1, 6), 1, H)
         mean_chunk(5, x_q1, 5)
         multiply(nc.gpsimd, 5, g_bf2)
         place(2, product(xm_q0, block(2), 1, 7), 1, H)
         acc = product(xm_q0, block(3), 1, 7)
-        xm_q1a = planes("xm1a", D // 2, "xm0_codes")
-        quantize(xm_q1a, slice(0, D // 2), flat(xm_bf1a[:]), E4M3)
+        regroup(xm_bf1a[:, block(1), :], xm_raw1a[:, :, block(1)])
+        xm_q1a = planes("xm1a", D // 2, "mean2", "xm0_scales")
+        quantize(xm_q1a, slice(0, D // 2), flat(xm_bf1a), E4M3)
         quantize_g(2, g_bf2)
         weighted_half(3, x_q1, wt1, 2)
-        g_bf3 = work[:, 5 * P : 7 * P, :]
+        g_bf3 = work[:, 9 * P // 2 : 13 * P // 2, :]
         mean_chunk(6, x_q1, 4)
         multiply(nc.gpsimd, 6, g_bf3)
-        place(3, acc, 1, H, unit=6)
+        place(3, acc, 1, H)
         mean_chunk(7, x_q1, 5)
         multiply(nc.gpsimd, 7, g_bf3)
         place(0, product(xm_q1a, block(0), 2, 6), 2, H)

@@ -23,9 +23,10 @@ LIST_ROWS = 16
 CHUNK = 128
 H = N // 2
 SCALE_FIRST = 32
-V_FIRST = 896
-SCALAR_SHARE = 64
-W_EARLY = 3 * H
+SCALE_STEP = 4
+V_CUTS = ((1024, 1024), (1024, 1024))
+V_SCALAR = ((1024, 1024), (1024, 352))
+X_AT = 2 * N - R // 2
 
 
 def tile_attend_ghv_poi_kernel(tc, xT, w_words, w_scales, vT, wt, xm, offs, out):
@@ -52,6 +53,9 @@ def tile_attend_ghv_poi_kernel(tc, xT, w_words, w_scales, vT, wt, xm, offs, out)
         def flat(tile_nj):
             return tile_nj.rearrange("p n j -> p (n j)")
 
+        def as_pairs(tile_nj, dtype):
+            return flat(tile_nj).bitcast(dtype).rearrange("p (n h) -> p n h", h=2)
+
         def planes(name, width, tag=None, scale_tag=None):
             return sb(name + "_codes", [P, width], U32, tag), sb(name + "_scales", [P, width], U8, scale_tag)
 
@@ -70,8 +74,13 @@ def tile_attend_ghv_poi_kernel(tc, xT, w_words, w_scales, vT, wt, xm, offs, out)
             )
 
         v_rows = vT.rearrange("(p j) t -> p j t", j=PACK)
-        v_all = [sb("v_all%d" % j, [P, T], F32) for j in range(PACK)]
-        nc.sync.dma_start(v_all[0][:, :V_FIRST], v_rows[:, 0, :V_FIRST])
+        v_raw = [[sb("v_raw%d%d" % (h, c), [P, 2, w], F32) for c, w in enumerate(V_CUTS[h])] for h in range(2)]
+
+        def load_v(h, c):
+            first = sum(V_CUTS[h][:c])
+            nc.sync.dma_start(v_raw[h][c][:], v_rows[:, 2 * h : 2 * h + 2, first : first + V_CUTS[h][c]])
+
+        load_v(0, 0)
         offsets = keep.tile([P, B * N // LIST_ROWS], U16, name="offsets")
         nc.sync.dma_start(offsets[:], offs)
 
@@ -82,97 +91,105 @@ def tile_attend_ghv_poi_kernel(tc, xT, w_words, w_scales, vT, wt, xm, offs, out)
         nc.gpsimd.memset(ws_all[:], 0)
         ws = sb("ws", [P, B * N // 4], I32)
         nc.gpsimd.memset(ws[:], 0)
-        nc.sync.dma_start(ws_all[SCALE_FIRST : SCALE_FIRST + 16 * 4 : 4, :], w_scales[0].bitcast(I32))
-        nc.sync.dma_start(v_all[0][:, V_FIRST:], v_rows[:, 0, V_FIRST:])
-        for j in range(1, PACK):
-            nc.sync.dma_start(v_all[j][:], v_rows[:, j, :])
+        nc.sync.dma_start(ws_all[SCALE_FIRST : SCALE_FIRST + 16 * SCALE_STEP : SCALE_STEP, :], w_scales[0].bitcast(I32))
+        load_v(0, 1)
+        for c in range(2):
+            load_v(1, c)
 
         def load_wt(b, tag=None):
             wt_b = sb("wt%d" % b, [P, PACK], F32, tag)
             nc.sync.dma_start(wt_b[:], wt[b].rearrange("(p t) o -> p (t o)", t=PACK))
             return wt_b
 
+        x_home = sb("x_home", [P, X_AT + PACK * R], F32)
+        x_raw0 = x_home[:, X_AT:].rearrange("p (j r) -> p j r", j=PACK)
+        nc.sync.dma_start(x_raw0, xT[0].rearrange("(p j) r -> p j r", j=PACK))
+        wt0 = load_wt(0)
+        w_all = sb("w_all", [P, T], I32)
+        nc.sync.dma_start(w_all[:], w_words[0].rearrange("p n t -> p (n t)").bitcast(I32))
+
         placed = [sb("placed%d" % k, [P, T], F32) for k in range(D // P)]
         for k in range(D // P):
             nc.gpsimd.memset(placed[k][:], 0.0)
         g_q = planes("g", B * N)
-        nc.gpsimd.memset(g_q[0][:, H:].bitcast(I32), 0)
-        nc.gpsimd.memset(g_q[1][:, H:].bitcast(I32), 0)
+        nc.gpsimd.memset(g_q[0][:, block(1, H)].bitcast(I32), 0)
+        nc.gpsimd.memset(g_q[1][:, block(1, H)].bitcast(I32), 0)
+
+        v_pairs = [sb("v_pairs%d" % h, [P, T, 2], BF16) for h in range(2)]
+
+        def round_v(h, c):
+            first, share, width = sum(V_CUTS[h][:c]), V_SCALAR[h][c], V_CUTS[h][c]
+            dst, src = v_pairs[h][:, first : first + width, :], v_raw[h][c]
+            if share > 0:
+                nc.scalar.activation(interleaved(dst[:, :share, :]), by_fours(src[:, :, :share]), ACT.Copy)
+            if share < width:
+                nc.vector.tensor_copy(interleaved(dst[:, share:, :]), by_fours(src[:, :, share:]))
+
+        round_v(0, 0)
 
         ws_picked = sb("ws_picked", [P, B * N], U8)
         nc.vector.tensor_copy(ws_picked[:], ws_all[:].bitcast(U8).indirect(offsets[:]))
         for q in range(4):
-            rows = slice(SCALE_FIRST + 16 * q, SCALE_FIRST + 16 * (q + 1), 4)
+            rows = slice(SCALE_FIRST + 4 * SCALE_STEP * q, SCALE_FIRST + 4 * SCALE_STEP * (q + 1), SCALE_STEP)
             nc.sync.dma_start(ws[32 * q : 32 * q + 4, :], ws_picked[rows, :].bitcast(I32))
 
+        round_v(0, 1)
+
+        spans = ((0, H), (H, H), (N, N))
+        v_picked = [sb("v_picked%d" % s, [P, 2, count], U32)[:] for s, (first, count) in enumerate(spans)]
+
+        def gather_pair(h, s):
+            nc.vector.tensor_copy(v_picked[s][:, h, :], flat(v_pairs[h][:]).bitcast(U32).indirect(listed(*spans[s])))
+
+        for s in range(3):
+            gather_pair(0, s)
+        round_v(1, 0)
         xm_rows = [xm[b].rearrange("(p j) d -> p j d", j=PACK) for b in range(B)]
-        x0_rows = xT[0].rearrange("(p j) r -> p j r", j=PACK)
-        x_flat0 = sb("x_flat0", [P, PACK * R], F32, "ws_all")
-        x_raw0 = [x_flat0[:, block(h, PACK * R // 2)].rearrange("p (j r) -> p j r", j=PACK) for h in range(2)]
-        for h in range(2):
-            nc.sync.dma_start(x_raw0[h], x0_rows[:, :, block(h, R // 2)])
-
-        v_flat = sb("v_flat", [P, PACK * B * N], F32)
-        v_picked = v_flat[:].rearrange("p (j n) -> p j n", j=PACK)
-
-        def gather_v(j, first, count, dst=None):
-            dst = v_picked[:, j, first : first + count] if dst is None else dst
-            nc.vector.tensor_copy(dst, v_all[j][:].indirect(listed(first, count)))
-
-        gather_v(0, 0, B * N)
-        w_all = sb("w_all", [P, T], I32, "v_all0")
-        nc.sync.dma_start(w_all[:], w_words[0].rearrange("p n t -> p (n t)").bitcast(I32))
-        wt0 = load_wt(0, "ws_picked")
-        gather_v(1, 0, B * N)
-        xm_raw0 = sb("xm_raw0", [P, PACK, D], F32, "v_all1")
-        nc.sync.dma_start(xm_raw0[:], xm_rows[0])
-        v_bf0 = [sb("v_bf0_%d" % h, [P, H, PACK], BF16) for h in range(2)]
-        for h in range(2):
-            nc.scalar.copy(interleaved(v_bf0[h][:, :, :2]), by_fours(v_picked[:, :2, block(h, H)]))
-
-        def weave(dst_nj, src_jn):
-            nc.gpsimd.tensor_scalar(dst_nj, src_jn.rearrange("p j n -> p n j"), 1.0, 0.0, MULT, ADD)
-
-        early_pair = sb("early_pair", [P, 2, H], F32)
-        gather_v(2, 0, H, early_pair[:, 0, :])
-        gather_v(2, H, B * N - H)
-        x_raw1 = sb("x_raw1", [P, PACK, R], F32, "v_all2")
+        xm_raw0 = [sb("xm_raw0%d" % k, [P, PACK, P], F32, tag)[:] for k, tag in enumerate(("ws_all", "v_raw01"))]
+        for k in range(2):
+            nc.sync.dma_start(xm_raw0[k], xm_rows[0][:, :, block(k)])
+        xm_raw0b = sb("xm_raw0b", [P, PACK, D // 2], F32, "v_raw10")[:]
+        nc.sync.dma_start(xm_raw0b, xm_rows[0][:, :, D // 2 :])
+        round_v(1, 1)
+        for s in range(3):
+            gather_pair(1, s)
+        x_raw1 = sb("x_raw1", [P, PACK, R], F32, "v_pairs1")
         nc.sync.dma_start(x_raw1[:], xT[1].rearrange("(p j) r -> p j r", j=PACK))
-        gather_v(3, 0, H, early_pair[:, 1, :])
-        weave(v_bf0[0][:, :, 2:], early_pair[:])
-        gather_v(3, N, N)
 
-        def deal_x(x_bf, raw, first, t0=0, tiles=PACK):
+        def weave_pairs(s, v_bf):
+            nc.scalar.copy(interleaved(as_pairs(v_bf, U32)), by_fours(v_picked[s]))
+
+        v_bf0, v_bf1 = (sb("v_bf%d" % s, [P, H, PACK], BF16)[:] for s in range(2))
+        weave_pairs(0, v_bf0)
+        weave_pairs(1, v_bf1)
+
+        def deal_x(copy, x_bf, raw, first):
             src = raw.rearrange("p j (m e t) -> p m j e t", e=2, t=PACK)
             dst = x_bf.rearrange("p t (m e) j -> p m j e t", e=2)
             pairs = slice(first // 8, first // 8 + src.shape[1])
-            nc.scalar.copy(dst[:, pairs, :, :, :], src[:, :, :, :, t0 : t0 + tiles])
+            copy(dst[:, pairs, :, :, :], src)
 
-        x_bf0 = [sb("x_bf0_%d" % u, [P, 2, P, PACK], BF16) for u in range(2)]
-        for h in range(2):
-            for u in range(2):
-                deal_x(x_bf0[u][:], x_raw0[h], h * R // 2, 2 * u, 2)
-        v_q = [planes("v0", H)]
-        quantize(v_q[0], slice(0, H), flat(v_bf0[0][:]), E4M3)
+        x_bf0 = sb("x_bf0", [P, PACK, P, PACK], BF16)[:]
+        deal_x(nc.scalar.copy, x_bf0, x_raw0[:, :, : R // 2], 0)
+        v_q0 = planes("v0", H)
+        quantize(v_q0, slice(0, H), flat(v_bf0), E4M3)
+        deal_x(nc.vector.tensor_copy, x_bf0, x_raw0[:, :, R // 2 :], R // 2)
+        v_bf23 = x_home[:, : 2 * N].bitcast(BF16).rearrange("p (n j) -> p n j", j=PACK)
+        weave_pairs(2, v_bf23)
         x_q0 = []
-        for u, tag in enumerate(("early_pair", "v_bf0_0")):
-            pair_q = planes("x0_%d" % u, R // 2, tag)
-            quantize(pair_q, slice(0, R // 2), x_bf0[u][:].rearrange("p t m j -> p (t m j)"), E4M3)
+        for u in range(2):
+            pair_q = planes("x0_%d" % u, R // 2)
+            quantize(pair_q, slice(0, R // 2), x_bf0[:, 2 * u : 2 * u + 2].rearrange("p t m j -> p (t m j)"), E4M3)
             x_q0.extend([(pair_q, block(0)), (pair_q, block(1))])
-        xm_raw1a = sb("xm_raw1a", [P, PACK, D // 2], F32, "x_bf0_0")
-        nc.sync.dma_start(xm_raw1a[:], xm_rows[1][:, :, : D // 2])
-        work = sb("work", [P, 8 * P, PACK], BF16, "ws_all")
-        v_bf2 = work[:, : 2 * P, :]
-        nc.scalar.copy(interleaved(v_bf2), by_fours(v_picked[:, :, block(2, H)]))
 
-        mean = [sb("mean%d" % h, [P, H // 4, PACK, 4], F32) for h in range(4)]
+        mean = [sb("mean%d" % h, [P, H // 4, PACK, 4], F32, "v_raw01" if h == 1 else None) for h in range(4)]
         av_wt = [sb("av_wt%d" % h, [P, H // 4, PACK, 4], F32) for h in range(4)]
 
-        def weighted_half(half, x_q, wt_b, bank):
+        def weighted_half(half, x_q, v_q, v_cols, wt_b, bank):
             for pair in range(2):
                 av = in_bank(bank + pair, [P, 2, H])
                 for u in range(2):
-                    mx(av[:, u, :], *x_q[2 * pair + u], v_q[half], slice(0, H), E4M3)
+                    mx(av[:, u, :], *x_q[2 * pair + u], v_q, v_cols, E4M3)
                 for u in range(2):
                     t = 2 * pair + u
                     nc.scalar.activation(
@@ -182,17 +199,18 @@ def tile_attend_ghv_poi_kernel(tc, xT, w_words, w_scales, vT, wt, xm, offs, out)
                         scale=wt_b[:, t : t + 1],
                     )
 
-        w_early = sb("w_early", [P, W_EARLY], U32, "x_bf0_1")
-        w_q = [(w_early, ws[:].bitcast(U8)[:, :W_EARLY])]
+        w_q = []
 
-        def gather_w(dst, first, count):
-            nc.vector.tensor_copy(dst, w_all[:].bitcast(U32).indirect(listed(first, count)))
+        def gather_w(first, count, tag=None):
+            picked = sb("w_picked%d" % first, [P, count], U32, tag)
+            nc.vector.tensor_copy(picked[:], w_all[:].bitcast(U32).indirect(listed(first, count)))
+            both = (picked, ws[:].bitcast(U8)[:, first : first + count])
+            w_q.extend((both, block(i)) for i in range(count // CHUNK))
 
         def mean_chunk(c, x_q, bank):
-            late = c * CHUNK // W_EARLY
             a = in_bank(bank, [P, PACK, CHUNK])
             for t in range(PACK):
-                mx(a[:, t, :], *x_q[t], w_q[late], block(c - late * W_EARLY // CHUNK), E4M3)
+                mx(a[:, t, :], *x_q[t], *w_q[c], E4M3)
             nc.scalar.activation(mean[c // 2][:, block(c % 2, CHUNK // 4), :, :], by_fours(a[:]), ACT.Exp)
 
         def multiply(engine, c, g_bf):
@@ -204,117 +222,109 @@ def tile_attend_ghv_poi_kernel(tc, xT, w_words, w_scales, vT, wt, xm, offs, out)
         def quantize_g(half, g_bf):
             quantize(g_q, block(half, H), flat(g_bf), E5M2)
 
-        def product(xm_q, cols, half, bank):
+        def product(xm_q, k, half, bank):
             acc = in_bank(bank, [P, N])
-            mx(acc[:], xm_q, cols, g_q, slice(min(half, 2) * H, min(half, 2) * H + N), E5M2)
+            first = max(half - 1, 0) * H
+            mx(acc[:], *xm_q[k], g_q, slice(first, first + N), E5M2)
             return acc
 
-        def place(k, acc, half, count, tag=None, unit=None):
-            if unit is None:
-                dw = sb("dw%d_%d" % (k, half), [P, count], F32, tag)[:]
-            else:
-                dw = flat(work[:, block(unit), :]).bitcast(F32)
-            first = max(half - 2, 0) * H
+        def place(k, acc, first, slot, count, tag=None, dw=None):
+            if dw is None:
+                dw = sb("dw%d_%d" % (k, slot), [P, count], F32, tag)[:]
             nc.scalar.copy(dw, acc[:, first : first + count])
-            nc.vector.tensor_copy(placed[k][:].indirect(listed(half * H, count)), dw)
+            nc.vector.tensor_copy(placed[k][:].indirect(listed(slot, count)), dw)
 
         def regroup(dst_nj, src_jn):
             nc.scalar.copy(interleaved(dst_nj), by_fours(src_jn))
 
-        weighted_half(0, x_q0, wt0, 2)
-        late_pair = v_picked[:, 2, H : 3 * H].rearrange("p (j n) -> p j n", j=2)
-        gather_w(w_early[:, :H], 0, H)
-        gather_v(3, H, H, late_pair[:, 1, :])
-        xm_raw1b = sb("xm_raw1b", [P, PACK, D // 2], F32, "v_all3")
-        nc.sync.dma_start(xm_raw1b[:], xm_rows[1][:, :, D // 2 :])
-        weave(v_bf0[1][:, :, 2:], late_pair)
-        gather_w(w_early[:, H:], H, W_EARLY - H)
-        g_bf0 = late_pair.rearrange("p j n -> p (j n)").bitcast(BF16).rearrange("p (n j) -> p n j", j=PACK)
+        def weave(dst_nj, src_jn):
+            nc.gpsimd.tensor_scalar(dst_nj, src_jn.rearrange("p j n -> p n j"), 1.0, 0.0, MULT, ADD)
+
+        weighted_half(0, x_q0, v_q0, slice(0, H), wt0, 2)
+        gather_w(0, H)
+        gather_w(H, 2 * H)
+        v_q23 = planes("v23", N, "ws_picked")
+        quantize(v_q23, slice(0, N), flat(v_bf23), E4M3)
+        xm_raw1 = sb("xm_raw1", [P, PACK, D], F32, "x_home")
+        nc.sync.dma_start(xm_raw1[:], xm_rows[1])
+        wt1 = load_wt(1, "v_picked2")
+        g_bf0 = sb("g_bf0", [P, H, PACK], BF16)
         for c in range(2):
             mean_chunk(c, x_q0, c)
+        for c in range(2):
             multiply(nc.vector, c, g_bf0)
-        xm_q0 = planes("xm0", D)
-        xm_bf00 = sb("xm_bf00", [P, P, PACK], BF16)
-        regroup(xm_bf00[:], xm_raw0[:, :, block(0)])
-        quantize(xm_q0, block(0), flat(xm_bf00[:]), E4M3)
-        quantize_g(0, g_bf0)
-        v_q.append(planes("v1", H, "av_wt0"))
-        quantize(v_q[1], slice(0, H), flat(v_bf0[1][:]), E4M3)
-        wt1 = load_wt(1, "v_bf0_1")
-        w_late = sb("w_late", [P, B * N - W_EARLY], U32, "xm_bf00")
-        w_q.append((w_late, ws[:].bitcast(U8)[:, W_EARLY:]))
-        gather_w(w_late[:], W_EARLY, B * N - W_EARLY)
-        v_q.append(planes("v2", H, "mean0"))
-        quantize(v_q[2], slice(0, H), flat(v_bf2), E4M3)
-        xm_bf01 = work[:, block(2), :]
-        regroup(xm_bf01, xm_raw0[:, :, block(1)])
-        quantize(xm_q0, block(1), flat(xm_bf01), E4M3)
-        place(0, product(xm_q0, block(0), 0, 6), 0, H)
-        xm_bf0b = work[:, P : 3 * P, :]
-        xm_raw0b = xm_raw0[:, :, D // 2 :]
-        weave(xm_bf0b[:, SCALAR_SHARE:, :], xm_raw0b[:, :, SCALAR_SHARE:])
-        regroup(xm_bf0b[:, :SCALAR_SHARE, :], xm_raw0b[:, :, :SCALAR_SHARE])
-        weighted_half(1, x_q0, wt0, 0)
-        quantize(xm_q0, block(1, D // 2), flat(xm_bf0b), E4M3)
-        g_bf1 = work[:, 2 * P : 4 * P, :]
+        xm_q0, xm_q1 = [], []
+
+        def quantize_xm(xm_q, name, grouped, tag=None):
+            width = grouped.shape[1]
+            both = planes(name, width, tag)
+            quantize(both, slice(0, width), flat(grouped), E4M3)
+            xm_q.extend((both, block(i)) for i in range(width // P))
+
+        xm_bf00 = sb("xm_bf00", [P, P, PACK], BF16, "w_picked0")
+        regroup(xm_bf00[:], xm_raw0[0])
+        quantize_xm(xm_q0, "xm00", xm_bf00[:])
+        quantize_g(0, g_bf0[:])
+        v_q1 = planes("v1", H, "av_wt0")
+        quantize(v_q1, slice(0, H), flat(v_bf1), E4M3)
+        xm_bf01 = sb("xm_bf01", [P, P, PACK], BF16, "ws_all")[:]
+        regroup(xm_bf01, xm_raw0[1])
+        quantize_xm(xm_q0, "xm01", xm_bf01)
+        gather_w(3 * H, H, "g_bf0")
+
+        place(0, product(xm_q0, 0, 0, 4), 0, 0, H)
+        xm_bf0b = sb("xm_bf0b", [P, D // 2, PACK], BF16, "ws_all")[:]
+        weave(xm_bf0b, xm_raw0b)
+        quantize_xm(xm_q0, "xm0b", xm_bf0b)
+        g_bf1 = sb("g_bf1", [P, H, PACK], BF16, "ws_all")[:]
         mean_chunk(2, x_q0, 2)
+        weighted_half(1, x_q0, v_q1, slice(0, H), wt0, 0)
         multiply(nc.gpsimd, 2, g_bf1)
-        place(1, product(xm_q0, block(1), 0, 7), 0, H)
-        mean_chunk(3, x_q0, 3)
+        after_weave = sb("after_weave", [P, PACK * R + 2 * H], BF16, "v_raw10")
+        place(1, product(xm_q0, 1, 0, 7), 0, 0, H, dw=after_weave[:, PACK * R :].bitcast(F32))
+        mean_chunk(3, x_q0, 4)
         multiply(nc.gpsimd, 3, g_bf1)
-        x_bf1 = work[:, 4 * P :, :].rearrange("p (t m) j -> p t m j", t=PACK)
-        deal_x(x_bf1, x_raw1[:, :, : R // 2], 0)
-        place(2, product(xm_q0, block(2), 0, 6), 0, H)
-        deal_x(x_bf1, x_raw1[:, :, R // 2 :], R // 2)
-        acc = product(xm_q0, block(3), 0, 6)
+        place(2, product(xm_q0, 2, 0, 6), 0, 0, H)
+        x_bf1 = after_weave[:, : PACK * R].rearrange("p (t m j) -> p t m j", t=PACK, j=PACK)
+        for h in range(2):
+            deal_x(nc.scalar.copy, x_bf1, x_raw1[:, :, block(h, R // 2)], h * R // 2)
+        acc = product(xm_q0, 3, 0, 5)
         quantize_g(1, g_bf1)
-        whole_q = planes("x1", R, "mean1")
+        whole_q = planes("x1", R, "v_raw01")
         quantize(whole_q, slice(0, R), x_bf1.rearrange("p t m j -> p (t m j)"), E4M3)
         x_q1 = [(whole_q, block(t)) for t in range(PACK)]
-        place(3, acc, 0, H)
+        place(3, acc, 0, 0, H, "av_wt1")
 
-        v_bf3 = work[:, 3 * P : 5 * P, :]
-        v_last = v_picked[:, :, block(3, H)]
-        weave(v_bf3[:, SCALAR_SHARE:, :], v_last[:, :, SCALAR_SHARE:])
-        regroup(v_bf3[:, :SCALAR_SHARE, :], v_last[:, :, :SCALAR_SHARE])
-        xm_bf1a = work[:, 5 * P : 7 * P, :]
-        regroup(xm_bf1a[:, block(0), :], xm_raw1a[:, :, block(0)])
-        v_q.append(planes("v3", H))
-        quantize(v_q[3], slice(0, H), flat(v_bf3), E4M3)
-        place(0, product(xm_q0, block(0), 1, 7), 1, H, unit=7)
-        g_bf2 = v_bf3
+        xm_bf1 = sb("xm_bf1", [P, D, PACK], BF16, "v_raw10")[:]
+        weave(xm_bf1, xm_raw1[:])
+        place(0, product(xm_q0, 0, 1, 7), H, H, H)
+        g_bf2 = sb("g_bf2", [P, H, PACK], BF16, "ws_all")[:]
         mean_chunk(4, x_q1, 4)
-        weighted_half(2, x_q1, wt1, 0)
+        weighted_half(2, x_q1, v_q23, block(0, H), wt1, 0)
         multiply(nc.gpsimd, 4, g_bf2)
-        place(1, product(xm_q0, block(1), 1, 6), 1, H)
+        place(1, product(xm_q0, 1, 1, 6), H, H, H)
         mean_chunk(5, x_q1, 5)
         multiply(nc.gpsimd, 5, g_bf2)
-        place(2, product(xm_q0, block(2), 1, 7), 1, H)
-        acc = product(xm_q0, block(3), 1, 7)
-        regroup(xm_bf1a[:, block(1), :], xm_raw1a[:, :, block(1)])
-        xm_q1a = planes("xm1a", D // 2, "mean2", "xm0_scales")
-        quantize(xm_q1a, slice(0, D // 2), flat(xm_bf1a), E4M3)
+        place(2, product(xm_q0, 2, 1, 7), H, H, H)
+        acc = product(xm_q0, 3, 1, 6)
         quantize_g(2, g_bf2)
-        weighted_half(3, x_q1, wt1, 2)
-        g_bf3 = work[:, 9 * P // 2 : 13 * P // 2, :]
+        quantize_xm(xm_q1, "xm1", xm_bf1, "mean2")
+        weighted_half(3, x_q1, v_q23, block(1, H), wt1, 2)
+        place(3, acc, H, H, H, "av_wt2")
+
+        g_bf3 = sb("g_bf3", [P, H, PACK], BF16, "v_raw10")[:]
         mean_chunk(6, x_q1, 4)
         multiply(nc.gpsimd, 6, g_bf3)
-        place(3, acc, 1, H)
+        place(0, product(xm_q1, 0, 2, 7), H, N, H)
         mean_chunk(7, x_q1, 5)
         multiply(nc.gpsimd, 7, g_bf3)
-        place(0, product(xm_q1a, block(0), 2, 6), 2, H)
-        acc = product(xm_q1a, block(1), 2, 6)
+        acc = product(xm_q1, 1, 2, 7)
         quantize_g(3, g_bf3)
-        place(1, acc, 2, H)
-        xm_bf1b = work[:, 6 * P :, :]
-        weave(xm_bf1b, xm_raw1b[:])
-        xm_q1b = planes("xm1b", D // 2)
-        quantize(xm_q1b, slice(0, D // 2), flat(xm_bf1b), E4M3)
+        place(1, acc, H, N, H, "av_wt3")
         for k in range(D // P):
-            xm_q1 = xm_q1a if k < 2 else xm_q1b
-            acc = product(xm_q1, block(k % 2), 3, 7 - k % 2)
+            acc = product(xm_q1, k, 3, 6 + k % 2)
             if k < 2:
-                place(k, acc, 3, H, "v_all3" if k == 1 else None)
+                place(k, acc, H, 3 * H, H)
             else:
-                place(k, acc, 2, N)
+                place(k, acc, 0, N, N)
             nc.sync.dma_start(out[block(k), :], placed[k][:])

@@ -26,13 +26,15 @@ SCALE_FIRST = 32
 SCALE_STEP = 4
 V_CUTS = ((1024, 1024), (1024, 1024))
 V_SCALAR = ((1024, 1024), (1024, 352))
-X_AT = 2 * N - R // 2
+FIRST_CHUNK = 64
+X1_FIRST = 192
 
 
 def tile_attend_ghv_poi_kernel(tc, xT, w_words, w_scales, vT, wt, xm, offs, out):
     nc = tc.nc
     with ExitStack() as ctx:
         keep = ctx.enter_context(tc.tile_pool(name="keep", bufs=1))
+        after_x = ctx.enter_context(tc.tile_pool(name="after_x", bufs=1))
         psum = ctx.enter_context(tc.psum_pool(name="psum", bufs=1))
 
         def in_bank(i, shape):
@@ -101,8 +103,10 @@ def tile_attend_ghv_poi_kernel(tc, xT, w_words, w_scales, vT, wt, xm, offs, out)
             nc.sync.dma_start(wt_b[:], wt[b].rearrange("(p t) o -> p (t o)", t=PACK))
             return wt_b
 
-        x_home = sb("x_home", [P, X_AT + PACK * R], F32)
-        x_raw0 = x_home[:, X_AT:].rearrange("p (j r) -> p j r", j=PACK)
+        def on_x(name, shape, dtype, at):
+            return after_x.tile(shape, dtype, name=name, align_bytes=64, offset=at)
+
+        x_raw0 = on_x("x_raw0", [P, PACK, R], F32, 0)[:]
         nc.sync.dma_start(x_raw0, xT[0].rearrange("(p j) r -> p j r", j=PACK))
         wt0 = load_wt(0)
         w_all = sb("w_all", [P, T], I32)
@@ -135,13 +139,13 @@ def tile_attend_ghv_poi_kernel(tc, xT, w_words, w_scales, vT, wt, xm, offs, out)
 
         round_v(0, 1)
 
-        spans = ((0, H), (H, H), (N, N))
+        spans = ((0, H), (H, 3 * H))
         v_picked = [sb("v_picked%d" % s, [P, 2, count], U32)[:] for s, (first, count) in enumerate(spans)]
 
         def gather_pair(h, s):
             nc.vector.tensor_copy(v_picked[s][:, h, :], flat(v_pairs[h][:]).bitcast(U32).indirect(listed(*spans[s])))
 
-        for s in range(3):
+        for s in range(2):
             gather_pair(0, s)
         round_v(1, 0)
         xm_rows = [xm[b].rearrange("(p j) d -> p j d", j=PACK) for b in range(B)]
@@ -151,7 +155,7 @@ def tile_attend_ghv_poi_kernel(tc, xT, w_words, w_scales, vT, wt, xm, offs, out)
         xm_raw0b = sb("xm_raw0b", [P, PACK, D // 2], F32, "v_raw10")[:]
         nc.sync.dma_start(xm_raw0b, xm_rows[0][:, :, D // 2 :])
         round_v(1, 1)
-        for s in range(3):
+        for s in range(2):
             gather_pair(1, s)
         x_raw1 = sb("x_raw1", [P, PACK, R], F32, "v_pairs1")
         nc.sync.dma_start(x_raw1[:], xT[1].rearrange("(p j) r -> p j r", j=PACK))
@@ -159,9 +163,8 @@ def tile_attend_ghv_poi_kernel(tc, xT, w_words, w_scales, vT, wt, xm, offs, out)
         def weave_pairs(s, v_bf):
             nc.scalar.copy(interleaved(as_pairs(v_bf, U32)), by_fours(v_picked[s]))
 
-        v_bf0, v_bf1 = (sb("v_bf%d" % s, [P, H, PACK], BF16)[:] for s in range(2))
+        v_bf0 = sb("v_bf0", [P, H, PACK], BF16)[:]
         weave_pairs(0, v_bf0)
-        weave_pairs(1, v_bf1)
 
         def deal_x(copy, x_bf, raw, first):
             src = raw.rearrange("p j (m e t) -> p m j e t", e=2, t=PACK)
@@ -169,21 +172,40 @@ def tile_attend_ghv_poi_kernel(tc, xT, w_words, w_scales, vT, wt, xm, offs, out)
             pairs = slice(first // 8, first // 8 + src.shape[1])
             copy(dst[:, pairs, :, :, :], src)
 
-        x_bf0 = sb("x_bf0", [P, PACK, P, PACK], BF16)[:]
+        x_bf0 = on_x("x_bf0", [P, PACK, P, PACK], BF16, 16 * R)[:]
         deal_x(nc.scalar.copy, x_bf0, x_raw0[:, :, : R // 2], 0)
-        v_q0 = planes("v0", H)
+        nc.gpsimd.tensor_scalar(
+            x_bf0[:, :, P // 2 :, :].rearrange("p t m j -> p m t j"),
+            x_raw0[:, :, R // 2 :].rearrange("p j (m t) -> p m t j", t=PACK),
+            1.0,
+            0.0,
+            MULT,
+            ADD,
+        )
+        v_woven = on_x("v_woven", [P, 3 * H, PACK], BF16, 4 * H)[:]
+        v_bf1, v_bf23 = v_woven[:, :H, :], v_woven[:, H:, :]
+        weave_pairs(1, v_woven)
+        v_q0 = (on_x("v0_codes", [P, H], U32, 0), sb("v0_scales", [P, H], U8))
         quantize(v_q0, slice(0, H), flat(v_bf0), E4M3)
-        deal_x(nc.vector.tensor_copy, x_bf0, x_raw0[:, :, R // 2 :], R // 2)
-        v_bf23 = x_home[:, : 2 * N].bitcast(BF16).rearrange("p (n j) -> p n j", j=PACK)
-        weave_pairs(2, v_bf23)
         x_q0 = []
         for u in range(2):
             pair_q = planes("x0_%d" % u, R // 2)
             quantize(pair_q, slice(0, R // 2), x_bf0[:, 2 * u : 2 * u + 2].rearrange("p t m j -> p (t m j)"), E4M3)
             x_q0.extend([(pair_q, block(0)), (pair_q, block(1))])
 
-        mean = [sb("mean%d" % h, [P, H // 4, PACK, 4], F32, "v_raw01" if h == 1 else None) for h in range(4)]
-        av_wt = [sb("av_wt%d" % h, [P, H // 4, PACK, 4], F32) for h in range(4)]
+        mean = {h: sb("mean%d" % h, [P, H // 4, PACK, 4], F32)[:] for h in (0, 2, 3)}
+        av_wt = {h: sb("av_wt%d" % h, [P, H // 4, PACK, 4], F32)[:] for h in (0, 2, 3)}
+        av_wt[1] = on_x("av_wt1", [P, H // 4, PACK, 4], F32, 24 * R)[:]
+        mean_of = {c: mean[c // 2][:, block(c % 2, CHUNK // 4), :, :] for c in (0, 1, 4, 5, 6, 7)}
+        mean_of[2] = sb("mean1_first", [P, CHUNK // 4, PACK, 4], F32)[:]
+
+        def weigh(half, av, t, wt_b, first, width):
+            nc.scalar.activation(
+                av_wt[half][:, first // 4 : (first + width) // 4, t, :],
+                av.rearrange("p (c i) -> p c i", i=4),
+                ACT.Copy,
+                scale=wt_b[:, t : t + 1],
+            )
 
         def weighted_half(half, x_q, v_q, v_cols, wt_b, bank):
             for pair in range(2):
@@ -191,32 +213,41 @@ def tile_attend_ghv_poi_kernel(tc, xT, w_words, w_scales, vT, wt, xm, offs, out)
                 for u in range(2):
                     mx(av[:, u, :], *x_q[2 * pair + u], v_q, v_cols, E4M3)
                 for u in range(2):
-                    t = 2 * pair + u
-                    nc.scalar.activation(
-                        av_wt[half][:, :, t, :],
-                        av[:, u, :].rearrange("p (c i) -> p c i", i=4),
-                        ACT.Copy,
-                        scale=wt_b[:, t : t + 1],
-                    )
+                    weigh(half, av[:, u, :], 2 * pair + u, wt_b, 0, H)
 
-        w_q = []
+        def weighted_chunk(c, x_q, v_q, wt_b, bank):
+            av = in_bank(bank, [P, PACK, CHUNK])
+            for t in range(PACK):
+                mx(av[:, t, :], *x_q[t], v_q, block(c - 4), E4M3)
+            for t in range(PACK):
+                weigh(c // 2, av[:, t, :], t, wt_b, c % 2 * CHUNK, CHUNK)
 
-        def gather_w(first, count, tag=None):
-            picked = sb("w_picked%d" % first, [P, count], U32, tag)
+        w_q = {}
+
+        def gather_w(first, count, picked):
             nc.vector.tensor_copy(picked[:], w_all[:].bitcast(U32).indirect(listed(first, count)))
             both = (picked, ws[:].bitcast(U8)[:, first : first + count])
-            w_q.extend((both, block(i)) for i in range(count // CHUNK))
+            for i in range(count // H):
+                w_q[first // H + i] = (both, i * H)
 
-        def mean_chunk(c, x_q, bank):
+        def mean_chunk(c, x_q, bank, width=CHUNK):
+            half, first = divmod(c * CHUNK, H)
+            both, at = w_q[half]
             a = in_bank(bank, [P, PACK, CHUNK])
             for t in range(PACK):
-                mx(a[:, t, :], *x_q[t], *w_q[c], E4M3)
-            nc.scalar.activation(mean[c // 2][:, block(c % 2, CHUNK // 4), :, :], by_fours(a[:]), ACT.Exp)
+                mx(a[:, t, :], *x_q[t], both, slice(at + first, at + first + CHUNK), E4M3)
+            for i in range(0, CHUNK, width):
+                dst = mean_of[c][:, i // 4 : (i + width) // 4, :, :]
+                nc.scalar.activation(dst, by_fours(a[:, :, i : i + width]), ACT.Exp)
 
-        def multiply(engine, c, g_bf):
-            part = block(c % 2, CHUNK // 4)
+        def multiply(engine, c, g_bf, width=CHUNK):
+            half, first = divmod(c * width, H)
+            chunk, at = divmod(c * width, CHUNK)
             engine.tensor_tensor(
-                interleaved(g_bf[:, block(c % 2), :]), mean[c // 2][:, part, :, :], av_wt[c // 2][:, part, :, :], MULT
+                interleaved(g_bf[:, first : first + width, :]),
+                mean_of[chunk][:, at // 4 : (at + width) // 4, :, :],
+                av_wt[half][:, first // 4 : (first + width) // 4, :, :],
+                MULT,
             )
 
         def quantize_g(half, g_bf):
@@ -241,19 +272,9 @@ def tile_attend_ghv_poi_kernel(tc, xT, w_words, w_scales, vT, wt, xm, offs, out)
             nc.gpsimd.tensor_scalar(dst_nj, src_jn.rearrange("p j n -> p n j"), 1.0, 0.0, MULT, ADD)
 
         weighted_half(0, x_q0, v_q0, slice(0, H), wt0, 2)
-        gather_w(0, H)
-        gather_w(H, 2 * H)
-        v_q23 = planes("v23", N, "ws_picked")
-        quantize(v_q23, slice(0, N), flat(v_bf23), E4M3)
-        xm_raw1 = sb("xm_raw1", [P, PACK, D], F32, "x_home")
-        nc.sync.dma_start(xm_raw1[:], xm_rows[1])
-        wt1 = load_wt(1, "v_picked2")
-        g_bf0 = sb("g_bf0", [P, H, PACK], BF16)
-        for c in range(2):
-            mean_chunk(c, x_q0, c)
-        for c in range(2):
-            multiply(nc.vector, c, g_bf0)
-        xm_q0, xm_q1 = [], []
+        gather_w(0, H, sb("w_picked0", [P, H], U32, "v_bf0"))
+        gather_w(N, N, on_x("w_picked23", [P, 2 * H], U32, 16 * R))
+        xm_q0 = []
 
         def quantize_xm(xm_q, name, grouped, tag=None):
             width = grouped.shape[1]
@@ -261,53 +282,67 @@ def tile_attend_ghv_poi_kernel(tc, xT, w_words, w_scales, vT, wt, xm, offs, out)
             quantize(both, slice(0, width), flat(grouped), E4M3)
             xm_q.extend((both, block(i)) for i in range(width // P))
 
-        xm_bf00 = sb("xm_bf00", [P, P, PACK], BF16, "w_picked0")
-        regroup(xm_bf00[:], xm_raw0[0])
+        xm_bf00 = on_x("xm_bf00", [P, P, PACK], BF16, 20 * R)
+        weave(xm_bf00[:], xm_raw0[0])
         quantize_xm(xm_q0, "xm00", xm_bf00[:])
-        quantize_g(0, g_bf0[:])
-        v_q1 = planes("v1", H, "av_wt0")
+        v_q1 = planes("v1", H, "ws_all")
         quantize(v_q1, slice(0, H), flat(v_bf1), E4M3)
-        xm_bf01 = sb("xm_bf01", [P, P, PACK], BF16, "ws_all")[:]
+        wt1 = load_wt(1, "v_picked1")
+        g_bf0 = on_x("g_bf0", [P, H, PACK], BF16, 20 * R)
+        for c in range(2):
+            mean_chunk(c, x_q0, c, FIRST_CHUNK)
+        for c in range(H // FIRST_CHUNK):
+            multiply(nc.vector, c, g_bf0, FIRST_CHUNK)
+        quantize_g(0, g_bf0[:])
+        xm_bf01 = sb("xm_bf01", [P, P, PACK], BF16, "v_bf0")[:]
         regroup(xm_bf01, xm_raw0[1])
-        quantize_xm(xm_q0, "xm01", xm_bf01)
-        gather_w(3 * H, H, "g_bf0")
+        quantize_xm(xm_q0, "xm01", xm_bf01, "mean0")
+        v_q23 = planes("v23", N, "av_wt0")
+        quantize(v_q23, slice(0, N), flat(v_bf23), E4M3)
+        gather_w(H, H, on_x("w_picked1", [P, H], U32, 20 * R))
+        xm_raw1 = sb("xm_raw1", [P, PACK, D], F32, "w_all")
+        nc.sync.dma_start(xm_raw1[:], xm_rows[1])
 
         place(0, product(xm_q0, 0, 0, 4), 0, 0, H)
-        xm_bf0b = sb("xm_bf0b", [P, D // 2, PACK], BF16, "ws_all")[:]
+        xm_bf0b = on_x("xm_bf0b", [P, D // 2, PACK], BF16, 4 * H)[:]
         weave(xm_bf0b, xm_raw0b)
         quantize_xm(xm_q0, "xm0b", xm_bf0b)
-        g_bf1 = sb("g_bf1", [P, H, PACK], BF16, "ws_all")[:]
+        g_bf1 = on_x("g_bf1", [P, H, PACK], BF16, 4 * H)[:]
+        weighted_half(1, x_q0, v_q1, block(0, H), wt0, 0)
         mean_chunk(2, x_q0, 2)
-        weighted_half(1, x_q0, v_q1, slice(0, H), wt0, 0)
         multiply(nc.gpsimd, 2, g_bf1)
-        after_weave = sb("after_weave", [P, PACK * R + 2 * H], BF16, "v_raw10")
-        place(1, product(xm_q0, 1, 0, 7), 0, 0, H, dw=after_weave[:, PACK * R :].bitcast(F32))
-        mean_chunk(3, x_q0, 4)
+        after_weave = sb("after_weave", [P, PACK * R + 2 * H + 2 * PACK * CHUNK], BF16, "v_raw10")
+        after_x1 = after_weave[:, PACK * R :].bitcast(F32)
+        place(1, product(xm_q0, 1, 0, 7), 0, 0, H, dw=after_x1[:, :H])
+        mean_of[3] = after_x1[:, H:].rearrange("p (c j i) -> p c j i", j=PACK, i=4)
+        mean_chunk(3, x_q0, 3)
         multiply(nc.gpsimd, 3, g_bf1)
         place(2, product(xm_q0, 2, 0, 6), 0, 0, H)
         x_bf1 = after_weave[:, : PACK * R].rearrange("p (t m j) -> p t m j", t=PACK, j=PACK)
-        for h in range(2):
-            deal_x(nc.scalar.copy, x_bf1, x_raw1[:, :, block(h, R // 2)], h * R // 2)
+        deal_x(nc.scalar.copy, x_bf1, x_raw1[:, :, :X1_FIRST], 0)
+        deal_x(nc.scalar.copy, x_bf1, x_raw1[:, :, X1_FIRST:], X1_FIRST)
         acc = product(xm_q0, 3, 0, 5)
         quantize_g(1, g_bf1)
-        whole_q = planes("x1", R, "v_raw01")
+        whole_q = (on_x("x1_codes", [P, R], U32, 28 * R), sb("x1_scales", [P, R], U8))
         quantize(whole_q, slice(0, R), x_bf1.rearrange("p t m j -> p (t m j)"), E4M3)
         x_q1 = [(whole_q, block(t)) for t in range(PACK)]
-        place(3, acc, 0, 0, H, "av_wt1")
+        place(3, acc, 0, 0, H, dw=on_x("dw_held", [P, H], F32, 24 * R)[:])
 
         xm_bf1 = sb("xm_bf1", [P, D, PACK], BF16, "v_raw10")[:]
         weave(xm_bf1, xm_raw1[:])
         place(0, product(xm_q0, 0, 1, 7), H, H, H)
-        g_bf2 = sb("g_bf2", [P, H, PACK], BF16, "ws_all")[:]
+        g_bf2 = on_x("g_bf2", [P, H, PACK], BF16, 4 * H)[:]
         mean_chunk(4, x_q1, 4)
-        weighted_half(2, x_q1, v_q23, block(0, H), wt1, 0)
+        weighted_chunk(4, x_q1, v_q23, wt1, 0)
         multiply(nc.gpsimd, 4, g_bf2)
         place(1, product(xm_q0, 1, 1, 6), H, H, H)
         mean_chunk(5, x_q1, 5)
+        weighted_chunk(5, x_q1, v_q23, wt1, 1)
         multiply(nc.gpsimd, 5, g_bf2)
         place(2, product(xm_q0, 2, 1, 7), H, H, H)
         acc = product(xm_q0, 3, 1, 6)
         quantize_g(2, g_bf2)
+        xm_q1 = []
         quantize_xm(xm_q1, "xm1", xm_bf1, "mean2")
         weighted_half(3, x_q1, v_q23, block(1, H), wt1, 2)
         place(3, acc, H, H, H, "av_wt2")

@@ -27,7 +27,8 @@ SCALE_STEP = 4
 V_CUTS = ((1024, 1024), (1024, 1024))
 V_SCALAR = ((1024, 1024), (1024, 352))
 FIRST_CHUNK = 64
-X1_FIRST = 192
+X0_SCALAR = 304
+X1_FIRST = 160
 
 
 def tile_attend_ghv_poi_kernel(tc, xT, w_words, w_scales, vT, wt, xm, offs, out):
@@ -140,13 +141,14 @@ def tile_attend_ghv_poi_kernel(tc, xT, w_words, w_scales, vT, wt, xm, offs, out)
         round_v(0, 1)
 
         spans = ((0, H), (H, 3 * H))
-        v_picked = [sb("v_picked%d" % s, [P, 2, count], U32)[:] for s, (first, count) in enumerate(spans)]
+        v_first = sb("v_first", [P, H], U32)[:]
+        v_later = sb("v_later", [P, 2, 3 * H], U32)[:]
 
-        def gather_pair(h, s):
-            nc.vector.tensor_copy(v_picked[s][:, h, :], flat(v_pairs[h][:]).bitcast(U32).indirect(listed(*spans[s])))
+        def gather_pair(h, s, dst):
+            nc.vector.tensor_copy(dst, flat(v_pairs[h][:]).bitcast(U32).indirect(listed(*spans[s])))
 
-        for s in range(2):
-            gather_pair(0, s)
+        gather_pair(0, 0, v_first)
+        gather_pair(0, 1, v_later[:, 0, :])
         round_v(1, 0)
         xm_rows = [xm[b].rearrange("(p j) d -> p j d", j=PACK) for b in range(B)]
         xm_raw0 = [sb("xm_raw0%d" % k, [P, PACK, P], F32, tag)[:] for k, tag in enumerate(("ws_all", "v_raw01"))]
@@ -155,16 +157,13 @@ def tile_attend_ghv_poi_kernel(tc, xT, w_words, w_scales, vT, wt, xm, offs, out)
         xm_raw0b = sb("xm_raw0b", [P, PACK, D // 2], F32, "v_raw10")[:]
         nc.sync.dma_start(xm_raw0b, xm_rows[0][:, :, D // 2 :])
         round_v(1, 1)
-        for s in range(2):
-            gather_pair(1, s)
+        v_bf0 = sb("v_bf0", [P, H, PACK], BF16, "v_raw11")[:]
+        nc.scalar.copy(as_pairs(v_bf0, U32)[:, :, 0], v_first)
+        gather_pair(1, 0, as_pairs(v_bf0, U32)[:, :, 1])
+        gather_pair(1, 1, v_later[:, 1, :])
         x_raw1 = sb("x_raw1", [P, PACK, R], F32, "v_pairs1")
         nc.sync.dma_start(x_raw1[:], xT[1].rearrange("(p j) r -> p j r", j=PACK))
 
-        def weave_pairs(s, v_bf):
-            nc.scalar.copy(interleaved(as_pairs(v_bf, U32)), by_fours(v_picked[s]))
-
-        v_bf0 = sb("v_bf0", [P, H, PACK], BF16)[:]
-        weave_pairs(0, v_bf0)
 
         def deal_x(copy, x_bf, raw, first):
             src = raw.rearrange("p j (m e t) -> p m j e t", e=2, t=PACK)
@@ -173,10 +172,10 @@ def tile_attend_ghv_poi_kernel(tc, xT, w_words, w_scales, vT, wt, xm, offs, out)
             copy(dst[:, pairs, :, :, :], src)
 
         x_bf0 = on_x("x_bf0", [P, PACK, P, PACK], BF16, 16 * R)[:]
-        deal_x(nc.scalar.copy, x_bf0, x_raw0[:, :, : R // 2], 0)
+        deal_x(nc.scalar.copy, x_bf0, x_raw0[:, :, :X0_SCALAR], 0)
         nc.gpsimd.tensor_scalar(
-            x_bf0[:, :, P // 2 :, :].rearrange("p t m j -> p m t j"),
-            x_raw0[:, :, R // 2 :].rearrange("p j (m t) -> p m t j", t=PACK),
+            x_bf0[:, :, X0_SCALAR // PACK :, :].rearrange("p t m j -> p m t j"),
+            x_raw0[:, :, X0_SCALAR:].rearrange("p j (m t) -> p m t j", t=PACK),
             1.0,
             0.0,
             MULT,
@@ -184,7 +183,7 @@ def tile_attend_ghv_poi_kernel(tc, xT, w_words, w_scales, vT, wt, xm, offs, out)
         )
         v_woven = on_x("v_woven", [P, 3 * H, PACK], BF16, 4 * H)[:]
         v_bf1, v_bf23 = v_woven[:, :H, :], v_woven[:, H:, :]
-        weave_pairs(1, v_woven)
+        nc.scalar.copy(interleaved(as_pairs(v_woven, U32)), by_fours(v_later))
         v_q0 = (on_x("v0_codes", [P, H], U32, 0), sb("v0_scales", [P, H], U8))
         quantize(v_q0, slice(0, H), flat(v_bf0), E4M3)
         x_q0 = []
@@ -272,7 +271,7 @@ def tile_attend_ghv_poi_kernel(tc, xT, w_words, w_scales, vT, wt, xm, offs, out)
             nc.gpsimd.tensor_scalar(dst_nj, src_jn.rearrange("p j n -> p n j"), 1.0, 0.0, MULT, ADD)
 
         weighted_half(0, x_q0, v_q0, slice(0, H), wt0, 2)
-        gather_w(0, H, sb("w_picked0", [P, H], U32, "v_bf0"))
+        gather_w(0, H, sb("w_picked0", [P, H], U32, "v_raw11"))
         gather_w(N, N, on_x("w_picked23", [P, 2 * H], U32, 16 * R))
         xm_q0 = []
 
@@ -287,14 +286,14 @@ def tile_attend_ghv_poi_kernel(tc, xT, w_words, w_scales, vT, wt, xm, offs, out)
         quantize_xm(xm_q0, "xm00", xm_bf00[:])
         v_q1 = planes("v1", H, "ws_all")
         quantize(v_q1, slice(0, H), flat(v_bf1), E4M3)
-        wt1 = load_wt(1, "v_picked1")
+        wt1 = load_wt(1, "v_later")
         g_bf0 = on_x("g_bf0", [P, H, PACK], BF16, 20 * R)
         for c in range(2):
             mean_chunk(c, x_q0, c, FIRST_CHUNK)
         for c in range(H // FIRST_CHUNK):
             multiply(nc.vector, c, g_bf0, FIRST_CHUNK)
         quantize_g(0, g_bf0[:])
-        xm_bf01 = sb("xm_bf01", [P, P, PACK], BF16, "v_bf0")[:]
+        xm_bf01 = sb("xm_bf01", [P, P, PACK], BF16, "v_raw11")[:]
         regroup(xm_bf01, xm_raw0[1])
         quantize_xm(xm_q0, "xm01", xm_bf01, "mean0")
         v_q23 = planes("v23", N, "av_wt0")
@@ -330,6 +329,7 @@ def tile_attend_ghv_poi_kernel(tc, xT, w_words, w_scales, vT, wt, xm, offs, out)
 
         xm_bf1 = sb("xm_bf1", [P, D, PACK], BF16, "v_raw10")[:]
         weave(xm_bf1, xm_raw1[:])
+        xm_bf1a, xm_bf1b = xm_bf1[:, : D // 2, :], xm_bf1[:, D // 2 :, :]
         place(0, product(xm_q0, 0, 1, 7), H, H, H)
         g_bf2 = on_x("g_bf2", [P, H, PACK], BF16, 4 * H)[:]
         mean_chunk(4, x_q1, 4)
@@ -343,11 +343,11 @@ def tile_attend_ghv_poi_kernel(tc, xT, w_words, w_scales, vT, wt, xm, offs, out)
         acc = product(xm_q0, 3, 1, 6)
         quantize_g(2, g_bf2)
         xm_q1 = []
-        quantize_xm(xm_q1, "xm1", xm_bf1, "mean2")
+        quantize_xm(xm_q1, "xm1a", xm_bf1a, "mean2")
         weighted_half(3, x_q1, v_q23, block(1, H), wt1, 2)
         place(3, acc, H, H, H, "av_wt2")
 
-        g_bf3 = sb("g_bf3", [P, H, PACK], BF16, "v_raw10")[:]
+        g_bf3 = xm_bf1a
         mean_chunk(6, x_q1, 4)
         multiply(nc.gpsimd, 6, g_bf3)
         place(0, product(xm_q1, 0, 2, 7), H, N, H)
@@ -355,6 +355,7 @@ def tile_attend_ghv_poi_kernel(tc, xT, w_words, w_scales, vT, wt, xm, offs, out)
         multiply(nc.gpsimd, 7, g_bf3)
         acc = product(xm_q1, 1, 2, 7)
         quantize_g(3, g_bf3)
+        quantize_xm(xm_q1, "xm1b", xm_bf1b, "mean3")
         place(1, acc, H, N, H, "av_wt3")
         for k in range(D // P):
             acc = product(xm_q1, k, 3, 6 + k % 2)

@@ -112,6 +112,9 @@ def tile_attend_ghv_poi_kernel(tc, xT, w_words, w_scales, vT, wt, xm, offs, out)
         wt0 = load_wt(0)
         w_all = sb("w_all", [P, T], I32)
         nc.sync.dma_start(w_all[:], w_words[0].rearrange("p n t -> p (n t)").bitcast(I32))
+        xm_rows = [xm[b].rearrange("(p j) d -> p j d", j=PACK) for b in range(B)]
+        xm_raw00 = sb("xm_raw00", [P, PACK, P], F32)[:]
+        nc.sync.dma_start(xm_raw00, xm_rows[0][:, :, block(0)])
 
         placed = [sb("placed%d" % k, [P, T], F32) for k in range(D // P)]
         for k in range(D // P):
@@ -150,10 +153,8 @@ def tile_attend_ghv_poi_kernel(tc, xT, w_words, w_scales, vT, wt, xm, offs, out)
         gather_pair(0, 0, v_first)
         gather_pair(0, 1, v_later[:, 0, :])
         round_v(1, 0)
-        xm_rows = [xm[b].rearrange("(p j) d -> p j d", j=PACK) for b in range(B)]
-        xm_raw0 = [sb("xm_raw0%d" % k, [P, PACK, P], F32, tag)[:] for k, tag in enumerate(("ws_all", "v_raw01"))]
-        for k in range(2):
-            nc.sync.dma_start(xm_raw0[k], xm_rows[0][:, :, block(k)])
+        xm_raw01 = sb("xm_raw01", [P, PACK, P], F32, "ws_all")[:]
+        nc.sync.dma_start(xm_raw01, xm_rows[0][:, :, block(1)])
         xm_raw0b = sb("xm_raw0b", [P, PACK, D // 2], F32, "v_raw10")[:]
         nc.sync.dma_start(xm_raw0b, xm_rows[0][:, :, D // 2 :])
         round_v(1, 1)
@@ -282,9 +283,9 @@ def tile_attend_ghv_poi_kernel(tc, xT, w_words, w_scales, vT, wt, xm, offs, out)
             xm_q.extend((both, block(i)) for i in range(width // P))
 
         xm_bf00 = on_x("xm_bf00", [P, P, PACK], BF16, 20 * R)
-        weave(xm_bf00[:], xm_raw0[0])
+        weave(xm_bf00[:], xm_raw00)
         quantize_xm(xm_q0, "xm00", xm_bf00[:])
-        v_q1 = planes("v1", H, "ws_all")
+        v_q1 = planes("v1", H, "xm_raw00")
         quantize(v_q1, slice(0, H), flat(v_bf1), E4M3)
         wt1 = load_wt(1, "v_later")
         g_bf0 = on_x("g_bf0", [P, H, PACK], BF16, 20 * R)
@@ -294,7 +295,7 @@ def tile_attend_ghv_poi_kernel(tc, xT, w_words, w_scales, vT, wt, xm, offs, out)
             multiply(nc.vector, c, g_bf0, FIRST_CHUNK)
         quantize_g(0, g_bf0[:])
         xm_bf01 = sb("xm_bf01", [P, P, PACK], BF16, "v_raw11")[:]
-        regroup(xm_bf01, xm_raw0[1])
+        regroup(xm_bf01, xm_raw01)
         quantize_xm(xm_q0, "xm01", xm_bf01, "mean0")
         v_q23 = planes("v23", N, "av_wt0")
         quantize(v_q23, slice(0, N), flat(v_bf23), E4M3)

@@ -167,8 +167,8 @@ def tile_attend_ghv_poi_kernel(tc, xT, w_words, w_scales, vT, wt, xm, offs, out)
 
 
         def deal_x(copy, x_bf, raw, first):
-            src = raw.rearrange("p j (m e t) -> p m j e t", e=2, t=PACK)
-            dst = x_bf.rearrange("p t (m e) j -> p m j e t", e=2)
+            src = raw.rearrange("p j (m e t) -> p m j t e", e=2, t=PACK)
+            dst = x_bf.rearrange("p t (m e) j -> p m j t e", e=2)
             pairs = slice(first // 8, first // 8 + src.shape[1])
             copy(dst[:, pairs, :, :, :], src)
 

@@ -160,8 +160,8 @@ def tile_attend_ghv_poi_kernel(tc, xT, w_words, w_scales, vT, wt, xm, offs, out)
         round_v(1, 1)
         v_bf0 = sb("v_bf0", [P, H, PACK], BF16, "v_raw11")[:]
         nc.scalar.copy(as_pairs(v_bf0, U32)[:, :, 0], v_first)
-        gather_pair(1, 0, as_pairs(v_bf0, U32)[:, :, 1])
         gather_pair(1, 1, v_later[:, 1, :])
+        gather_pair(1, 0, as_pairs(v_bf0, U32)[:, :, 1])
         x_raw1 = sb("x_raw1", [P, PACK, R], F32, "v_pairs1")
         nc.sync.dma_start(x_raw1[:], xT[1].rearrange("(p j) r -> p j r", j=PACK))
 
@@ -186,18 +186,20 @@ def tile_attend_ghv_poi_kernel(tc, xT, w_words, w_scales, vT, wt, xm, offs, out)
         v_bf1, v_bf23 = v_woven[:, :H, :], v_woven[:, H:, :]
         nc.scalar.copy(interleaved(as_pairs(v_woven, U32)), by_fours(v_later))
         v_q0 = (on_x("v0_codes", [P, H], U32, 0), sb("v0_scales", [P, H], U8))
-        quantize(v_q0, slice(0, H), flat(v_bf0), E4M3)
         x_q0 = []
         for u in range(2):
             pair_q = planes("x0_%d" % u, R // 2)
             quantize(pair_q, slice(0, R // 2), x_bf0[:, 2 * u : 2 * u + 2].rearrange("p t m j -> p (t m j)"), E4M3)
             x_q0.extend([(pair_q, block(0)), (pair_q, block(1))])
+            if u == 0:
+                quantize(v_q0, slice(0, H), flat(v_bf0), E4M3)
 
-        mean = {h: sb("mean%d" % h, [P, H // 4, PACK, 4], F32)[:] for h in (0, 2, 3)}
+        mean = {h: sb("mean%d" % h, [P, H // 4, PACK, 4], F32)[:] for h in (0, 2)}
         av_wt = {h: sb("av_wt%d" % h, [P, H // 4, PACK, 4], F32)[:] for h in (0, 2, 3)}
         av_wt[1] = on_x("av_wt1", [P, H // 4, PACK, 4], F32, 24 * R)[:]
-        mean_of = {c: mean[c // 2][:, block(c % 2, CHUNK // 4), :, :] for c in (0, 1, 4, 5, 6, 7)}
-        mean_of[2] = sb("mean1_first", [P, CHUNK // 4, PACK, 4], F32)[:]
+        mean_of = {c: mean[c // 2][:, block(c % 2, CHUNK // 4), :, :] for c in (0, 1, 4, 5)}
+        for c in (2, 6):
+            mean_of[c] = sb("mean_chunk%d" % c, [P, CHUNK // 4, PACK, 4], F32)[:]
 
         def weigh(half, av, t, wt_b, first, width):
             nc.scalar.activation(
@@ -346,7 +348,9 @@ def tile_attend_ghv_poi_kernel(tc, xT, w_words, w_scales, vT, wt, xm, offs, out)
         xm_q1 = []
         quantize_xm(xm_q1, "xm1a", xm_bf1a, "mean2")
         weighted_half(3, x_q1, v_q23, block(1, H), wt1, 2)
-        place(3, acc, H, H, H, "av_wt2")
+        after_third = sb("after_third", [P, H + PACK * CHUNK], F32, "av_wt2")
+        place(3, acc, H, H, H, dw=after_third[:, :H])
+        mean_of[7] = after_third[:, H:].rearrange("p (c j i) -> p c j i", j=PACK, i=4)
 
         g_bf3 = xm_bf1a
         mean_chunk(6, x_q1, 4)
@@ -356,7 +360,7 @@ def tile_attend_ghv_poi_kernel(tc, xT, w_words, w_scales, vT, wt, xm, offs, out)
         multiply(nc.gpsimd, 7, g_bf3)
         acc = product(xm_q1, 1, 2, 7)
         quantize_g(3, g_bf3)
-        quantize_xm(xm_q1, "xm1b", xm_bf1b, "mean3")
+        quantize_xm(xm_q1, "xm1b", xm_bf1b, "av_wt2")
         place(1, acc, H, N, H, "av_wt3")
         for k in range(D // P):
             acc = product(xm_q1, k, 3, 6 + k % 2)

from contextlib import ExitStack

import concourse.mybir as mybir

B, N, T, D, R = 2, 512, 2048, 512, 512
FLOPS = 3 * 2 * B * N * D * R

F32 = mybir.dt.float32
BF16 = mybir.dt.bfloat16
I32 = mybir.dt.int32
U32 = mybir.dt.uint32
U16 = mybir.dt.uint16
U8 = mybir.dt.uint8
E4M3 = mybir.dt.float8_e4m3fn_x4
E5M2 = mybir.dt.float8_e5m2_x4
ACT = mybir.ActivationFunctionType
MULT = mybir.AluOpType.mult
ADD = mybir.AluOpType.add

P = 128
PACK = 4
LIST_ROWS = 16
CHUNK = 128
H = N // 2
SCALE_FIRST = 32
SCALE_STEP = 4
V_CUTS = ((1024, 1024), (1024, 1024))
V_SCALAR = ((1024, 1024), (1024, 352))
FIRST_CHUNK = 64
X0_SCALAR = 304
X1_FIRST = 160


def tile_attend_ghv_poi_kernel(tc, xT, w_words, w_scales, vT, wt, xm, offs, out):
    nc = tc.nc
    with ExitStack() as ctx:
        keep = ctx.enter_context(tc.tile_pool(name="keep", bufs=1))
        after_x = ctx.enter_context(tc.tile_pool(name="after_x", bufs=1))
        psum = ctx.enter_context(tc.psum_pool(name="psum", bufs=1))

        def in_bank(i, shape):
            return psum.tile(shape, F32, name="bank%d" % i)

        def sb(name, shape, dtype, tag=None):
            return keep.tile(shape, dtype, name=name, tag=tag or name, align_bytes=64)

        def block(i, width=P):
            return slice(i * width, (i + 1) * width)

        def interleaved(tile_nj):
            return tile_nj.rearrange("p (c i) j -> p c j i", i=4)

        def by_fours(tile_jn):
            return tile_jn.rearrange("p j (c i) -> p c j i", i=4)

        def flat(tile_nj):
            return tile_nj.rearrange("p n j -> p (n j)")

        def as_pairs(tile_nj, dtype):
            return flat(tile_nj).bitcast(dtype).rearrange("p (n h) -> p n h", h=2)

        def planes(name, width, tag=None, scale_tag=None):
            return sb(name + "_codes", [P, width], U32, tag), sb(name + "_scales", [P, width], U8, scale_tag)

        def quantize(q, cols, grouped, fmt):
            nc.vector.quantize_mx(out=q[0][:, cols].bitcast(fmt), scales=q[1][:, cols], in_=grouped)

        def mx(acc, lhs_q, lhs_cols, rhs_q, rhs_cols, rhs_fmt):
            nc.tensor.matmul_mx(
                out=acc,
                lhsT=lhs_q[0][:, lhs_cols].bitcast(E4M3),
                lhsT_scale=lhs_q[1][:, lhs_cols],
                rhs=rhs_q[0][:, rhs_cols].bitcast(rhs_fmt),
                rhs_scale=rhs_q[1][:, rhs_cols],
                start=True,
                stop=True,
            )

        v_rows = vT.rearrange("(p j) t -> p j t", j=PACK)
        v_raw = [[sb("v_raw%d%d" % (h, c), [P, 2, w], F32) for c, w in enumerate(V_CUTS[h])] for h in range(2)]

        def load_v(h, c):
            first = sum(V_CUTS[h][:c])
            nc.sync.dma_start(v_raw[h][c][:], v_rows[:, 2 * h : 2 * h + 2, first : first + V_CUTS[h][c]])

        load_v(0, 0)
        offsets = keep.tile([P, B * N // LIST_ROWS], U16, name="offsets")
        nc.sync.dma_start(offsets[:], offs)

        def listed(first, count):
            return offsets[:, first // LIST_ROWS : (first + count) // LIST_ROWS]

        ws_all = sb("ws_all", [P, T // 4], I32)
        nc.gpsimd.memset(ws_all[:], 0)
        ws = sb("ws", [P, B * N // 4], I32)
        nc.gpsimd.memset(ws[:], 0)
        nc.sync.dma_start(ws_all[SCALE_FIRST : SCALE_FIRST + 16 * SCALE_STEP : SCALE_STEP, :], w_scales[0].bitcast(I32))
        load_v(0, 1)
        for c in range(2):
            load_v(1, c)

        def load_wt(b, tag=None):
            wt_b = sb("wt%d" % b, [P, PACK], F32, tag)
            nc.sync.dma_start(wt_b[:], wt[b].rearrange("(p t) o -> p (t o)", t=PACK))
            return wt_b

        def on_x(name, shape, dtype, at):
            return after_x.tile(shape, dtype, name=name, align_bytes=64, offset=at)

        x_raw0 = on_x("x_raw0", [P, PACK, R], F32, 0)[:]
        nc.sync.dma_start(x_raw0, xT[0].rearrange("(p j) r -> p j r", j=PACK))
        wt0 = load_wt(0)
        w_all = sb("w_all", [P, T], I32)
        nc.sync.dma_start(w_all[:], w_words[0].rearrange("p n t -> p (n t)").bitcast(I32))
        xm_rows = [xm[b].rearrange("(p j) d -> p j d", j=PACK) for b in range(B)]
        xm_raw00 = sb("xm_raw00", [P, PACK, P], F32)[:]
        nc.sync.dma_start(xm_raw00, xm_rows[0][:, :, block(0)])

        placed = [sb("placed%d" % k, [P, T], F32) for k in range(D // P)]
        for k in range(D // P):
            nc.gpsimd.memset(placed[k][:], 0.0)
        g_q = planes("g", B * N)
        nc.gpsimd.memset(g_q[0][:, block(1, H)].bitcast(I32), 0)
        nc.gpsimd.memset(g_q[1][:, block(1, H)].bitcast(I32), 0)

        v_pairs = [sb("v_pairs%d" % h, [P, T, 2], BF16) for h in range(2)]

        def round_v(h, c):
            first, share, width = sum(V_CUTS[h][:c]), V_SCALAR[h][c], V_CUTS[h][c]
            dst, src = v_pairs[h][:, first : first + width, :], v_raw[h][c]
            if share > 0:
                nc.scalar.activation(interleaved(dst[:, :share, :]), by_fours(src[:, :, :share]), ACT.Copy)
            if share < width:
                nc.vector.tensor_copy(interleaved(dst[:, share:, :]), by_fours(src[:, :, share:]))

        round_v(0, 0)

        ws_picked = sb("ws_picked", [P, B * N], U8)
        nc.vector.tensor_copy(ws_picked[:], ws_all[:].bitcast(U8).indirect(offsets[:]))
        for q in range(4):
            rows = slice(SCALE_FIRST + 4 * SCALE_STEP * q, SCALE_FIRST + 4 * SCALE_STEP * (q + 1), SCALE_STEP)
            nc.sync.dma_start(ws[32 * q : 32 * q + 4, :], ws_picked[rows, :].bitcast(I32))

        round_v(0, 1)

        spans = ((0, H), (H, 3 * H))
        v_first = sb("v_first", [P, H], U32)[:]
        v_later = sb("v_later", [P, 2, 3 * H], U32)[:]

        def gather_pair(h, s, dst):
            nc.vector.tensor_copy(dst, flat(v_pairs[h][:]).bitcast(U32).indirect(listed(*spans[s])))

        gather_pair(0, 0, v_first)
        gather_pair(0, 1, v_later[:, 0, :])
        round_v(1, 0)
        xm_raw01 = sb("xm_raw01", [P, PACK, P], F32, "ws_all")[:]
        nc.sync.dma_start(xm_raw01, xm_rows[0][:, :, block(1)])
        xm_raw0b = sb("xm_raw0b", [P, PACK, D // 2], F32, "v_raw10")[:]
        nc.sync.dma_start(xm_raw0b, xm_rows[0][:, :, D // 2 :])
        round_v(1, 1)
        v_bf0 = sb("v_bf0", [P, H, PACK], BF16, "v_raw11")[:]
        nc.scalar.copy(as_pairs(v_bf0, U32)[:, :, 0], v_first)
        gather_pair(1, 1, v_later[:, 1, :])
        gather_pair(1, 0, as_pairs(v_bf0, U32)[:, :, 1])
        x_raw1 = sb("x_raw1", [P, PACK, R], F32, "v_pairs1")
        nc.sync.dma_start(x_raw1[:], xT[1].rearrange("(p j) r -> p j r", j=PACK))


        def deal_x(copy, x_bf, raw, first):
            src = raw.rearrange("p j (m e t) -> p m j t e", e=2, t=PACK)
            dst = x_bf.rearrange("p t (m e) j -> p m j t e", e=2)
            pairs = slice(first // 8, first // 8 + src.shape[1])
            copy(dst[:, pairs, :, :, :], src)

        x_bf0 = on_x("x_bf0", [P, PACK, P, PACK], BF16, 16 * R)[:]
        deal_x(nc.scalar.copy, x_bf0, x_raw0[:, :, :X0_SCALAR], 0)
        nc.gpsimd.tensor_scalar(
            x_bf0[:, :, X0_SCALAR // PACK :, :].rearrange("p t m j -> p m t j"),
            x_raw0[:, :, X0_SCALAR:].rearrange("p j (m t) -> p m t j", t=PACK),
            1.0,
            0.0,
            MULT,
            ADD,
        )
        v_woven = on_x("v_woven", [P, 3 * H, PACK], BF16, 4 * H)[:]
        v_bf1, v_bf23 = v_woven[:, :H, :], v_woven[:, H:, :]
        nc.scalar.copy(interleaved(as_pairs(v_woven, U32)), by_fours(v_later))
        v_q0 = (on_x("v0_codes", [P, H], U32, 0), sb("v0_scales", [P, H], U8))
        x_q0 = []
        for u in range(2):
            pair_q = planes("x0_%d" % u, R // 2)
            quantize(pair_q, slice(0, R // 2), x_bf0[:, 2 * u : 2 * u + 2].rearrange("p t m j -> p (t m j)"), E4M3)
            x_q0.extend([(pair_q, block(0)), (pair_q, block(1))])
            if u == 0:
                quantize(v_q0, slice(0, H), flat(v_bf0), E4M3)

        mean = {h: sb("mean%d" % h, [P, H // 4, PACK, 4], F32)[:] for h in (0, 2)}
        av_wt = {h: sb("av_wt%d" % h, [P, H // 4, PACK, 4], F32)[:] for h in (0, 2, 3)}
        av_wt[1] = on_x("av_wt1", [P, H // 4, PACK, 4], F32, 24 * R)[:]
        mean_of = {c: mean[c // 2][:, block(c % 2, CHUNK // 4), :, :] for c in (0, 1, 4, 5)}
        for c in (2, 6):
            mean_of[c] = sb("mean_chunk%d" % c, [P, CHUNK // 4, PACK, 4], F32)[:]

        def weigh(half, av, t, wt_b, first, width):
            nc.scalar.activation(
                av_wt[half][:, first // 4 : (first + width) // 4, t, :],
                av.rearrange("p (c i) -> p c i", i=4),
                ACT.Copy,
                scale=wt_b[:, t : t + 1],
            )

        def weighted_half(half, x_q, v_q, v_cols, wt_b, bank):
            for pair in range(2):
                av = in_bank(bank + pair, [P, 2, H])
                for u in range(2):
                    mx(av[:, u, :], *x_q[2 * pair + u], v_q, v_cols, E4M3)
                for u in range(2):
                    weigh(half, av[:, u, :], 2 * pair + u, wt_b, 0, H)

        def weighted_chunk(c, x_q, v_q, wt_b, bank):
            av = in_bank(bank, [P, PACK, CHUNK])
            for t in range(PACK):
                mx(av[:, t, :], *x_q[t], v_q, block(c - 4), E4M3)
            for t in range(PACK):
                weigh(c // 2, av[:, t, :], t, wt_b, c % 2 * CHUNK, CHUNK)

        w_q = {}

        def gather_w(first, count, picked):
            nc.vector.tensor_copy(picked[:], w_all[:].bitcast(U32).indirect(listed(first, count)))
            both = (picked, ws[:].bitcast(U8)[:, first : first + count])
            for i in range(count // H):
                w_q[first // H + i] = (both, i * H)

        def mean_chunk(c, x_q, bank, width=CHUNK):
            half, first = divmod(c * CHUNK, H)
            both, at = w_q[half]
            a = in_bank(bank, [P, PACK, CHUNK])
            for t in range(PACK):
                mx(a[:, t, :], *x_q[t], both, slice(at + first, at + first + CHUNK), E4M3)
            for i in range(0, CHUNK, width):
                dst = mean_of[c][:, i // 4 : (i + width) // 4, :, :]
                nc.scalar.activation(dst, by_fours(a[:, :, i : i + width]), ACT.Exp)

        def multiply(engine, c, g_bf, width=CHUNK):
            half, first = divmod(c * width, H)
            chunk, at = divmod(c * width, CHUNK)
            engine.tensor_tensor(
                interleaved(g_bf[:, first : first + width, :]),
                mean_of[chunk][:, at // 4 : (at + width) // 4, :, :],
                av_wt[half][:, first // 4 : (first + width) // 4, :, :],
                MULT,
            )

        def quantize_g(half, g_bf):
            quantize(g_q, block(half, H), flat(g_bf), E5M2)

        def product(xm_q, k, half, bank):
            acc = in_bank(bank, [P, N])
            first = max(half - 1, 0) * H
            mx(acc[:], *xm_q[k], g_q, slice(first, first + N), E5M2)
            return acc

        def place(k, acc, first, slot, count, tag=None, dw=None):
            if dw is None:
                dw = sb("dw%d_%d" % (k, slot), [P, count], F32, tag)[:]
            nc.scalar.copy(dw, acc[:, first : first + count])
            nc.vector.tensor_copy(placed[k][:].indirect(listed(slot, count)), dw)

        def regroup(dst_nj, src_jn):
            nc.scalar.copy(interleaved(dst_nj), by_fours(src_jn))

        def weave(dst_nj, src_jn):
            nc.gpsimd.tensor_scalar(dst_nj, src_jn.rearrange("p j n -> p n j"), 1.0, 0.0, MULT, ADD)

        weighted_half(0, x_q0, v_q0, slice(0, H), wt0, 2)
        gather_w(0, H, sb("w_picked0", [P, H], U32, "v_raw11"))
        gather_w(N, N, on_x("w_picked23", [P, 2 * H], U32, 16 * R))
        xm_q0 = []

        def quantize_xm(xm_q, name, grouped, tag=None):
            width = grouped.shape[1]
            both = planes(name, width, tag)
            quantize(both, slice(0, width), flat(grouped), E4M3)
            xm_q.extend((both, block(i)) for i in range(width // P))

        xm_bf00 = on_x("xm_bf00", [P, P, PACK], BF16, 20 * R)
        weave(xm_bf00[:], xm_raw00)
        quantize_xm(xm_q0, "xm00", xm_bf00[:])
        v_q1 = planes("v1", H, "xm_raw00")
        quantize(v_q1, slice(0, H), flat(v_bf1), E4M3)
        wt1 = load_wt(1, "v_later")
        g_bf0 = on_x("g_bf0", [P, H, PACK], BF16, 20 * R)
        for c in range(2):
            mean_chunk(c, x_q0, c, FIRST_CHUNK)
        for c in range(H // FIRST_CHUNK):
            multiply(nc.vector, c, g_bf0, FIRST_CHUNK)
        quantize_g(0, g_bf0[:])
        xm_bf01 = sb("xm_bf01", [P, P, PACK], BF16, "v_raw11")[:]
        regroup(xm_bf01, xm_raw01)
        quantize_xm(xm_q0, "xm01", xm_bf01, "mean0")
        v_q23 = planes("v23", N, "av_wt0")
        quantize(v_q23, slice(0, N), flat(v_bf23), E4M3)
        gather_w(H, H, on_x("w_picked1", [P, H], U32, 20 * R))
        xm_raw1 = sb("xm_raw1", [P, PACK, D], F32, "w_all")
        nc.sync.dma_start(xm_raw1[:], xm_rows[1])

        place(0, product(xm_q0, 0, 0, 4), 0, 0, H)
        xm_bf0b = on_x("xm_bf0b", [P, D // 2, PACK], BF16, 4 * H)[:]
        weave(xm_bf0b, xm_raw0b)
        quantize_xm(xm_q0, "xm0b", xm_bf0b)
        g_bf1 = on_x("g_bf1", [P, H, PACK], BF16, 4 * H)[:]
        weighted_half(1, x_q0, v_q1, block(0, H), wt0, 0)
        mean_chunk(2, x_q0, 2)
        multiply(nc.gpsimd, 2, g_bf1)
        after_weave = sb("after_weave", [P, PACK * R + 2 * H + 2 * PACK * CHUNK], BF16, "v_raw10")
        after_x1 = after_weave[:, PACK * R :].bitcast(F32)
        place(1, product(xm_q0, 1, 0, 7), 0, 0, H, dw=after_x1[:, :H])
        mean_of[3] = after_x1[:, H:].rearrange("p (c j i) -> p c j i", j=PACK, i=4)
        mean_chunk(3, x_q0, 3)
        multiply(nc.gpsimd, 3, g_bf1)
        place(2, product(xm_q0, 2, 0, 6), 0, 0, H)
        x_bf1 = after_weave[:, : PACK * R].rearrange("p (t m j) -> p t m j", t=PACK, j=PACK)
        deal_x(nc.scalar.copy, x_bf1, x_raw1[:, :, :X1_FIRST], 0)
        deal_x(nc.scalar.copy, x_bf1, x_raw1[:, :, X1_FIRST:], X1_FIRST)
        acc = product(xm_q0, 3, 0, 5)
        quantize_g(1, g_bf1)
        whole_q = (on_x("x1_codes", [P, R], U32, 28 * R), sb("x1_scales", [P, R], U8))
        quantize(whole_q, slice(0, R), x_bf1.rearrange("p t m j -> p (t m j)"), E4M3)
        x_q1 = [(whole_q, block(t)) for t in range(PACK)]
        place(3, acc, 0, 0, H, dw=on_x("dw_held", [P, H], F32, 24 * R)[:])

        xm_bf1 = sb("xm_bf1", [P, D, PACK], BF16, "v_raw10")[:]
        weave(xm_bf1, xm_raw1[:])
        xm_bf1a, xm_bf1b = xm_bf1[:, : D // 2, :], xm_bf1[:, D // 2 :, :]
        place(0, product(xm_q0, 0, 1, 7), H, H, H)
        g_bf2 = on_x("g_bf2", [P, H, PACK], BF16, 4 * H)[:]
        mean_chunk(4, x_q1, 4)
        weighted_chunk(4, x_q1, v_q23, wt1, 0)
        multiply(nc.gpsimd, 4, g_bf2)
        place(1, product(xm_q0, 1, 1, 6), H, H, H)
        mean_chunk(5, x_q1, 5)
        weighted_chunk(5, x_q1, v_q23, wt1, 1)
        multiply(nc.gpsimd, 5, g_bf2)
        place(2, product(xm_q0, 2, 1, 7), H, H, H)
        acc = product(xm_q0, 3, 1, 6)
        quantize_g(2, g_bf2)
        xm_q1 = []
        quantize_xm(xm_q1, "xm1a", xm_bf1a, "mean2")
        weighted_half(3, x_q1, v_q23, block(1, H), wt1, 2)
        after_third = sb("after_third", [P, H + PACK * CHUNK], F32, "av_wt2")
        place(3, acc, H, H, H, dw=after_third[:, :H])
        mean_of[7] = after_third[:, H:].rearrange("p (c j i) -> p c j i", j=PACK, i=4)

        g_bf3 = xm_bf1a
        mean_chunk(6, x_q1, 4)
        multiply(nc.gpsimd, 6, g_bf3)
        place(0, product(xm_q1, 0, 2, 7), H, N, H)
        mean_chunk(7, x_q1, 5)
        multiply(nc.gpsimd, 7, g_bf3)
        acc = product(xm_q1, 1, 2, 7)
        quantize_g(3, g_bf3)
        quantize_xm(xm_q1, "xm1b", xm_bf1b, "av_wt2")
        place(1, acc, H, N, H, "av_wt3")
        for k in range(D // P):
            acc = product(xm_q1, k, 3, 6 + k % 2)
            if k < 2:
                place(k, acc, H, 3 * H, H)
            else:
                place(k, acc, 0, N, N)
            nc.sync.dma_start(out[block(k), :], placed[k][:])
